import numpy as np
import ml_dtypes


def mxq(x, axis, fmt="e4m3"):
    dtype, down = {"e4m3": (ml_dtypes.float8_e4m3fn, 7), "e5m2": (ml_dtypes.float8_e5m2, 14)}[fmt]
    v = np.moveaxis(np.asarray(x, np.float32).astype(ml_dtypes.bfloat16).astype(np.float64), axis, -1)
    blocks = v.reshape(v.shape[:-1] + (-1, 32))
    amax = np.abs(blocks).max(-1, keepdims=True)
    byte = np.maximum(np.where(amax > 0, np.frexp(amax)[1] - 1 + 127, 0) - down, 1)
    scale = np.exp2(byte - 127.0)
    codes = (blocks / scale).astype(np.float32).astype(dtype).astype(np.float64)
    return np.moveaxis((codes * scale).reshape(v.shape), -1, axis)


WIDE = False


def mx_kscale(k):
    if not WIDE:
        return np.ones(k)
    levels = np.array([18, -18])
    if k % 512:
        return np.exp2(np.random.permutation(np.resize(levels, k // 32))).repeat(32)
    a = np.empty((k // 512, 16))
    for p in range(k // 512):
        a[p, :8] = np.random.permutation(np.resize(levels, 8))
        for g in range(8):
            far = levels[np.abs(levels - a[p, g]) >= 10]
            a[p, g + 8] = far[np.random.randint(len(far))]
    return np.exp2(a.ravel()).repeat(32)


def f64(x):
    return np.asarray(x).astype(np.float64)


def striped(idx):
    return np.tile(np.asarray(idx).reshape(-1, 16).T, (8, 1)).astype(np.uint16)


def unstriped(offs):
    return offs[:16].T.reshape(-1).astype(np.int64)

def planes(y):
    n, m = y.shape
    v = y.astype(np.float32).astype(ml_dtypes.bfloat16).astype(np.float64).reshape(n // 32, 32, m)
    top = np.abs(v).max(1)
    byte = np.clip(np.where(top > 0, np.frexp(top)[1] - 1 + 127 - 7, 1), 1, 254)
    codes = (v * np.exp2(127.0 - byte)[:, None, :]).reshape(n, m).astype(np.float32).astype(ml_dtypes.float8_e4m3fn).view(np.uint8)
    words = codes.reshape(n // 512, 128, 4, m).transpose(0, 1, 3, 2)
    return np.ascontiguousarray(words), np.ascontiguousarray(byte.astype(np.uint8).reshape(n // 512, 16, m))


def setup_inputs():
    n = np.random.standard_normal
    uni = np.random.uniform
    idx = np.random.permutation(2048)[:512]
    w_ = uni(0.5, 1.5, (512, 1))
    f_d = mx_kscale(512)
    f_r = mx_kscale(512)
    return {
        "xT": (0.5 * n((512, 512)) * f_d[:, None] * f_r[None, :]).astype(np.float32),
        "cT": (n((512, 2048)) / np.sqrt(512) / f_d[:, None]).astype(np.float32),
        "us": (uni(0.75, 1.3, (512, 1)) / f_r[:, None]).astype(np.float32),
        "ts": np.tile(uni(0.75, 1.3, 2048), (128, 1)).astype(np.float32),
        "wt": (w_ / f_r[:, None]).astype(np.float32),
        "wd": (w_).astype(np.float32),
        "offs": striped(idx),
    }


def reference(xT, cT, us, ts, wt, wd, offs):
    idx = unstriped(offs)
    cT_i = f64(cT)[:, idx]
    ts_i = f64(ts)[:1][:, idx]
    a = mxq(f64(xT), 0, "e4m3").T @ mxq(cT_i, 0, "e4m3")
    z = f64(us) * ts_i * a
    m = (z).max(-1, keepdims=True)
    e = np.exp(z - m)
    tot = (e).sum(-1, keepdims=True)
    p = e / tot
    g = f64(wt) * p
    num = mxq(f64(xT), 1, "e4m3") @ mxq(g, 0, "e4m3")
    h = f64(wd) * p
    ht = h.T
    den = (ht).sum(-1, keepdims=True)
    dr = den.T
    mean = num / dr
    out_0 = np.zeros((512, 2048))
    out_0[:, idx] = mean
    return (out_0,) + planes(out_0)

@@ -1,0 +1,216 @@
+from contextlib import ExitStack
+
+import concourse.mybir as mybir
+from concourse.masks import make_identity
+
+F32 = mybir.dt.float32
+BF16 = mybir.dt.bfloat16
+I32 = mybir.dt.int32
+U32 = mybir.dt.uint32
+U16 = mybir.dt.uint16
+U8 = mybir.dt.uint8
+FP8X4 = mybir.dt.float8_e4m3fn_x4
+ALU = mybir.AluOpType
+ACT = mybir.ActivationFunctionType
+AXIS_X = mybir.AxisListType.X
+
+P = 128
+LANES = 4
+D, R, SLOTS, T = 512, 512, 512, 2048
+FLOPS = 2 * 2 * D * R * SLOTS
+HALF = SLOTS // 2
+CHUNK_WIDTHS = (256, 256, 512, 512, 256, 256)
+SCALAR_CHUNKS = 2
+
+
+def tile_attend_gkmeans_pl_kernel(tc, xT, cT, us, ts, wt, wd, offs, out_0, out_1, out_2):
+    nc = tc.nc
+    with ExitStack() as ctx:
+        sb = ctx.enter_context(tc.tile_pool(name="sb", bufs=1))
+        ps = ctx.enter_context(tc.psum_pool(name="ps", bufs=1))
+
+        def mx_tiles(name, width):
+            codes = sb.tile([P, width], U32, name=name + "_codes", align_bytes=64)
+            scales = sb.tile([P, width], U8, name=name + "_scales", align_bytes=64)
+            return codes, scales
+
+        x_raw = sb.tile([P, LANES, R], F32, name="x_raw")
+        nc.sync.dma_start(out=x_raw[:], in_=xT.rearrange("(p j) r -> p j r", j=LANES))
+        offsets = sb.tile([P, SLOTS // 16], U16, name="offsets")
+        nc.sync.dma_start(offsets[:], offs)
+        ts_window = sb.tile([P, T], F32, name="ts_window")
+        nc.sync.dma_start(out=ts_window[P - 1:P, :], in_=ts[0:1, :])
+        nc.vector.memset(ts_window[0:P - 1, :], 0.0)
+        c_planes = [sb.tile([P, T], F32, name=f"c_plane{j}") for j in range(LANES)]
+        c_rows = cT.rearrange("(p j) n -> p j n", j=LANES)
+        for j in range(LANES):
+            nc.sync.dma_start(out=c_planes[j][:], in_=c_rows[:, j, :])
+
+        row_factors = []
+        for name, vec in (("us_sb", us), ("wt_sb", wt), ("wd_sb", wd)):
+            tile = sb.tile([P, LANES], F32, name=name)
+            nc.scalar.dma_start(out=tile[:], in_=vec.rearrange("(s t) o -> s (t o)", t=LANES))
+            row_factors.append(tile)
+        us_sb, wt_sb, wd_sb = row_factors
+
+        ident = sb.tile([P, P], F32, name="ident")
+        make_identity(nc, ident[:])
+
+        ts_row = sb.tile([P, SLOTS], F32, name="ts_row")
+        nc.vector.tensor_copy(ts_row[:], ts_window[:].indirect(offsets[:]))
+        ts_turned = ps.tile([P, LANES, P], F32, name="ts_turned", tag="bank6")
+        for c in range(LANES):
+            nc.tensor.transpose(ts_turned[:, c, :], ts_row[:, c * P:(c + 1) * P], ident[:])
+        ts_cols = sb.tile([P, LANES], F32, name="ts_cols")
+        nc.scalar.copy(ts_cols[:], ts_turned[:, :, P - 1])
+
+        def spread_columns(spread, cols, bank):
+            count = cols.shape[1]
+            spread_ps = ps.tile([P, count * P], F32, name="spread_ps", tag=bank)
+            for c in range(count):
+                nc.tensor.transpose(spread_ps[:, c * P:(c + 1) * P], cols[:, c:c + 1].to_broadcast([P, P]), ident[:])
+            nc.scalar.copy(spread, spread_ps[:])
+
+        ts_all = sb.tile([P, SLOTS], F32, name="ts_all")
+        spread_columns(ts_all[:], ts_cols[:], "bank7")
+
+        x_by_d = sb.tile([P, R * LANES], BF16, name="x_by_d", align_bytes=64)
+        nc.scalar.copy(
+            x_by_d[:].rearrange("p (t s j) -> p s j t", t=LANES, j=LANES),
+            x_raw[:].rearrange("p j (s t) -> p s j t", t=LANES),
+        )
+        xd_codes, xd_scales = mx_tiles("xd", R)
+        nc.vector.quantize_mx(out=xd_codes[:].bitcast(FP8X4), scales=xd_scales[:], in_=x_by_d[:])
+
+        x_pairs = x_by_d[:].bitcast(F32)
+        x_by_r = sb.tile([P, D * LANES], BF16, name="x_by_r", align_bytes=64)
+        for u in range(2):
+            turned = ps.tile([P, LANES * P], F32, name=f"x_turned{u}", tag=f"bank{4 + u}")
+            for t in range(LANES):
+                nc.tensor.transpose(turned[:, t * P:(t + 1) * P], x_pairs[:, 2 * P * t + u:2 * P * (t + 1):2], ident[:])
+            nc.scalar.copy(
+                x_by_r[:, u * 2 * R:(u + 1) * 2 * R].rearrange("s (e p t) -> s e p t", e=2, t=LANES),
+                turned[:].bitcast(BF16).rearrange("s (t p e) -> s e p t", t=LANES, e=2),
+            )
+        xr_codes, xr_scales = mx_tiles("xr", D)
+        nc.vector.quantize_mx(out=xr_codes[:].bitcast(FP8X4), scales=xr_scales[:], in_=x_by_r[:])
+
+        c_by_d = sb.tile([P, SLOTS * LANES], BF16, name="c_by_d", align_bytes=64)
+        c_lanes = c_by_d[:].rearrange("p (i j) -> p i j", j=LANES)
+        c_first = sb.tile([P, 2, SLOTS], BF16, name="c_first")
+        for j in range(2):
+            nc.vector.tensor_copy(c_first[:, j, :], c_planes[j][:].indirect(offsets[:]))
+        nc.scalar.copy(c_lanes[:, :, 0:2], c_first[:].rearrange("p j i -> p i j"))
+        for j in range(2, LANES):
+            nc.vector.tensor_copy(c_lanes[:, :, j], c_planes[j][:].indirect(offsets[:]))
+        c_codes, c_scales = mx_tiles("c", SLOTS)
+        nc.vector.quantize_mx(out=c_codes[:].bitcast(FP8X4), scales=c_scales[:], in_=c_by_d[:])
+
+        g_pairs = sb.tile([P, 2 * SLOTS * 2], BF16, name="g_pairs")
+        g_pair_lanes = g_pairs[:].rearrange("s (u i e) -> s u i e", u=2, e=2)
+        den_ps = [ps.tile([P, HALF], F32, name=f"den_ps{a}", tag=f"bank{5 + a}") for a in range(2)]
+        for t in range(LANES):
+            rows = slice(t * P, (t + 1) * P)
+            scores = ps.tile([P, SLOTS], F32, name=f"scores{t}", tag=f"bank{t}")
+            nc.tensor.matmul_mx(out=scores[:], lhsT=xd_codes[:, rows].bitcast(FP8X4), lhsT_scale=xd_scales[:, rows],
+                                rhs=c_codes[:].bitcast(FP8X4), rhs_scale=c_scales[:], start=True, stop=True)
+            z = sb.tile([P, SLOTS], F32, name=f"z{t}")
+            nc.vector.scalar_tensor_tensor(z[:], scores[:], us_sb[:, t:t + 1], ts_all[:], ALU.mult, ALU.mult)
+            neg_max = sb.tile([P, 1], F32, name=f"neg_max{t}")
+            nc.vector.tensor_reduce(neg_max[:], z[:], AXIS_X, ALU.max, negate=True)
+            e = sb.tile([P, SLOTS], F32, name=f"e{t}")
+            tot = sb.tile([P, 1], F32, name=f"tot{t}")
+            nc.scalar.activation(e[:], z[:], ACT.Exp, bias=neg_max[:], scale=1.0, accum_out=tot[:])
+            inv_tot = sb.tile([P, 1], F32, name=f"inv_tot{t}")
+            nc.vector.reciprocal(inv_tot[:], tot[:])
+            h = sb.tile([P, SLOTS], F32, name=f"h{t}")
+            if t < LANES - 1:
+                h_factor = sb.tile([P, 1], F32, name=f"h_factor{t}")
+                nc.scalar.activation(h_factor[:], wd_sb[:, t:t + 1], ACT.Copy, scale=inv_tot[:])
+                nc.scalar.activation(h[:], e[:], ACT.Copy, scale=h_factor[:])
+            else:
+                nc.vector.tensor_scalar(h[:], e[:], inv_tot[:], wd_sb[:, t:t + 1], ALU.mult, ALU.mult)
+            for c in range(LANES):
+                a, b = divmod(c, 2)
+                nc.tensor.matmul(den_ps[a][:, b * P:(b + 1) * P], h[:, c * P:(c + 1) * P], ident[:], is_transpose=True,
+                                 start=(t == 0 and b == 0), stop=(t == LANES - 1 and b == 1))
+            nc.vector.tensor_scalar(g_pair_lanes[:, t // 2, :, t % 2], e[:], inv_tot[:], wt_sb[:, t:t + 1], ALU.mult, ALU.mult)
+
+        g_codes, g_scales = mx_tiles("g", SLOTS)
+        inv_den_all = sb.tile([P, SLOTS], F32, name="inv_den_all")
+        halves = [slice(a * HALF, (a + 1) * HALF) for a in range(2)]
+        g_by_r = [sb.tile([P, HALF * LANES], BF16, name=f"g_by_r{a}", align_bytes=64) for a in range(2)]
+        dens = [sb.tile([P, 2], F32, name=f"den{a}") for a in range(2)]
+        den_terms = sb.tile([P, P], F32, name="den_terms")
+        for a in range(2):
+            nc.vector.tensor_copy(
+                g_by_r[a][:].bitcast(I32).rearrange("s (i u) -> s i u", u=2),
+                g_pairs[:].bitcast(I32).rearrange("s (u i) -> s i u", u=2)[:, halves[a], :],
+            )
+            for b in range(2):
+                nc.scalar.activation(den_terms[:], den_ps[a][:, b * P:(b + 1) * P], ACT.Copy, accum_out=dens[a][:, b:b + 1])
+
+        windows = [sb.tile([P, T], F32, name=f"window{j}") for j in range(LANES)]
+        nums = [sb.tile([P, SLOTS], F32, name=f"num{j}") for j in range(LANES)]
+
+        def numerators(j, slots, bank):
+            feats = slice(j * P, (j + 1) * P)
+            num_ps = ps.tile([P, slots.stop - slots.start], F32, name="num_ps", tag=bank)
+            nc.tensor.matmul_mx(out=num_ps[:], lhsT=xr_codes[:, feats].bitcast(FP8X4), lhsT_scale=xr_scales[:, feats],
+                                rhs=g_codes[:, slots].bitcast(FP8X4), rhs_scale=g_scales[:, slots], start=True, stop=True)
+            nc.scalar.copy(nums[j][:, slots], num_ps[:])
+
+        def scatter_means(j, slots):
+            listed = offsets[:, slots.start // 16:slots.stop // 16]
+            nc.vector.tensor_tensor(windows[j][:].indirect(listed), nums[j][:, slots], inv_den_all[:, slots], ALU.mult)
+
+        for a in range(2):
+            nc.vector.quantize_mx(out=g_codes[:, halves[a]].bitcast(FP8X4), scales=g_scales[:, halves[a]], in_=g_by_r[a][:])
+            inv_den = sb.tile([P, 2], F32, name=f"inv_den{a}")
+            nc.vector.reciprocal(inv_den[:], dens[a][:])
+            numerators(0, halves[a], f"bank{a}")
+            spread_columns(inv_den_all[:, halves[a]], inv_den[:], ("bank7", "bank4")[a])
+        all_slots = slice(0, SLOTS)
+        for j in range(1, LANES):
+            numerators(j, all_slots, f"bank{(j + 1) % LANES}")
+
+        for j in range(LANES):
+            for a in range(2):
+                nc.vector.memset(windows[j][:, a * T // 2:(a + 1) * T // 2], 0.0)
+
+        chunks = []
+        lo = 0
+        for width in CHUNK_WIDTHS:
+            chunks.append(slice(lo, lo + width))
+            lo = lo + width
+        y_pairs = [sb.tile([P, 2 * width * 2], BF16, name=f"y_pairs{k}") for k, width in enumerate(CHUNK_WIDTHS)]
+        out_rows = out_0.rearrange("(p j) n -> p j n", j=LANES)
+        for j in range(LANES):
+            for slots in (halves if j == 0 else [all_slots]):
+                scatter_means(j, slots)
+            nc.sync.dma_start(out=out_rows[:, j, :], in_=windows[j][:])
+            for k, cols in enumerate(chunks):
+                lane = y_pairs[k][:].rearrange("p (u n e) -> p u n e", u=2, e=2)[:, j // 2, :, j % 2]
+                nc.scalar.copy(lane, windows[j][:, cols])
+
+        y_scales = sb.tile([P, T], U8, name="y_scales", align_bytes=64)
+        words_out = out_1[0].rearrange("p n l -> p (n l)").bitcast(I32)
+        for k, cols in enumerate(chunks):
+            width = CHUNK_WIDTHS[k]
+            y_by_d = sb.tile([P, width * LANES], BF16, name=f"y_by_d{k}", align_bytes=64)
+            if k < len(chunks) - SCALAR_CHUNKS:
+                nc.vector.tensor_copy(
+                    y_by_d[:].bitcast(I32).rearrange("p (n u) -> p n u", u=2),
+                    y_pairs[k][:].bitcast(I32).rearrange("p (u n) -> p n u", u=2),
+                )
+            else:
+                nc.scalar.copy(
+                    y_by_d[:].bitcast(U32).rearrange("p (n u) -> p n u", u=2),
+                    y_pairs[k][:].bitcast(U32).rearrange("p (u n) -> p n u", u=2),
+                )
+            y_codes = sb.tile([P, width], U32, name=f"y_codes{k}", align_bytes=64)
+            nc.vector.quantize_mx(out=y_codes[:].bitcast(FP8X4), scales=y_scales[:, cols], in_=y_by_d[:])
+            nc.sync.dma_start(out=words_out[:, cols], in_=y_codes[:].bitcast(I32))
+        for q in range(4):
+            queue = nc.sync if q % 2 == 0 else nc.scalar
+            queue.dma_start(out=out_2[0, 4 * q:4 * q + 4, :].bitcast(I32), in_=y_scales[32 * q:32 * q + 4, :].bitcast(I32))

@@ -19,8 +19,9 @@ LANES = 4
 D, R, SLOTS, T = 512, 512, 512, 2048
 FLOPS = 2 * 2 * D * R * SLOTS
 HALF = SLOTS // 2
-CHUNK_WIDTHS = (256, 256, 512, 512, 256, 256)
-SCALAR_CHUNKS = 2
+BLOCK = 256
+CHUNK_BLOCKS = (2, 2, 1, 1, 1, 1)
+SCALAR_CHUNKS = 3
 
 
 def tile_attend_gkmeans_pl_kernel(tc, xT, cT, us, ts, wt, wd, offs, out_0, out_1, out_2):
@@ -109,6 +110,7 @@ def tile_attend_gkmeans_pl_kernel(tc, xT, cT, us, ts, wt, wd, offs, out_0, out_1
         g_pairs = sb.tile([P, 2 * SLOTS * 2], BF16, name="g_pairs")
         g_pair_lanes = g_pairs[:].rearrange("s (u i e) -> s u i e", u=2, e=2)
         den_ps = [ps.tile([P, HALF], F32, name=f"den_ps{a}", tag=f"bank{5 + a}") for a in range(2)]
+        exps = []
         for t in range(LANES):
             rows = slice(t * P, (t + 1) * P)
             scores = ps.tile([P, SLOTS], F32, name=f"scores{t}", tag=f"bank{t}")
@@ -124,22 +126,28 @@ def tile_attend_gkmeans_pl_kernel(tc, xT, cT, us, ts, wt, wd, offs, out_0, out_1
             inv_tot = sb.tile([P, 1], F32, name=f"inv_tot{t}")
             nc.vector.reciprocal(inv_tot[:], tot[:])
             h = sb.tile([P, SLOTS], F32, name=f"h{t}")
-            if t < LANES - 1:
-                h_factor = sb.tile([P, 1], F32, name=f"h_factor{t}")
-                nc.scalar.activation(h_factor[:], wd_sb[:, t:t + 1], ACT.Copy, scale=inv_tot[:])
-                nc.scalar.activation(h[:], e[:], ACT.Copy, scale=h_factor[:])
+            if t < 2:
+                nc.gpsimd.tensor_scalar(h[:], e[:], inv_tot[:], wd_sb[:, t:t + 1], ALU.mult, ALU.mult)
             else:
                 nc.vector.tensor_scalar(h[:], e[:], inv_tot[:], wd_sb[:, t:t + 1], ALU.mult, ALU.mult)
             for c in range(LANES):
                 a, b = divmod(c, 2)
                 nc.tensor.matmul(den_ps[a][:, b * P:(b + 1) * P], h[:, c * P:(c + 1) * P], ident[:], is_transpose=True,
                                  start=(t == 0 and b == 0), stop=(t == LANES - 1 and b == 1))
-            nc.vector.tensor_scalar(g_pair_lanes[:, t // 2, :, t % 2], e[:], inv_tot[:], wt_sb[:, t:t + 1], ALU.mult, ALU.mult)
+            exps.append((e, inv_tot))
+        for t, (e, inv_tot) in enumerate(exps):
+            lane = g_pair_lanes[:, t // 2, :, t % 2]
+            if t < 2:
+                g_factor = sb.tile([P, 1], F32, name=f"g_factor{t}")
+                nc.scalar.activation(g_factor[:], wt_sb[:, t:t + 1], ACT.Copy, scale=inv_tot[:])
+                nc.scalar.activation(lane, e[:], ACT.Copy, scale=g_factor[:])
+            else:
+                nc.vector.tensor_scalar(lane, e[:], inv_tot[:], wt_sb[:, t:t + 1], ALU.mult, ALU.mult)
 
         g_codes, g_scales = mx_tiles("g", SLOTS)
         inv_den_all = sb.tile([P, SLOTS], F32, name="inv_den_all")
         halves = [slice(a * HALF, (a + 1) * HALF) for a in range(2)]
-        g_by_r = [sb.tile([P, HALF * LANES], BF16, name=f"g_by_r{a}", align_bytes=64) for a in range(2)]
+        g_by_r = [sb.tile([P, HALF * LANES], BF16, name=f"g_by_r{a}", tag=f"late{a}", align_bytes=64) for a in range(2)]
         dens = [sb.tile([P, 2], F32, name=f"den{a}") for a in range(2)]
         den_terms = sb.tile([P, P], F32, name="den_terms")
         for a in range(2):
@@ -150,7 +158,7 @@ def tile_attend_gkmeans_pl_kernel(tc, xT, cT, us, ts, wt, wd, offs, out_0, out_1
             for b in range(2):
                 nc.scalar.activation(den_terms[:], den_ps[a][:, b * P:(b + 1) * P], ACT.Copy, accum_out=dens[a][:, b:b + 1])
 
-        windows = [sb.tile([P, T], F32, name=f"window{j}") for j in range(LANES)]
+        windows = [sb.tile([P, T], F32, name=f"window{j}") for j in range(2)]
         nums = [sb.tile([P, SLOTS], F32, name=f"num{j}") for j in range(LANES)]
 
         def numerators(j, slots, bank):
@@ -174,40 +182,49 @@ def tile_attend_gkmeans_pl_kernel(tc, xT, cT, us, ts, wt, wd, offs, out_0, out_1
         for j in range(1, LANES):
             numerators(j, all_slots, f"bank{(j + 1) % LANES}")
 
-        for j in range(LANES):
-            for a in range(2):
-                nc.vector.memset(windows[j][:, a * T // 2:(a + 1) * T // 2], 0.0)
+        for j in range(2):
+            nc.vector.memset(windows[j][:], 0.0)
+        for a in range(2):
+            windows.append(sb.tile([P, T], F32, name=f"window{2 + a}", tag=f"late{1 - a}", align_bytes=64))
+            nc.gpsimd.memset(windows[2 + a][:], 0.0)
+
+        y_pairs = sb.tile([P, T * LANES], BF16, name="y_pairs")
+        pair_lanes = y_pairs[:].rearrange("p (b u n e) -> p b u n e", u=2, n=BLOCK, e=2)
+
+        def round_into_lane(copy, j, blocks):
+            source = windows[j][:].rearrange("p (b n) -> p b n", n=BLOCK)
+            copy(pair_lanes[:, blocks, j // 2, :, j % 2], source[:, blocks, :])
 
         chunks = []
         lo = 0
-        for width in CHUNK_WIDTHS:
-            chunks.append(slice(lo, lo + width))
-            lo = lo + width
-        y_pairs = [sb.tile([P, 2 * width * 2], BF16, name=f"y_pairs{k}") for k, width in enumerate(CHUNK_WIDTHS)]
+        for count in CHUNK_BLOCKS:
+            chunks.append(slice(lo, lo + count))
+            lo = lo + count
         out_rows = out_0.rearrange("(p j) n -> p j n", j=LANES)
         for j in range(LANES):
             for slots in (halves if j == 0 else [all_slots]):
                 scatter_means(j, slots)
             nc.sync.dma_start(out=out_rows[:, j, :], in_=windows[j][:])
-            for k, cols in enumerate(chunks):
-                lane = y_pairs[k][:].rearrange("p (u n e) -> p u n e", u=2, e=2)[:, j // 2, :, j % 2]
-                nc.scalar.copy(lane, windows[j][:, cols])
+            if j < 2:
+                round_into_lane(nc.scalar.copy, j, slice(0, T // BLOCK))
+            elif j == 2:
+                round_into_lane(nc.scalar.copy, j, slice(chunks[1].start, T // BLOCK))
+        for j in (2, 3):
+            round_into_lane(nc.vector.tensor_copy, j, chunks[0])
+        for blocks in chunks[1:]:
+            round_into_lane(nc.scalar.copy, 3, blocks)
 
         y_scales = sb.tile([P, T], U8, name="y_scales", align_bytes=64)
         words_out = out_1[0].rearrange("p n l -> p (n l)").bitcast(I32)
-        for k, cols in enumerate(chunks):
-            width = CHUNK_WIDTHS[k]
+        for k, blocks in enumerate(chunks):
+            width = CHUNK_BLOCKS[k] * BLOCK
+            cols = slice(blocks.start * BLOCK, blocks.stop * BLOCK)
             y_by_d = sb.tile([P, width * LANES], BF16, name=f"y_by_d{k}", align_bytes=64)
-            if k < len(chunks) - SCALAR_CHUNKS:
-                nc.vector.tensor_copy(
-                    y_by_d[:].bitcast(I32).rearrange("p (n u) -> p n u", u=2),
-                    y_pairs[k][:].bitcast(I32).rearrange("p (u n) -> p n u", u=2),
-                )
-            else:
-                nc.scalar.copy(
-                    y_by_d[:].bitcast(U32).rearrange("p (n u) -> p n u", u=2),
-                    y_pairs[k][:].bitcast(U32).rearrange("p (u n) -> p n u", u=2),
-                )
+            copy, word = (nc.vector.tensor_copy, I32) if k < len(chunks) - SCALAR_CHUNKS else (nc.scalar.copy, U32)
+            copy(
+                y_by_d[:].bitcast(word).rearrange("p (b n u) -> p b n u", n=BLOCK, u=2),
+                y_pairs[:].bitcast(word).rearrange("p (b u n) -> p b n u", u=2, n=BLOCK)[:, blocks, :, :],
+            )
             y_codes = sb.tile([P, width], U32, name=f"y_codes{k}", align_bytes=64)
             nc.vector.quantize_mx(out=y_codes[:].bitcast(FP8X4), scales=y_scales[:, cols], in_=y_by_d[:])
             nc.sync.dma_start(out=words_out[:, cols], in_=y_codes[:].bitcast(I32))

@@ -30,8 +30,8 @@ def tile_attend_gkmeans_pl_kernel(tc, xT, cT, us, ts, wt, wd, offs, out_0, out_1
         sb = ctx.enter_context(tc.tile_pool(name="sb", bufs=1))
         ps = ctx.enter_context(tc.psum_pool(name="ps", bufs=1))
 
-        def mx_tiles(name, width):
-            codes = sb.tile([P, width], U32, name=name + "_codes", align_bytes=64)
+        def mx_tiles(name, width, tag=""):
+            codes = sb.tile([P, width], U32, name=name + "_codes", tag=tag, align_bytes=64)
             scales = sb.tile([P, width], U8, name=name + "_scales", align_bytes=64)
             return codes, scales
 
@@ -40,7 +40,7 @@ def tile_attend_gkmeans_pl_kernel(tc, xT, cT, us, ts, wt, wd, offs, out_0, out_1
         offsets = sb.tile([P, SLOTS // 16], U16, name="offsets")
         nc.sync.dma_start(offsets[:], offs)
         ts_window = sb.tile([P, T], F32, name="ts_window")
-        nc.sync.dma_start(out=ts_window[P - 1:P, :], in_=ts[0:1, :])
+        nc.scalar.dma_start(out=ts_window[P - 1:P, :], in_=ts[0:1, :])
         nc.vector.memset(ts_window[0:P - 1, :], 0.0)
         c_planes = [sb.tile([P, T], F32, name=f"c_plane{j}") for j in range(LANES)]
         c_rows = cT.rearrange("(p j) n -> p j n", j=LANES)
@@ -83,6 +83,25 @@ def tile_attend_gkmeans_pl_kernel(tc, xT, cT, us, ts, wt, wd, offs, out_0, out_1
         xd_codes, xd_scales = mx_tiles("xd", R)
         nc.vector.quantize_mx(out=xd_codes[:].bitcast(FP8X4), scales=xd_scales[:], in_=x_by_d[:])
 
+        c_by_d = sb.tile([P, SLOTS * LANES], BF16, name="c_by_d", tag="after_c", align_bytes=64)
+        c_lanes = c_by_d[:].rearrange("p (i j) -> p i j", j=LANES)
+        c_first = sb.tile([P, 2, SLOTS], BF16, name="c_first")
+        for j in range(2):
+            nc.vector.tensor_copy(c_first[:, j, :], c_planes[j][:].indirect(offsets[:]))
+        nc.scalar.copy(c_lanes[:, :, 0:2], c_first[:].rearrange("p j i -> p i j"))
+        nc.vector.tensor_copy(c_lanes[:, :, 2], c_planes[2][:].indirect(offsets[:]))
+        halves = [slice(a * HALF, (a + 1) * HALF) for a in range(2)]
+
+        def listed(slots):
+            return offsets[:, slots.start // 16:slots.stop // 16]
+
+        for slots in halves:
+            nc.vector.tensor_copy(c_lanes[:, slots, 3], c_planes[3][:].indirect(listed(slots)))
+        c_codes, c_scales = mx_tiles("c", SLOTS)
+        for slots in halves:
+            nc.vector.quantize_mx(out=c_codes[:, slots].bitcast(FP8X4), scales=c_scales[:, slots],
+                                  in_=c_by_d[:, slots.start * LANES:slots.stop * LANES])
+
         x_pairs = x_by_d[:].bitcast(F32)
         x_by_r = sb.tile([P, D * LANES], BF16, name="x_by_r", align_bytes=64)
         for u in range(2):
@@ -93,19 +112,8 @@ def tile_attend_gkmeans_pl_kernel(tc, xT, cT, us, ts, wt, wd, offs, out_0, out_1
                 x_by_r[:, u * 2 * R:(u + 1) * 2 * R].rearrange("s (e p t) -> s e p t", e=2, t=LANES),
                 turned[:].bitcast(BF16).rearrange("s (t p e) -> s e p t", t=LANES, e=2),
             )
-        xr_codes, xr_scales = mx_tiles("xr", D)
+        xr_codes, xr_scales = mx_tiles("xr", D, "after_c")
         nc.vector.quantize_mx(out=xr_codes[:].bitcast(FP8X4), scales=xr_scales[:], in_=x_by_r[:])
-
-        c_by_d = sb.tile([P, SLOTS * LANES], BF16, name="c_by_d", align_bytes=64)
-        c_lanes = c_by_d[:].rearrange("p (i j) -> p i j", j=LANES)
-        c_first = sb.tile([P, 2, SLOTS], BF16, name="c_first")
-        for j in range(2):
-            nc.vector.tensor_copy(c_first[:, j, :], c_planes[j][:].indirect(offsets[:]))
-        nc.scalar.copy(c_lanes[:, :, 0:2], c_first[:].rearrange("p j i -> p i j"))
-        for j in range(2, LANES):
-            nc.vector.tensor_copy(c_lanes[:, :, j], c_planes[j][:].indirect(offsets[:]))
-        c_codes, c_scales = mx_tiles("c", SLOTS)
-        nc.vector.quantize_mx(out=c_codes[:].bitcast(FP8X4), scales=c_scales[:], in_=c_by_d[:])
 
         g_pairs = sb.tile([P, 2 * SLOTS * 2], BF16, name="g_pairs")
         g_pair_lanes = g_pairs[:].rearrange("s (u i e) -> s u i e", u=2, e=2)
@@ -114,8 +122,9 @@ def tile_attend_gkmeans_pl_kernel(tc, xT, cT, us, ts, wt, wd, offs, out_0, out_1
         for t in range(LANES):
             rows = slice(t * P, (t + 1) * P)
             scores = ps.tile([P, SLOTS], F32, name=f"scores{t}", tag=f"bank{t}")
-            nc.tensor.matmul_mx(out=scores[:], lhsT=xd_codes[:, rows].bitcast(FP8X4), lhsT_scale=xd_scales[:, rows],
-                                rhs=c_codes[:].bitcast(FP8X4), rhs_scale=c_scales[:], start=True, stop=True)
+            for slots in halves:
+                nc.tensor.matmul_mx(out=scores[:, slots], lhsT=xd_codes[:, rows].bitcast(FP8X4), lhsT_scale=xd_scales[:, rows],
+                                    rhs=c_codes[:, slots].bitcast(FP8X4), rhs_scale=c_scales[:, slots], start=True, stop=True)
             z = sb.tile([P, SLOTS], F32, name=f"z{t}")
             nc.vector.scalar_tensor_tensor(z[:], scores[:], us_sb[:, t:t + 1], ts_all[:], ALU.mult, ALU.mult)
             neg_max = sb.tile([P, 1], F32, name=f"neg_max{t}")
@@ -144,9 +153,8 @@ def tile_attend_gkmeans_pl_kernel(tc, xT, cT, us, ts, wt, wd, offs, out_0, out_1
             else:
                 nc.vector.tensor_scalar(lane, e[:], inv_tot[:], wt_sb[:, t:t + 1], ALU.mult, ALU.mult)
 
-        g_codes, g_scales = mx_tiles("g", SLOTS)
+        g_codes, g_scales = mx_tiles("g", SLOTS, "after_products")
         inv_den_all = sb.tile([P, SLOTS], F32, name="inv_den_all")
-        halves = [slice(a * HALF, (a + 1) * HALF) for a in range(2)]
         g_by_r = [sb.tile([P, HALF * LANES], BF16, name=f"g_by_r{a}", tag=f"late{a}", align_bytes=64) for a in range(2)]
         dens = [sb.tile([P, 2], F32, name=f"den{a}") for a in range(2)]
         den_terms = sb.tile([P, P], F32, name="den_terms")
@@ -169,8 +177,7 @@ def tile_attend_gkmeans_pl_kernel(tc, xT, cT, us, ts, wt, wd, offs, out_0, out_1
             nc.scalar.copy(nums[j][:, slots], num_ps[:])
 
         def scatter_means(j, slots):
-            listed = offsets[:, slots.start // 16:slots.stop // 16]
-            nc.vector.tensor_tensor(windows[j][:].indirect(listed), nums[j][:, slots], inv_den_all[:, slots], ALU.mult)
+            nc.vector.tensor_tensor(windows[j][:].indirect(listed(slots)), nums[j][:, slots], inv_den_all[:, slots], ALU.mult)
 
         for a in range(2):
             nc.vector.quantize_mx(out=g_codes[:, halves[a]].bitcast(FP8X4), scales=g_scales[:, halves[a]], in_=g_by_r[a][:])
@@ -185,7 +192,7 @@ def tile_attend_gkmeans_pl_kernel(tc, xT, cT, us, ts, wt, wd, offs, out_0, out_1
         for j in range(2):
             nc.vector.memset(windows[j][:], 0.0)
         for a in range(2):
-            windows.append(sb.tile([P, T], F32, name=f"window{2 + a}", tag=f"late{1 - a}", align_bytes=64))
+            windows.append(sb.tile([P, T], F32, name=f"window{2 + a}", tag=("late1", "after_products")[a], align_bytes=64))
             nc.gpsimd.memset(windows[2 + a][:], 0.0)
 
         y_pairs = sb.tile([P, T * LANES], BF16, name="y_pairs")

@@ -20,8 +20,7 @@ D, R, SLOTS, T = 512, 512, 512, 2048
 FLOPS = 2 * 2 * D * R * SLOTS
 HALF = SLOTS // 2
 BLOCK = 256
-CHUNK_BLOCKS = (2, 2, 1, 1, 1, 1)
-SCALAR_CHUNKS = 3
+DIRECT = 512
 
 
 def tile_attend_gkmeans_pl_kernel(tc, xT, cT, us, ts, wt, wd, offs, out_0, out_1, out_2):
@@ -34,6 +33,12 @@ def tile_attend_gkmeans_pl_kernel(tc, xT, cT, us, ts, wt, wd, offs, out_0, out_1
             codes = sb.tile([P, width], U32, name=name + "_codes", tag=tag, align_bytes=64)
             scales = sb.tile([P, width], U8, name=name + "_scales", align_bytes=64)
             return codes, scales
+
+        def interleave(copy, lanes_last, staged):
+            copy(
+                lanes_last.rearrange("p (b c n j) -> p b c j n", c=BLOCK // 4, n=4, j=LANES),
+                staged.rearrange("p (b j c n) -> p b c j n", j=LANES, c=BLOCK // 4, n=4),
+            )
 
         x_raw = sb.tile([P, LANES, R], F32, name="x_raw")
         nc.sync.dma_start(out=x_raw[:], in_=xT.rearrange("(p j) r -> p j r", j=LANES))
@@ -85,11 +90,8 @@ def tile_attend_gkmeans_pl_kernel(tc, xT, cT, us, ts, wt, wd, offs, out_0, out_1
 
         c_by_d = sb.tile([P, SLOTS * LANES], BF16, name="c_by_d", tag="after_c", align_bytes=64)
         c_lanes = c_by_d[:].rearrange("p (i j) -> p i j", j=LANES)
-        c_first = sb.tile([P, 2, SLOTS], BF16, name="c_first")
-        for j in range(2):
-            nc.vector.tensor_copy(c_first[:, j, :], c_planes[j][:].indirect(offsets[:]))
-        nc.scalar.copy(c_lanes[:, :, 0:2], c_first[:].rearrange("p j i -> p i j"))
-        nc.vector.tensor_copy(c_lanes[:, :, 2], c_planes[2][:].indirect(offsets[:]))
+        for j in range(LANES - 1):
+            nc.vector.tensor_copy(c_lanes[:, :, j], c_planes[j][:].indirect(offsets[:]))
         halves = [slice(a * HALF, (a + 1) * HALF) for a in range(2)]
 
         def listed(slots):
@@ -115,8 +117,8 @@ def tile_attend_gkmeans_pl_kernel(tc, xT, cT, us, ts, wt, wd, offs, out_0, out_1
         xr_codes, xr_scales = mx_tiles("xr", D, "after_c")
         nc.vector.quantize_mx(out=xr_codes[:].bitcast(FP8X4), scales=xr_scales[:], in_=x_by_r[:])
 
-        g_pairs = sb.tile([P, 2 * SLOTS * 2], BF16, name="g_pairs")
-        g_pair_lanes = g_pairs[:].rearrange("s (u i e) -> s u i e", u=2, e=2)
+        g_staged = sb.tile([P, SLOTS * LANES], BF16, name="g_staged")
+        g_runs = g_staged[:].rearrange("s (a t i) -> s a t i", a=2, t=LANES)
         den_ps = [ps.tile([P, HALF], F32, name=f"den_ps{a}", tag=f"bank{5 + a}") for a in range(2)]
         exps = []
         for t in range(LANES):
@@ -145,13 +147,14 @@ def tile_attend_gkmeans_pl_kernel(tc, xT, cT, us, ts, wt, wd, offs, out_0, out_1
                                  start=(t == 0 and b == 0), stop=(t == LANES - 1 and b == 1))
             exps.append((e, inv_tot))
         for t, (e, inv_tot) in enumerate(exps):
-            lane = g_pair_lanes[:, t // 2, :, t % 2]
+            lane = g_runs[:, :, t, :]
+            e_runs = e[:].rearrange("s (a i) -> s a i", a=2)
             if t < 2:
                 g_factor = sb.tile([P, 1], F32, name=f"g_factor{t}")
                 nc.scalar.activation(g_factor[:], wt_sb[:, t:t + 1], ACT.Copy, scale=inv_tot[:])
-                nc.scalar.activation(lane, e[:], ACT.Copy, scale=g_factor[:])
+                nc.scalar.activation(lane, e_runs, ACT.Copy, scale=g_factor[:])
             else:
-                nc.vector.tensor_scalar(lane, e[:], inv_tot[:], wt_sb[:, t:t + 1], ALU.mult, ALU.mult)
+                nc.vector.tensor_scalar(lane, e_runs, inv_tot[:], wt_sb[:, t:t + 1], ALU.mult, ALU.mult)
 
         g_codes, g_scales = mx_tiles("g", SLOTS, "after_products")
         inv_den_all = sb.tile([P, SLOTS], F32, name="inv_den_all")
@@ -159,10 +162,7 @@ def tile_attend_gkmeans_pl_kernel(tc, xT, cT, us, ts, wt, wd, offs, out_0, out_1
         dens = [sb.tile([P, 2], F32, name=f"den{a}") for a in range(2)]
         den_terms = sb.tile([P, P], F32, name="den_terms")
         for a in range(2):
-            nc.vector.tensor_copy(
-                g_by_r[a][:].bitcast(I32).rearrange("s (i u) -> s i u", u=2),
-                g_pairs[:].bitcast(I32).rearrange("s (u i) -> s i u", u=2)[:, halves[a], :],
-            )
+            interleave(nc.vector.tensor_copy, g_by_r[a][:], g_staged[:, a * HALF * LANES:(a + 1) * HALF * LANES])
             for b in range(2):
                 nc.scalar.activation(den_terms[:], den_ps[a][:, b * P:(b + 1) * P], ACT.Copy, accum_out=dens[a][:, b:b + 1])
 
@@ -195,44 +195,44 @@ def tile_attend_gkmeans_pl_kernel(tc, xT, cT, us, ts, wt, wd, offs, out_0, out_1
             windows.append(sb.tile([P, T], F32, name=f"window{2 + a}", tag=("late1", "after_products")[a], align_bytes=64))
             nc.gpsimd.memset(windows[2 + a][:], 0.0)
 
-        y_pairs = sb.tile([P, T * LANES], BF16, name="y_pairs")
-        pair_lanes = y_pairs[:].rearrange("p (b u n e) -> p b u n e", u=2, n=BLOCK, e=2)
+        y_direct = sb.tile([P, DIRECT * LANES], BF16, name="y_direct", align_bytes=64)
+        y_staged = sb.tile([P, (T - DIRECT) * LANES], BF16, name="y_staged")
+        staged_runs = y_staged[:].rearrange("p (b j n) -> p b j n", j=LANES, n=BLOCK)
 
-        def round_into_lane(copy, j, blocks):
-            source = windows[j][:].rearrange("p (b n) -> p b n", n=BLOCK)
-            copy(pair_lanes[:, blocks, j // 2, :, j % 2], source[:, blocks, :])
+        def round_direct(j):
+            nc.scalar.copy(y_direct[:].rearrange("p (n j) -> p n j", j=LANES)[:, :, j], windows[j][:, 0:DIRECT])
 
-        chunks = []
-        lo = 0
-        for count in CHUNK_BLOCKS:
-            chunks.append(slice(lo, lo + count))
-            lo = lo + count
+        def round_staged(copy, j, blocks):
+            source = windows[j][:, DIRECT:T].rearrange("p (b n) -> p b n", n=BLOCK)
+            copy(staged_runs[:, blocks, j, :], source[:, blocks, :])
+
         out_rows = out_0.rearrange("(p j) n -> p j n", j=LANES)
+        last = LANES - 1
         for j in range(LANES):
             for slots in (halves if j == 0 else [all_slots]):
                 scatter_means(j, slots)
             nc.sync.dma_start(out=out_rows[:, j, :], in_=windows[j][:])
-            if j < 2:
-                round_into_lane(nc.scalar.copy, j, slice(0, T // BLOCK))
-            elif j == 2:
-                round_into_lane(nc.scalar.copy, j, slice(chunks[1].start, T // BLOCK))
-        for j in (2, 3):
-            round_into_lane(nc.vector.tensor_copy, j, chunks[0])
-        for blocks in chunks[1:]:
-            round_into_lane(nc.scalar.copy, 3, blocks)
+            if j < last:
+                round_staged(nc.scalar.copy, j, slice(0, (T - DIRECT) // BLOCK))
+            round_direct(j)
+
+        chunks = []
+        lo = 0
+        for count, copy in ((2, nc.vector.tensor_copy), (2, nc.vector.tensor_copy), (1, nc.scalar.copy), (1, nc.scalar.copy)):
+            chunks.append((slice(lo, lo + count), copy))
+            lo = lo + count
+        for blocks, copy in chunks:
+            round_staged(copy, last, blocks)
+        ready = [(slice(0, DIRECT), y_direct)]
+        for k, (blocks, copy) in enumerate(chunks):
+            y_by_d = sb.tile([P, (blocks.stop - blocks.start) * BLOCK * LANES], BF16, name=f"y_by_d{k}", align_bytes=64)
+            interleave(copy, y_by_d[:], y_staged[:, blocks.start * BLOCK * LANES:blocks.stop * BLOCK * LANES])
+            ready.append((slice(DIRECT + blocks.start * BLOCK, DIRECT + blocks.stop * BLOCK), y_by_d))
 
         y_scales = sb.tile([P, T], U8, name="y_scales", align_bytes=64)
         words_out = out_1[0].rearrange("p n l -> p (n l)").bitcast(I32)
-        for k, blocks in enumerate(chunks):
-            width = CHUNK_BLOCKS[k] * BLOCK
-            cols = slice(blocks.start * BLOCK, blocks.stop * BLOCK)
-            y_by_d = sb.tile([P, width * LANES], BF16, name=f"y_by_d{k}", align_bytes=64)
-            copy, word = (nc.vector.tensor_copy, I32) if k < len(chunks) - SCALAR_CHUNKS else (nc.scalar.copy, U32)
-            copy(
-                y_by_d[:].bitcast(word).rearrange("p (b n u) -> p b n u", n=BLOCK, u=2),
-                y_pairs[:].bitcast(word).rearrange("p (b u n) -> p b n u", u=2, n=BLOCK)[:, blocks, :, :],
-            )
-            y_codes = sb.tile([P, width], U32, name=f"y_codes{k}", align_bytes=64)
+        for k, (cols, y_by_d) in enumerate(ready):
+            y_codes = sb.tile([P, cols.stop - cols.start], U32, name=f"y_codes{k}", align_bytes=64)
             nc.vector.quantize_mx(out=y_codes[:].bitcast(FP8X4), scales=y_scales[:, cols], in_=y_by_d[:])
             nc.sync.dma_start(out=words_out[:, cols], in_=y_codes[:].bitcast(I32))
         for q in range(4):

@@ -40,13 +40,13 @@ def tile_attend_gkmeans_pl_kernel(tc, xT, cT, us, ts, wt, wd, offs, out_0, out_1
                 staged.rearrange("p (b j c n) -> p b c j n", j=LANES, c=BLOCK // 4, n=4),
             )
 
-        x_raw = sb.tile([P, LANES, R], F32, name="x_raw")
-        nc.sync.dma_start(out=x_raw[:], in_=xT.rearrange("(p j) r -> p j r", j=LANES))
         offsets = sb.tile([P, SLOTS // 16], U16, name="offsets")
         nc.sync.dma_start(offsets[:], offs)
-        ts_window = sb.tile([P, T], F32, name="ts_window")
+        ts_window = sb.tile([P, T], F32, name="ts_window", tag="ts_then_window2")
         nc.scalar.dma_start(out=ts_window[P - 1:P, :], in_=ts[0:1, :])
         nc.vector.memset(ts_window[0:P - 1, :], 0.0)
+        x_raw = sb.tile([P, LANES, R], F32, name="x_raw")
+        nc.sync.dma_start(out=x_raw[:], in_=xT.rearrange("(p j) r -> p j r", j=LANES))
         c_planes = [sb.tile([P, T], F32, name=f"c_plane{j}") for j in range(LANES)]
         c_rows = cT.rearrange("(p j) n -> p j n", j=LANES)
         for j in range(LANES):
@@ -64,6 +64,11 @@ def tile_attend_gkmeans_pl_kernel(tc, xT, cT, us, ts, wt, wd, offs, out_0, out_1
 
         ts_row = sb.tile([P, SLOTS], F32, name="ts_row")
         nc.vector.tensor_copy(ts_row[:], ts_window[:].indirect(offsets[:]))
+        windows = [sb.tile([P, T], F32, name=f"window{j}") for j in range(2)]
+        nc.vector.memset(windows[0][:], 0.0)
+        nc.gpsimd.memset(windows[1][:], 0.0)
+        windows.append(sb.tile([P, T], F32, name="window2", tag="ts_then_window2"))
+        nc.gpsimd.memset(windows[2][:], 0.0)
         ts_turned = ps.tile([P, LANES, P], F32, name="ts_turned", tag="bank6")
         for c in range(LANES):
             nc.tensor.transpose(ts_turned[:, c, :], ts_row[:, c * P:(c + 1) * P], ident[:])
@@ -88,7 +93,20 @@ def tile_attend_gkmeans_pl_kernel(tc, xT, cT, us, ts, wt, wd, offs, out_0, out_1
         xd_codes, xd_scales = mx_tiles("xd", R)
         nc.vector.quantize_mx(out=xd_codes[:].bitcast(FP8X4), scales=xd_scales[:], in_=x_by_d[:])
 
-        c_by_d = sb.tile([P, SLOTS * LANES], BF16, name="c_by_d", tag="after_c", align_bytes=64)
+        x_pairs = x_by_d[:].bitcast(F32)
+        x_by_r = sb.tile([P, D * LANES], BF16, name="x_by_r", align_bytes=64)
+        for u in range(2):
+            turned = ps.tile([P, LANES * P], F32, name=f"x_turned{u}", tag=f"bank{4 + u}")
+            for t in range(LANES):
+                nc.tensor.transpose(turned[:, t * P:(t + 1) * P], x_pairs[:, 2 * P * t + u:2 * P * (t + 1):2], ident[:])
+            nc.scalar.copy(
+                x_by_r[:, u * 2 * R:(u + 1) * 2 * R].rearrange("s (e p t) -> s e p t", e=2, t=LANES),
+                turned[:].bitcast(BF16).rearrange("s (t p e) -> s e p t", t=LANES, e=2),
+            )
+        xr_codes, xr_scales = mx_tiles("xr", D)
+        nc.vector.quantize_mx(out=xr_codes[:].bitcast(FP8X4), scales=xr_scales[:], in_=x_by_r[:])
+
+        c_by_d = sb.tile([P, SLOTS * LANES], BF16, name="c_by_d", tag="c_then_window3", align_bytes=64)
         c_lanes = c_by_d[:].rearrange("p (i j) -> p i j", j=LANES)
         for j in range(LANES - 1):
             nc.vector.tensor_copy(c_lanes[:, :, j], c_planes[j][:].indirect(offsets[:]))
@@ -103,71 +121,96 @@ def tile_attend_gkmeans_pl_kernel(tc, xT, cT, us, ts, wt, wd, offs, out_0, out_1
         for slots in halves:
             nc.vector.quantize_mx(out=c_codes[:, slots].bitcast(FP8X4), scales=c_scales[:, slots],
                                   in_=c_by_d[:, slots.start * LANES:slots.stop * LANES])
+        windows.append(sb.tile([P, T], F32, name="window3", tag="c_then_window3", align_bytes=64))
+        nc.gpsimd.memset(windows[3][:], 0.0)
 
-        x_pairs = x_by_d[:].bitcast(F32)
-        x_by_r = sb.tile([P, D * LANES], BF16, name="x_by_r", align_bytes=64)
-        for u in range(2):
-            turned = ps.tile([P, LANES * P], F32, name=f"x_turned{u}", tag=f"bank{4 + u}")
-            for t in range(LANES):
-                nc.tensor.transpose(turned[:, t * P:(t + 1) * P], x_pairs[:, 2 * P * t + u:2 * P * (t + 1):2], ident[:])
-            nc.scalar.copy(
-                x_by_r[:, u * 2 * R:(u + 1) * 2 * R].rearrange("s (e p t) -> s e p t", e=2, t=LANES),
-                turned[:].bitcast(BF16).rearrange("s (t p e) -> s e p t", t=LANES, e=2),
-            )
-        xr_codes, xr_scales = mx_tiles("xr", D, "after_c")
-        nc.vector.quantize_mx(out=xr_codes[:].bitcast(FP8X4), scales=xr_scales[:], in_=x_by_r[:])
-
+        all_slots = slice(0, SLOTS)
         g_staged = sb.tile([P, SLOTS * LANES], BF16, name="g_staged")
         g_runs = g_staged[:].rearrange("s (a t i) -> s a t i", a=2, t=LANES)
-        den_ps = [ps.tile([P, HALF], F32, name=f"den_ps{a}", tag=f"bank{5 + a}") for a in range(2)]
-        exps = []
-        for t in range(LANES):
-            rows = slice(t * P, (t + 1) * P)
-            scores = ps.tile([P, SLOTS], F32, name=f"scores{t}", tag=f"bank{t}")
-            for slots in halves:
-                nc.tensor.matmul_mx(out=scores[:, slots], lhsT=xd_codes[:, rows].bitcast(FP8X4), lhsT_scale=xd_scales[:, rows],
-                                    rhs=c_codes[:, slots].bitcast(FP8X4), rhs_scale=c_scales[:, slots], start=True, stop=True)
-            z = sb.tile([P, SLOTS], F32, name=f"z{t}")
-            nc.vector.scalar_tensor_tensor(z[:], scores[:], us_sb[:, t:t + 1], ts_all[:], ALU.mult, ALU.mult)
-            neg_max = sb.tile([P, 1], F32, name=f"neg_max{t}")
-            nc.vector.tensor_reduce(neg_max[:], z[:], AXIS_X, ALU.max, negate=True)
-            e = sb.tile([P, SLOTS], F32, name=f"e{t}")
-            tot = sb.tile([P, 1], F32, name=f"tot{t}")
-            nc.scalar.activation(e[:], z[:], ACT.Exp, bias=neg_max[:], scale=1.0, accum_out=tot[:])
-            inv_tot = sb.tile([P, 1], F32, name=f"inv_tot{t}")
-            nc.vector.reciprocal(inv_tot[:], tot[:])
-            h = sb.tile([P, SLOTS], F32, name=f"h{t}")
-            if t < 2:
-                nc.gpsimd.tensor_scalar(h[:], e[:], inv_tot[:], wd_sb[:, t:t + 1], ALU.mult, ALU.mult)
-            else:
-                nc.vector.tensor_scalar(h[:], e[:], inv_tot[:], wd_sb[:, t:t + 1], ALU.mult, ALU.mult)
-            for c in range(LANES):
-                a, b = divmod(c, 2)
-                nc.tensor.matmul(den_ps[a][:, b * P:(b + 1) * P], h[:, c * P:(c + 1) * P], ident[:], is_transpose=True,
-                                 start=(t == 0 and b == 0), stop=(t == LANES - 1 and b == 1))
-            exps.append((e, inv_tot))
-        for t, (e, inv_tot) in enumerate(exps):
-            lane = g_runs[:, :, t, :]
-            e_runs = e[:].rearrange("s (a i) -> s a i", a=2)
-            if t < 2:
-                g_factor = sb.tile([P, 1], F32, name=f"g_factor{t}")
-                nc.scalar.activation(g_factor[:], wt_sb[:, t:t + 1], ACT.Copy, scale=inv_tot[:])
-                nc.scalar.activation(lane, e_runs, ACT.Copy, scale=g_factor[:])
-            else:
-                nc.vector.tensor_scalar(lane, e_runs, inv_tot[:], wt_sb[:, t:t + 1], ALU.mult, ALU.mult)
+        den_ps = [ps.tile([P, HALF], F32, name=f"den_ps{a}", tag=f"bank{6 + a}") for a in range(2)]
+        zs = [sb.tile([P, SLOTS], F32, name=f"z{t}") for t in range(LANES)]
+        es = [sb.tile([P, SLOTS], F32, name=f"e{t}") for t in range(LANES)]
+        hs = [sb.tile([P, SLOTS], F32, name=f"h{t}") for t in range(LANES)]
+        tots = [sb.tile([P, 1], F32, name=f"tot{t}") for t in range(LANES)]
+        inv_tots = [sb.tile([P, 1], F32, name=f"inv_tot{t}") for t in range(LANES)]
 
-        g_codes, g_scales = mx_tiles("g", SLOTS, "after_products")
+        def scaled_scores(t, slots, bank):
+            rows = slice(t * P, (t + 1) * P)
+            scores = ps.tile([P, slots.stop - slots.start], F32, name="scores", tag=bank)
+            nc.tensor.matmul_mx(out=scores[:], lhsT=xd_codes[:, rows].bitcast(FP8X4), lhsT_scale=xd_scales[:, rows],
+                                rhs=c_codes[:, slots].bitcast(FP8X4), rhs_scale=c_scales[:, slots], start=True, stop=True)
+            nc.vector.scalar_tensor_tensor(zs[t][:, slots], scores[:], us_sb[:, t:t + 1], ts_all[:, slots], ALU.mult, ALU.mult)
+
+        def exponentials(t):
+            neg_max = sb.tile([P, 1], F32, name=f"neg_max{t}")
+            nc.vector.tensor_reduce(neg_max[:], zs[t][:], AXIS_X, ALU.max, negate=True)
+            nc.scalar.activation(es[t][:], zs[t][:], ACT.Exp, bias=neg_max[:], scale=1.0, accum_out=tots[t][:])
+
+        def invert_total(t):
+            nc.vector.reciprocal(inv_tots[t][:], tots[t][:])
+
+        def den_terms_of(engine, t, halves_now):
+            slots = slice(halves_now[0] * HALF, (halves_now[-1] + 1) * HALF)
+            engine.tensor_scalar(hs[t][:, slots], es[t][:, slots], inv_tots[t][:], wd_sb[:, t:t + 1], ALU.mult, ALU.mult)
+            for a in halves_now:
+                for b in range(2):
+                    c = 2 * a + b
+                    nc.tensor.matmul(den_ps[a][:, b * P:(b + 1) * P], hs[t][:, c * P:(c + 1) * P], ident[:], is_transpose=True,
+                                     start=(t == 0 and b == 0), stop=(t == LANES - 1 and b == 1))
+
+        def weights_of(engine, t, halves_now):
+            some = slice(halves_now[0], halves_now[-1] + 1)
+            e_runs = es[t][:].rearrange("s (a i) -> s a i", a=2)
+            engine.tensor_scalar(g_runs[:, some, t, :], e_runs[:, some, :], inv_tots[t][:], wt_sb[:, t:t + 1], ALU.mult, ALU.mult)
+
+        def weights_on_scalar(t, pieces):
+            g_factor = sb.tile([P, 1], F32, name=f"g_factor{t}")
+            nc.scalar.activation(g_factor[:], wt_sb[:, t:t + 1], ACT.Copy, scale=inv_tots[t][:])
+            e_runs = es[t][:].rearrange("s (a i) -> s a i", a=2)
+            for some in pieces:
+                nc.scalar.activation(g_runs[:, some, t, :], e_runs[:, some, :], ACT.Copy, scale=g_factor[:])
+
+        for a in range(2):
+            for t in range(2):
+                scaled_scores(t, halves[a], f"bank{2 * a + t}")
+        exponentials(0)
+        exponentials(1)
+        invert_total(0)
+        den_terms_of(nc.gpsimd, 0, (0, 1))
+        weights_on_scalar(0, [slice(0, 2)])
+        invert_total(1)
+        den_terms_of(nc.gpsimd, 1, (0, 1))
+        scaled_scores(2, all_slots, "bank4")
+        scaled_scores(3, all_slots, "bank5")
+        exponentials(2)
+        exponentials(3)
+        weights_on_scalar(1, [slice(0, 1), slice(1, 2)])
+        invert_total(2)
+        den_terms_of(nc.vector, 2, (0, 1))
+        weights_of(nc.vector, 2, (0, 1))
+        invert_total(3)
+
+        g_codes, g_scales = mx_tiles("g", SLOTS)
         inv_den_all = sb.tile([P, SLOTS], F32, name="inv_den_all")
-        g_by_r = [sb.tile([P, HALF * LANES], BF16, name=f"g_by_r{a}", tag=f"late{a}", align_bytes=64) for a in range(2)]
+        g_by_r = [sb.tile([P, HALF * LANES], BF16, name=f"g_by_r{a}", align_bytes=64) for a in range(2)]
         dens = [sb.tile([P, 2], F32, name=f"den{a}") for a in range(2)]
         den_terms = sb.tile([P, P], F32, name="den_terms")
-        for a in range(2):
+        nums = [sb.tile([P, SLOTS], F32, name=f"num{j}") for j in range(LANES)]
+
+        def interleave_weights(a):
             interleave(nc.vector.tensor_copy, g_by_r[a][:], g_staged[:, a * HALF * LANES:(a + 1) * HALF * LANES])
+
+        def quantise_weights(a):
+            nc.vector.quantize_mx(out=g_codes[:, halves[a]].bitcast(FP8X4), scales=g_scales[:, halves[a]], in_=g_by_r[a][:])
+
+        def sum_den(a):
             for b in range(2):
                 nc.scalar.activation(den_terms[:], den_ps[a][:, b * P:(b + 1) * P], ACT.Copy, accum_out=dens[a][:, b:b + 1])
 
-        windows = [sb.tile([P, T], F32, name=f"window{j}") for j in range(2)]
-        nums = [sb.tile([P, SLOTS], F32, name=f"num{j}") for j in range(LANES)]
+        def spread_inverse_den(a):
+            inv_den = sb.tile([P, 2], F32, name=f"inv_den{a}")
+            nc.vector.reciprocal(inv_den[:], dens[a][:])
+            spread_columns(inv_den_all[:, halves[a]], inv_den[:], f"bank{a}")
 
         def numerators(j, slots, bank):
             feats = slice(j * P, (j + 1) * P)
@@ -179,21 +222,23 @@ def tile_attend_gkmeans_pl_kernel(tc, xT, cT, us, ts, wt, wd, offs, out_0, out_1
         def scatter_means(j, slots):
             nc.vector.tensor_tensor(windows[j][:].indirect(listed(slots)), nums[j][:, slots], inv_den_all[:, slots], ALU.mult)
 
-        for a in range(2):
-            nc.vector.quantize_mx(out=g_codes[:, halves[a]].bitcast(FP8X4), scales=g_scales[:, halves[a]], in_=g_by_r[a][:])
-            inv_den = sb.tile([P, 2], F32, name=f"inv_den{a}")
-            nc.vector.reciprocal(inv_den[:], dens[a][:])
-            numerators(0, halves[a], f"bank{a}")
-            spread_columns(inv_den_all[:, halves[a]], inv_den[:], ("bank7", "bank4")[a])
-        all_slots = slice(0, SLOTS)
+        last = LANES - 1
+        den_terms_of(nc.vector, last, (0,))
+        weights_of(nc.vector, last, (0,))
+        den_terms_of(nc.vector, last, (1,))
+        interleave_weights(0)
+        sum_den(0)
+        quantise_weights(0)
+        spread_inverse_den(0)
+        numerators(0, halves[0], "bank2")
+        weights_of(nc.vector, last, (1,))
+        sum_den(1)
+        interleave_weights(1)
+        spread_inverse_den(1)
+        quantise_weights(1)
+        numerators(0, halves[1], "bank3")
         for j in range(1, LANES):
-            numerators(j, all_slots, f"bank{(j + 1) % LANES}")
-
-        for j in range(2):
-            nc.vector.memset(windows[j][:], 0.0)
-        for a in range(2):
-            windows.append(sb.tile([P, T], F32, name=f"window{2 + a}", tag=("late1", "after_products")[a], align_bytes=64))
-            nc.gpsimd.memset(windows[2 + a][:], 0.0)
+            numerators(j, all_slots, ("bank4", "bank5", "bank2")[j - 1])
 
         y_direct = sb.tile([P, DIRECT * LANES], BF16, name="y_direct", align_bytes=64)
         y_staged = sb.tile([P, (T - DIRECT) * LANES], BF16, name="y_staged")
@@ -207,7 +252,6 @@ def tile_attend_gkmeans_pl_kernel(tc, xT, cT, us, ts, wt, wd, offs, out_0, out_1
             copy(staged_runs[:, blocks, j, :], source[:, blocks, :])
 
         out_rows = out_0.rearrange("(p j) n -> p j n", j=LANES)
-        last = LANES - 1
         for j in range(LANES):
             for slots in (halves if j == 0 else [all_slots]):
                 scatter_means(j, slots)

@@ -81,6 +81,7 @@ def tile_attend_gkmeans_pl_kernel(tc, xT, cT, us, ts, wt, wd, offs, out_0, out_1
             for c in range(count):
                 nc.tensor.transpose(spread_ps[:, c * P:(c + 1) * P], cols[:, c:c + 1].to_broadcast([P, P]), ident[:])
             nc.scalar.copy(spread, spread_ps[:])
+            return spread_ps
 
         ts_all = sb.tile([P, SLOTS], F32, name="ts_all")
         spread_columns(ts_all[:], ts_cols[:], "bank7")
@@ -197,6 +198,8 @@ def tile_attend_gkmeans_pl_kernel(tc, xT, cT, us, ts, wt, wd, offs, out_0, out_1
         den_terms = sb.tile([P, P], F32, name="den_terms")
         nums = [sb.tile([P, SLOTS], F32, name=f"num{j}") for j in range(LANES)]
 
+        means = [sb.tile([P, SLOTS], F32, name=f"mean{j}") for j in range(LANES)]
+
         def interleave_weights(a):
             interleave(nc.vector.tensor_copy, g_by_r[a][:], g_staged[:, a * HALF * LANES:(a + 1) * HALF * LANES])
 
@@ -210,7 +213,7 @@ def tile_attend_gkmeans_pl_kernel(tc, xT, cT, us, ts, wt, wd, offs, out_0, out_1
         def spread_inverse_den(a):
             inv_den = sb.tile([P, 2], F32, name=f"inv_den{a}")
             nc.vector.reciprocal(inv_den[:], dens[a][:])
-            spread_columns(inv_den_all[:, halves[a]], inv_den[:], f"bank{a}")
+            return spread_columns(inv_den_all[:, halves[a]], inv_den[:], f"bank{a}")
 
         def numerators(j, slots, bank):
             feats = slice(j * P, (j + 1) * P)
@@ -220,7 +223,7 @@ def tile_attend_gkmeans_pl_kernel(tc, xT, cT, us, ts, wt, wd, offs, out_0, out_1
             nc.scalar.copy(nums[j][:, slots], num_ps[:])
 
         def scatter_means(j, slots):
-            nc.vector.tensor_tensor(windows[j][:].indirect(listed(slots)), nums[j][:, slots], inv_den_all[:, slots], ALU.mult)
+            nc.vector.tensor_copy(windows[j][:].indirect(listed(slots)), means[j][:, slots])
 
         last = LANES - 1
         den_terms_of(nc.vector, last, (0,))
@@ -229,16 +232,19 @@ def tile_attend_gkmeans_pl_kernel(tc, xT, cT, us, ts, wt, wd, offs, out_0, out_1
         interleave_weights(0)
         sum_den(0)
         quantise_weights(0)
-        spread_inverse_den(0)
         numerators(0, halves[0], "bank2")
+        spread_ps = spread_inverse_den(0)
+        nc.vector.tensor_tensor(means[0][:, halves[0]], spread_ps[:], nums[0][:, halves[0]], ALU.mult)
         weights_of(nc.vector, last, (1,))
         sum_den(1)
         interleave_weights(1)
-        spread_inverse_den(1)
+        spread_ps = spread_inverse_den(1)
         quantise_weights(1)
         numerators(0, halves[1], "bank3")
+        nc.vector.tensor_tensor(means[0][:, halves[1]], spread_ps[:], nums[0][:, halves[1]], ALU.mult)
         for j in range(1, LANES):
             numerators(j, all_slots, ("bank4", "bank5", "bank2")[j - 1])
+            nc.gpsimd.tensor_tensor(means[j][:], nums[j][:], inv_den_all[:], ALU.mult)
 
         y_direct = sb.tile([P, DIRECT * LANES], BF16, name="y_direct", align_bytes=64)
         y_staged = sb.tile([P, (T - DIRECT) * LANES], BF16, name="y_staged")

@@ -19,8 +19,7 @@ LANES = 4
 D, R, SLOTS, T = 512, 512, 512, 2048
 FLOPS = 2 * 2 * D * R * SLOTS
 HALF = SLOTS // 2
-BLOCK = 256
-DIRECT = 512
+SCATTER_ORDER = (0, 2, 1, 3)
 
 
 def tile_attend_gkmeans_pl_kernel(tc, xT, cT, us, ts, wt, wd, offs, out_0, out_1, out_2):
@@ -36,17 +35,17 @@ def tile_attend_gkmeans_pl_kernel(tc, xT, cT, us, ts, wt, wd, offs, out_0, out_1
 
         def interleave(copy, lanes_last, staged):
             copy(
-                lanes_last.rearrange("p (b c n j) -> p b c j n", c=BLOCK // 4, n=4, j=LANES),
-                staged.rearrange("p (b j c n) -> p b c j n", j=LANES, c=BLOCK // 4, n=4),
+                lanes_last.rearrange("p (c n j) -> p c j n", n=4, j=LANES),
+                staged.rearrange("p j (c n) -> p c j n", n=4),
             )
 
+        x_raw = sb.tile([P, LANES, R], F32, name="x_raw")
+        nc.sync.dma_start(out=x_raw[:], in_=xT.rearrange("(p j) r -> p j r", j=LANES))
         offsets = sb.tile([P, SLOTS // 16], U16, name="offsets")
         nc.sync.dma_start(offsets[:], offs)
         ts_window = sb.tile([P, T], F32, name="ts_window", tag="ts_then_window2")
         nc.scalar.dma_start(out=ts_window[P - 1:P, :], in_=ts[0:1, :])
         nc.vector.memset(ts_window[0:P - 1, :], 0.0)
-        x_raw = sb.tile([P, LANES, R], F32, name="x_raw")
-        nc.sync.dma_start(out=x_raw[:], in_=xT.rearrange("(p j) r -> p j r", j=LANES))
         c_planes = [sb.tile([P, T], F32, name=f"c_plane{j}") for j in range(LANES)]
         c_rows = cT.rearrange("(p j) n -> p j n", j=LANES)
         for j in range(LANES):
@@ -55,7 +54,7 @@ def tile_attend_gkmeans_pl_kernel(tc, xT, cT, us, ts, wt, wd, offs, out_0, out_1
         row_factors = []
         for name, vec in (("us_sb", us), ("wt_sb", wt), ("wd_sb", wd)):
             tile = sb.tile([P, LANES], F32, name=name)
-            nc.scalar.dma_start(out=tile[:], in_=vec.rearrange("(s t) o -> s (t o)", t=LANES))
+            nc.sync.dma_start(out=tile[:], in_=vec.rearrange("(s t) o -> s (t o)", t=LANES))
             row_factors.append(tile)
         us_sb, wt_sb, wd_sb = row_factors
 
@@ -88,8 +87,8 @@ def tile_attend_gkmeans_pl_kernel(tc, xT, cT, us, ts, wt, wd, offs, out_0, out_1
 
         x_by_d = sb.tile([P, R * LANES], BF16, name="x_by_d", align_bytes=64)
         nc.scalar.copy(
-            x_by_d[:].rearrange("p (t s j) -> p s j t", t=LANES, j=LANES),
-            x_raw[:].rearrange("p j (s t) -> p s j t", t=LANES),
+            x_by_d[:].rearrange("p (t s j) -> p s t j", t=LANES, j=LANES),
+            x_raw[:].rearrange("p j (s t) -> p s t j", t=LANES),
         )
         xd_codes, xd_scales = mx_tiles("xd", R)
         nc.vector.quantize_mx(out=xd_codes[:].bitcast(FP8X4), scales=xd_scales[:], in_=x_by_d[:])
@@ -201,7 +200,7 @@ def tile_attend_gkmeans_pl_kernel(tc, xT, cT, us, ts, wt, wd, offs, out_0, out_1
         means = [sb.tile([P, SLOTS], F32, name=f"mean{j}") for j in range(LANES)]
 
         def interleave_weights(a):
-            interleave(nc.vector.tensor_copy, g_by_r[a][:], g_staged[:, a * HALF * LANES:(a + 1) * HALF * LANES])
+            interleave(nc.vector.tensor_copy, g_by_r[a][:], g_runs[:, a])
 
         def quantise_weights(a):
             nc.vector.quantize_mx(out=g_codes[:, halves[a]].bitcast(FP8X4), scales=g_scales[:, halves[a]], in_=g_by_r[a][:])
@@ -232,9 +231,8 @@ def tile_attend_gkmeans_pl_kernel(tc, xT, cT, us, ts, wt, wd, offs, out_0, out_1
         interleave_weights(0)
         sum_den(0)
         quantise_weights(0)
+        spread_inverse_den(0)
         numerators(0, halves[0], "bank2")
-        spread_ps = spread_inverse_den(0)
-        nc.vector.tensor_tensor(means[0][:, halves[0]], spread_ps[:], nums[0][:, halves[0]], ALU.mult)
         weights_of(nc.vector, last, (1,))
         sum_den(1)
         interleave_weights(1)
@@ -242,49 +240,52 @@ def tile_attend_gkmeans_pl_kernel(tc, xT, cT, us, ts, wt, wd, offs, out_0, out_1
         quantise_weights(1)
         numerators(0, halves[1], "bank3")
         nc.vector.tensor_tensor(means[0][:, halves[1]], spread_ps[:], nums[0][:, halves[1]], ALU.mult)
-        for j in range(1, LANES):
-            numerators(j, all_slots, ("bank4", "bank5", "bank2")[j - 1])
+        for j, bank in zip(SCATTER_ORDER[1:], ("bank4", "bank5", "bank2")):
+            numerators(j, all_slots, bank)
             nc.gpsimd.tensor_tensor(means[j][:], nums[j][:], inv_den_all[:], ALU.mult)
 
-        y_direct = sb.tile([P, DIRECT * LANES], BF16, name="y_direct", align_bytes=64)
-        y_staged = sb.tile([P, (T - DIRECT) * LANES], BF16, name="y_staged")
-        staged_runs = y_staged[:].rearrange("p (b j n) -> p b j n", j=LANES, n=BLOCK)
+        staged_cols = (slice(0, 512), slice(512, 640))
+        scalar_cols = (slice(640, 1152), slice(1152, 1280))
+        gpsimd_cols = (slice(1280, 1792), slice(1792, 2048))
+        stores = (staged_cols, scalar_cols, gpsimd_cols[:1], gpsimd_cols[1:])
+        staged_width = staged_cols[-1].stop
 
-        def round_direct(j):
-            nc.scalar.copy(y_direct[:].rearrange("p (n j) -> p n j", j=LANES)[:, :, j], windows[j][:, 0:DIRECT])
+        y_by_d = {cols.start: sb.tile([P, (cols.stop - cols.start) * LANES], BF16, name=f"y_by_d{cols.start}", align_bytes=64)
+                  for cols in staged_cols + scalar_cols + gpsimd_cols}
+        y_staged = sb.tile([P, LANES, staged_width], BF16, name="y_staged", tag="staged_then_codes", align_bytes=64)
 
-        def round_staged(copy, j, blocks):
-            source = windows[j][:, DIRECT:T].rearrange("p (b n) -> p b n", n=BLOCK)
-            copy(staged_runs[:, blocks, j, :], source[:, blocks, :])
+        def round_on_gpsimd(rounded, source):
+            nc.gpsimd.tensor_scalar(rounded, source, 1.0, 1.0, ALU.mult, ALU.mult)
+
+        def round_into_lane(copy, j, cols):
+            copy(y_by_d[cols.start][:].rearrange("p (n j) -> p n j", j=LANES)[:, :, j], windows[j][:, cols])
 
         out_rows = out_0.rearrange("(p j) n -> p j n", j=LANES)
-        for j in range(LANES):
-            for slots in (halves if j == 0 else [all_slots]):
-                scatter_means(j, slots)
+        for j in SCATTER_ORDER:
+            if j == 0:
+                nc.vector.tensor_tensor(windows[0][:].indirect(listed(halves[0])), nums[0][:, halves[0]],
+                                        inv_den_all[:, halves[0]], ALU.mult)
+                scatter_means(0, halves[1])
+            else:
+                scatter_means(j, all_slots)
             nc.sync.dma_start(out=out_rows[:, j, :], in_=windows[j][:])
-            if j < last:
-                round_staged(nc.scalar.copy, j, slice(0, (T - DIRECT) // BLOCK))
-            round_direct(j)
-
-        chunks = []
-        lo = 0
-        for count, copy in ((2, nc.vector.tensor_copy), (2, nc.vector.tensor_copy), (1, nc.scalar.copy), (1, nc.scalar.copy)):
-            chunks.append((slice(lo, lo + count), copy))
-            lo = lo + count
-        for blocks, copy in chunks:
-            round_staged(copy, last, blocks)
-        ready = [(slice(0, DIRECT), y_direct)]
-        for k, (blocks, copy) in enumerate(chunks):
-            y_by_d = sb.tile([P, (blocks.stop - blocks.start) * BLOCK * LANES], BF16, name=f"y_by_d{k}", align_bytes=64)
-            interleave(copy, y_by_d[:], y_staged[:, blocks.start * BLOCK * LANES:blocks.stop * BLOCK * LANES])
-            ready.append((slice(DIRECT + blocks.start * BLOCK, DIRECT + blocks.stop * BLOCK), y_by_d))
+            round_staged = (nc.scalar.copy, round_on_gpsimd, round_on_gpsimd, nc.vector.tensor_copy)[j]
+            round_staged(y_staged[:, j, :], windows[j][:, 0:staged_width])
+            for cols in scalar_cols:
+                round_into_lane(nc.scalar.copy, j, cols)
+            for cols in gpsimd_cols:
+                round_into_lane(round_on_gpsimd if j < 2 else nc.scalar.copy, j, cols)
 
         y_scales = sb.tile([P, T], U8, name="y_scales", align_bytes=64)
         words_out = out_1[0].rearrange("p n l -> p (n l)").bitcast(I32)
-        for k, (cols, y_by_d) in enumerate(ready):
-            y_codes = sb.tile([P, cols.stop - cols.start], U32, name=f"y_codes{k}", align_bytes=64)
-            nc.vector.quantize_mx(out=y_codes[:].bitcast(FP8X4), scales=y_scales[:, cols], in_=y_by_d[:])
-            nc.sync.dma_start(out=words_out[:, cols], in_=y_codes[:].bitcast(I32))
+        for cols in staged_cols:
+            interleave(nc.vector.tensor_copy, y_by_d[cols.start][:], y_staged[:, :, cols])
+        for k, pieces in enumerate(stores):
+            lo, hi = pieces[0].start, pieces[-1].stop
+            y_codes = sb.tile([P, hi - lo], U32, name=f"y_codes{k}", tag="staged_then_codes" if k == 1 else "", align_bytes=64)
+            for cols in pieces:
+                nc.vector.quantize_mx(out=y_codes[:, cols.start - lo:cols.stop - lo].bitcast(FP8X4), scales=y_scales[:, cols],
+                                      in_=y_by_d[cols.start][:])
+            nc.sync.dma_start(out=words_out[:, lo:hi], in_=y_codes[:].bitcast(I32))
         for q in range(4):
-            queue = nc.sync if q % 2 == 0 else nc.scalar
-            queue.dma_start(out=out_2[0, 4 * q:4 * q + 4, :].bitcast(I32), in_=y_scales[32 * q:32 * q + 4, :].bitcast(I32))
+            nc.sync.dma_start(out=out_2[0, 4 * q:4 * q + 4, :].bitcast(I32), in_=y_scales[32 * q:32 * q + 4, :].bitcast(I32))

@@ -80,7 +80,6 @@ def tile_attend_gkmeans_pl_kernel(tc, xT, cT, us, ts, wt, wd, offs, out_0, out_1
             for c in range(count):
                 nc.tensor.transpose(spread_ps[:, c * P:(c + 1) * P], cols[:, c:c + 1].to_broadcast([P, P]), ident[:])
             nc.scalar.copy(spread, spread_ps[:])
-            return spread_ps
 
         ts_all = sb.tile([P, SLOTS], F32, name="ts_all")
         spread_columns(ts_all[:], ts_cols[:], "bank7")
@@ -152,11 +151,12 @@ def tile_attend_gkmeans_pl_kernel(tc, xT, cT, us, ts, wt, wd, offs, out_0, out_1
         def den_terms_of(engine, t, halves_now):
             slots = slice(halves_now[0] * HALF, (halves_now[-1] + 1) * HALF)
             engine.tensor_scalar(hs[t][:, slots], es[t][:, slots], inv_tots[t][:], wd_sb[:, t:t + 1], ALU.mult, ALU.mult)
-            for a in halves_now:
-                for b in range(2):
-                    c = 2 * a + b
-                    nc.tensor.matmul(den_ps[a][:, b * P:(b + 1) * P], hs[t][:, c * P:(c + 1) * P], ident[:], is_transpose=True,
-                                     start=(t == 0 and b == 0), stop=(t == LANES - 1 and b == 1))
+
+        def add_turned(t, a):
+            for b in range(2):
+                c = 2 * a + b
+                nc.tensor.matmul(den_ps[a][:, b * P:(b + 1) * P], hs[t][:, c * P:(c + 1) * P], ident[:], is_transpose=True,
+                                 start=(t == 0 and b == 0), stop=(t == LANES - 1 and b == 1))
 
         def weights_of(engine, t, halves_now):
             some = slice(halves_now[0], halves_now[-1] + 1)
@@ -177,6 +177,8 @@ def tile_attend_gkmeans_pl_kernel(tc, xT, cT, us, ts, wt, wd, offs, out_0, out_1
         exponentials(1)
         invert_total(0)
         den_terms_of(nc.gpsimd, 0, (0, 1))
+        add_turned(0, 0)
+        add_turned(0, 1)
         weights_on_scalar(0, [slice(0, 2)])
         invert_total(1)
         den_terms_of(nc.gpsimd, 1, (0, 1))
@@ -184,20 +186,22 @@ def tile_attend_gkmeans_pl_kernel(tc, xT, cT, us, ts, wt, wd, offs, out_0, out_1
         scaled_scores(3, all_slots, "bank5")
         exponentials(2)
         exponentials(3)
-        weights_on_scalar(1, [slice(0, 1), slice(1, 2)])
+        weights_on_scalar(1, [slice(0, 1)])
         invert_total(2)
         den_terms_of(nc.vector, 2, (0, 1))
         weights_of(nc.vector, 2, (0, 1))
         invert_total(3)
 
         g_codes, g_scales = mx_tiles("g", SLOTS)
-        inv_den_all = sb.tile([P, SLOTS], F32, name="inv_den_all")
+        inv_den_all = [sb.tile([P, HALF], F32, name=f"inv_den_all{a}", tag=f"inv_den_then_lanes{a}", align_bytes=64) for a in range(2)]
         g_by_r = [sb.tile([P, HALF * LANES], BF16, name=f"g_by_r{a}", align_bytes=64) for a in range(2)]
         dens = [sb.tile([P, 2], F32, name=f"den{a}") for a in range(2)]
         den_terms = sb.tile([P, P], F32, name="den_terms")
-        nums = [sb.tile([P, SLOTS], F32, name=f"num{j}") for j in range(LANES)]
+        nums = {j: sb.tile([P, SLOTS], F32, name=f"num{j}", tag=f"num{j}", align_bytes=64) for j in (0, 3)}
 
-        means = [sb.tile([P, SLOTS], F32, name=f"mean{j}") for j in range(LANES)]
+        means = {j: sb.tile([P, SLOTS], F32, name=f"mean{j}") for j in range(1, LANES)}
+
+        inv_dens = []
 
         def interleave_weights(a):
             interleave(nc.vector.tensor_copy, g_by_r[a][:], g_runs[:, a])
@@ -212,7 +216,8 @@ def tile_attend_gkmeans_pl_kernel(tc, xT, cT, us, ts, wt, wd, offs, out_0, out_1
         def spread_inverse_den(a):
             inv_den = sb.tile([P, 2], F32, name=f"inv_den{a}")
             nc.vector.reciprocal(inv_den[:], dens[a][:])
-            return spread_columns(inv_den_all[:, halves[a]], inv_den[:], f"bank{a}")
+            spread_columns(inv_den_all[a][:], inv_den[:], f"bank{a}")
+            inv_dens.append(inv_den)
 
         def numerators(j, slots, bank):
             feats = slice(j * P, (j + 1) * P)
@@ -224,68 +229,94 @@ def tile_attend_gkmeans_pl_kernel(tc, xT, cT, us, ts, wt, wd, offs, out_0, out_1
         def scatter_means(j, slots):
             nc.vector.tensor_copy(windows[j][:].indirect(listed(slots)), means[j][:, slots])
 
+        def means_by_slot(j, product_bank, turned_bank):
+            feats = slice(j * P, (j + 1) * P)
+            num_by_slot = ps.tile([P, LANES, P], F32, name="num_by_slot", tag=product_bank)
+            mean_by_slot = sb.tile([P, LANES, P], F32, name=f"mean_by_slot{j}", tag=f"by_slot{j}", align_bytes=64)
+            mean_ps = ps.tile([P, LANES, P], F32, name="mean_ps", tag=turned_bank)
+            for c in range(LANES):
+                slots = slice(c * P, (c + 1) * P)
+                nc.tensor.matmul_mx(out=num_by_slot[:, c, :], lhsT=g_codes[:, slots].bitcast(FP8X4), lhsT_scale=g_scales[:, slots],
+                                    rhs=xr_codes[:, feats].bitcast(FP8X4), rhs_scale=xr_scales[:, feats], start=True, stop=True)
+            for c in range(LANES):
+                nc.scalar.activation(mean_by_slot[:, c, :], num_by_slot[:, c, :], ACT.Copy, scale=inv_dens[c // 2][:, c % 2:c % 2 + 1])
+                nc.tensor.transpose(mean_ps[:, c, :], mean_by_slot[:, c, :], ident[:])
+            nc.scalar.copy(means[j][:], mean_ps[:].rearrange("p c i -> p (c i)"))
+
         last = LANES - 1
         den_terms_of(nc.vector, last, (0,))
+        for t in (2, 1, 3):
+            add_turned(t, 0)
         weights_of(nc.vector, last, (0,))
         den_terms_of(nc.vector, last, (1,))
+        for t in (2, 1, 3):
+            add_turned(t, 1)
         interleave_weights(0)
-        sum_den(0)
+        nc.vector.tensor_reduce(dens[0][:], den_ps[0][:].rearrange("i (b s) -> i b s", b=2), AXIS_X, ALU.add)
         quantise_weights(0)
         spread_inverse_den(0)
         numerators(0, halves[0], "bank2")
-        weights_of(nc.vector, last, (1,))
+        weights_of(nc.vector, 1, (1,))
         sum_den(1)
+        weights_of(nc.vector, last, (1,))
+        spread_inverse_den(1)
         interleave_weights(1)
-        spread_ps = spread_inverse_den(1)
         quantise_weights(1)
         numerators(0, halves[1], "bank3")
-        nc.vector.tensor_tensor(means[0][:, halves[1]], spread_ps[:], nums[0][:, halves[1]], ALU.mult)
-        for j, bank in zip(SCATTER_ORDER[1:], ("bank4", "bank5", "bank2")):
-            numerators(j, all_slots, bank)
-            nc.gpsimd.tensor_tensor(means[j][:], nums[j][:], inv_den_all[:], ALU.mult)
+        means_by_slot(SCATTER_ORDER[1], "bank4", "bank5")
+        means_by_slot(SCATTER_ORDER[2], "bank2", "bank6")
+        numerators(last, all_slots, "bank4")
+        for a, slots in enumerate(halves):
+            nc.gpsimd.tensor_tensor(means[last][:, slots], nums[last][:, slots], inv_den_all[a][:], ALU.mult)
 
-        staged_cols = (slice(0, 512), slice(512, 640))
-        scalar_cols = (slice(640, 1152), slice(1152, 1280))
+        staged_cols, scalar_cols = slice(0, 640), slice(640, 1280)
         gpsimd_cols = (slice(1280, 1792), slice(1792, 2048))
-        stores = (staged_cols, scalar_cols, gpsimd_cols[:1], gpsimd_cols[1:])
-        staged_width = staged_cols[-1].stop
+        pieces = (slice(0, 512), slice(512, 640))
 
-        y_by_d = {cols.start: sb.tile([P, (cols.stop - cols.start) * LANES], BF16, name=f"y_by_d{cols.start}", align_bytes=64)
-                  for cols in staged_cols + scalar_cols + gpsimd_cols}
-        y_staged = sb.tile([P, LANES, staged_width], BF16, name="y_staged", tag="staged_then_codes", align_bytes=64)
+        def lanes_tile(cols, tag):
+            return sb.tile([P, (cols.stop - cols.start) * LANES], BF16, name=f"y_by_d{cols.start}", tag=tag, align_bytes=64)
+
+        y_staged = sb.tile([P, LANES, staged_cols.stop], BF16, name="y_staged", tag="num3", align_bytes=64)
+        y_of_vector = lanes_tile(staged_cols, "")
+        y_of_scalar = lanes_tile(scalar_cols, f"by_slot{SCATTER_ORDER[2]}")
+        y_of_gpsimd = [lanes_tile(cols, f"inv_den_then_lanes{a}") for a, cols in enumerate(gpsimd_cols)]
 
         def round_on_gpsimd(rounded, source):
             nc.gpsimd.tensor_scalar(rounded, source, 1.0, 1.0, ALU.mult, ALU.mult)
 
-        def round_into_lane(copy, j, cols):
-            copy(y_by_d[cols.start][:].rearrange("p (n j) -> p n j", j=LANES)[:, :, j], windows[j][:, cols])
+        def lane(y_by_d, j):
+            return y_by_d[:].rearrange("p (n j) -> p n j", j=LANES)[:, :, j]
 
         out_rows = out_0.rearrange("(p j) n -> p j n", j=LANES)
         for j in SCATTER_ORDER:
             if j == 0:
-                nc.vector.tensor_tensor(windows[0][:].indirect(listed(halves[0])), nums[0][:, halves[0]],
-                                        inv_den_all[:, halves[0]], ALU.mult)
-                scatter_means(0, halves[1])
+                for a, slots in enumerate(halves):
+                    nc.vector.tensor_tensor(windows[0][:].indirect(listed(slots)), nums[0][:, slots], inv_den_all[a][:], ALU.mult)
             else:
                 scatter_means(j, all_slots)
             nc.sync.dma_start(out=out_rows[:, j, :], in_=windows[j][:])
-            round_staged = (nc.scalar.copy, round_on_gpsimd, round_on_gpsimd, nc.vector.tensor_copy)[j]
-            round_staged(y_staged[:, j, :], windows[j][:, 0:staged_width])
-            for cols in scalar_cols:
-                round_into_lane(nc.scalar.copy, j, cols)
-            for cols in gpsimd_cols:
-                round_into_lane(round_on_gpsimd if j < 2 else nc.scalar.copy, j, cols)
+            nc.scalar.copy(lane(y_of_scalar, j), windows[j][:, scalar_cols])
+            round_staged = round_on_gpsimd if j < last else nc.vector.tensor_copy
+            round_staged(y_staged[:, j, :], windows[j][:, staged_cols])
+            round_lane = round_on_gpsimd if j < 2 else nc.scalar.copy
+            for cols, y_by_d in zip(gpsimd_cols, y_of_gpsimd):
+                round_lane(lane(y_by_d, j), windows[j][:, cols])
 
         y_scales = sb.tile([P, T], U8, name="y_scales", align_bytes=64)
         words_out = out_1[0].rearrange("p n l -> p (n l)").bitcast(I32)
-        for cols in staged_cols:
-            interleave(nc.vector.tensor_copy, y_by_d[cols.start][:], y_staged[:, :, cols])
-        for k, pieces in enumerate(stores):
-            lo, hi = pieces[0].start, pieces[-1].stop
-            y_codes = sb.tile([P, hi - lo], U32, name=f"y_codes{k}", tag="staged_then_codes" if k == 1 else "", align_bytes=64)
-            for cols in pieces:
-                nc.vector.quantize_mx(out=y_codes[:, cols.start - lo:cols.stop - lo].bitcast(FP8X4), scales=y_scales[:, cols],
-                                      in_=y_by_d[cols.start][:])
-            nc.sync.dma_start(out=words_out[:, lo:hi], in_=y_codes[:].bitcast(I32))
+        for piece in pieces:
+            interleave(nc.vector.tensor_copy, y_of_vector[:, piece.start * LANES:piece.stop * LANES], y_staged[:, :, piece])
+
+        def quantise_and_store(cols, y_by_d, parts, tag):
+            y_codes = sb.tile([P, cols.stop - cols.start], U32, name=f"y_codes{cols.start}", tag=tag, align_bytes=64)
+            for part in parts:
+                nc.vector.quantize_mx(out=y_codes[:, part].bitcast(FP8X4), scales=y_scales[:, cols][:, part],
+                                      in_=y_by_d[:, part.start * LANES:part.stop * LANES])
+            nc.sync.dma_start(out=words_out[:, cols], in_=y_codes[:].bitcast(I32))
+
+        quantise_and_store(staged_cols, y_of_vector, pieces, "")
+        quantise_and_store(scalar_cols, y_of_scalar, pieces, "num3")
+        for cols, y_by_d in zip(gpsimd_cols, y_of_gpsimd):
+            quantise_and_store(cols, y_by_d, [slice(0, cols.stop - cols.start)], "")
         for q in range(4):
             nc.sync.dma_start(out=out_2[0, 4 * q:4 * q + 4, :].bitcast(I32), in_=y_scales[32 * q:32 * q + 4, :].bitcast(I32))

@@ -20,6 +20,7 @@ D, R, SLOTS, T = 512, 512, 512, 2048
 FLOPS = 2 * 2 * D * R * SLOTS
 HALF = SLOTS // 2
 SCATTER_ORDER = (0, 2, 1, 3)
+GROUP = 512
 
 
 def tile_attend_gkmeans_pl_kernel(tc, xT, cT, us, ts, wt, wd, offs, out_0, out_1, out_2):
@@ -102,8 +103,17 @@ def tile_attend_gkmeans_pl_kernel(tc, xT, cT, us, ts, wt, wd, offs, out_0, out_1
                 x_by_r[:, u * 2 * R:(u + 1) * 2 * R].rearrange("s (e p t) -> s e p t", e=2, t=LANES),
                 turned[:].bitcast(BF16).rearrange("s (t p e) -> s e p t", t=LANES, e=2),
             )
-        xr_codes, xr_scales = mx_tiles("xr", D)
-        nc.vector.quantize_mx(out=xr_codes[:].bitcast(FP8X4), scales=xr_scales[:], in_=x_by_r[:])
+        xr_tiles = {}
+
+        def quantise_features(planes, tag):
+            codes, scales = mx_tiles(f"xr{planes.start}", len(planes) * P, tag)
+            nc.vector.quantize_mx(out=codes[:].bitcast(FP8X4), scales=scales[:],
+                                  in_=x_by_r[:, planes.start * P * LANES:planes.stop * P * LANES])
+            for j in planes:
+                feats = slice((j - planes.start) * P, (j - planes.start + 1) * P)
+                xr_tiles[j] = (codes[:, feats].bitcast(FP8X4), scales[:, feats])
+
+        quantise_features(range(0, 2), "")
 
         c_by_d = sb.tile([P, SLOTS * LANES], BF16, name="c_by_d", tag="c_then_window3", align_bytes=64)
         c_lanes = c_by_d[:].rearrange("p (i j) -> p i j", j=LANES)
@@ -194,7 +204,7 @@ def tile_attend_gkmeans_pl_kernel(tc, xT, cT, us, ts, wt, wd, offs, out_0, out_1
 
         g_codes, g_scales = mx_tiles("g", SLOTS)
         inv_den_all = [sb.tile([P, HALF], F32, name=f"inv_den_all{a}", tag=f"inv_den_then_lanes{a}", align_bytes=64) for a in range(2)]
-        g_by_r = [sb.tile([P, HALF * LANES], BF16, name=f"g_by_r{a}", align_bytes=64) for a in range(2)]
+        g_by_r = [sb.tile([P, HALF * LANES], BF16, name=f"g_by_r{a}", tag=f"g_by_r{a}", align_bytes=64) for a in range(2)]
         dens = [sb.tile([P, 2], F32, name=f"den{a}") for a in range(2)]
         den_terms = sb.tile([P, P], F32, name="den_terms")
         nums = {j: sb.tile([P, SLOTS], F32, name=f"num{j}", tag=f"num{j}", align_bytes=64) for j in (0, 3)}
@@ -220,9 +230,8 @@ def tile_attend_gkmeans_pl_kernel(tc, xT, cT, us, ts, wt, wd, offs, out_0, out_1
             inv_dens.append(inv_den)
 
         def numerators(j, slots, bank):
-            feats = slice(j * P, (j + 1) * P)
             num_ps = ps.tile([P, slots.stop - slots.start], F32, name="num_ps", tag=bank)
-            nc.tensor.matmul_mx(out=num_ps[:], lhsT=xr_codes[:, feats].bitcast(FP8X4), lhsT_scale=xr_scales[:, feats],
+            nc.tensor.matmul_mx(out=num_ps[:], lhsT=xr_tiles[j][0], lhsT_scale=xr_tiles[j][1],
                                 rhs=g_codes[:, slots].bitcast(FP8X4), rhs_scale=g_scales[:, slots], start=True, stop=True)
             nc.scalar.copy(nums[j][:, slots], num_ps[:])
 
@@ -230,14 +239,13 @@ def tile_attend_gkmeans_pl_kernel(tc, xT, cT, us, ts, wt, wd, offs, out_0, out_1
             nc.vector.tensor_copy(windows[j][:].indirect(listed(slots)), means[j][:, slots])
 
         def means_by_slot(j, product_bank, turned_bank):
-            feats = slice(j * P, (j + 1) * P)
             num_by_slot = ps.tile([P, LANES, P], F32, name="num_by_slot", tag=product_bank)
             mean_by_slot = sb.tile([P, LANES, P], F32, name=f"mean_by_slot{j}", tag=f"by_slot{j}", align_bytes=64)
             mean_ps = ps.tile([P, LANES, P], F32, name="mean_ps", tag=turned_bank)
             for c in range(LANES):
                 slots = slice(c * P, (c + 1) * P)
                 nc.tensor.matmul_mx(out=num_by_slot[:, c, :], lhsT=g_codes[:, slots].bitcast(FP8X4), lhsT_scale=g_scales[:, slots],
-                                    rhs=xr_codes[:, feats].bitcast(FP8X4), rhs_scale=xr_scales[:, feats], start=True, stop=True)
+                                    rhs=xr_tiles[j][0], rhs_scale=xr_tiles[j][1], start=True, stop=True)
             for c in range(LANES):
                 nc.scalar.activation(mean_by_slot[:, c, :], num_by_slot[:, c, :], ACT.Copy, scale=inv_dens[c // 2][:, c % 2:c % 2 + 1])
                 nc.tensor.transpose(mean_ps[:, c, :], mean_by_slot[:, c, :], ident[:])
@@ -256,6 +264,7 @@ def tile_attend_gkmeans_pl_kernel(tc, xT, cT, us, ts, wt, wd, offs, out_0, out_1
         quantise_weights(0)
         spread_inverse_den(0)
         numerators(0, halves[0], "bank2")
+        quantise_features(range(2, 4), "g_by_r0")
         weights_of(nc.vector, 1, (1,))
         sum_den(1)
         weights_of(nc.vector, last, (1,))
@@ -302,7 +311,7 @@ def tile_attend_gkmeans_pl_kernel(tc, xT, cT, us, ts, wt, wd, offs, out_0, out_1
             for cols, y_by_d in zip(gpsimd_cols, y_of_gpsimd):
                 round_lane(lane(y_by_d, j), windows[j][:, cols])
 
-        y_scales = sb.tile([P, T], U8, name="y_scales", align_bytes=64)
+        y_scales = sb.tile([P, GROUP], U8, name="y_scales", align_bytes=64)
         words_out = out_1[0].rearrange("p n l -> p (n l)").bitcast(I32)
         for piece in pieces:
             interleave(nc.vector.tensor_copy, y_of_vector[:, piece.start * LANES:piece.stop * LANES], y_staged[:, :, piece])
@@ -310,13 +319,15 @@ def tile_attend_gkmeans_pl_kernel(tc, xT, cT, us, ts, wt, wd, offs, out_0, out_1
         def quantise_and_store(cols, y_by_d, parts, tag):
             y_codes = sb.tile([P, cols.stop - cols.start], U32, name=f"y_codes{cols.start}", tag=tag, align_bytes=64)
             for part in parts:
-                nc.vector.quantize_mx(out=y_codes[:, part].bitcast(FP8X4), scales=y_scales[:, cols][:, part],
+                k, within = divmod(cols.start + part.start, GROUP)
+                nc.vector.quantize_mx(out=y_codes[:, part].bitcast(FP8X4), scales=y_scales[4 * k:P, within:within + part.stop - part.start],
                                       in_=y_by_d[:, part.start * LANES:part.stop * LANES])
             nc.sync.dma_start(out=words_out[:, cols], in_=y_codes[:].bitcast(I32))
 
         quantise_and_store(staged_cols, y_of_vector, pieces, "")
-        quantise_and_store(scalar_cols, y_of_scalar, pieces, "num3")
+        quantise_and_store(scalar_cols, y_of_scalar, (slice(0, 128), slice(128, 384), slice(384, 640)), "num3")
         for cols, y_by_d in zip(gpsimd_cols, y_of_gpsimd):
-            quantise_and_store(cols, y_by_d, [slice(0, cols.stop - cols.start)], "")
+            quantise_and_store(cols, y_by_d, [slice(lo, lo + 256) for lo in range(0, cols.stop - cols.start, 256)], "")
+        scales_out = out_2[0].rearrange("(q r) (k c) -> q k r c", r=4, c=GROUP)
         for q in range(4):
-            nc.sync.dma_start(out=out_2[0, 4 * q:4 * q + 4, :].bitcast(I32), in_=y_scales[32 * q:32 * q + 4, :].bitcast(I32))
+            nc.sync.dma_start(out=scales_out[q].bitcast(I32), in_=y_scales[32 * q:32 * q + 16, :].bitcast(I32))

@@ -84,6 +84,8 @@ def tile_attend_gkmeans_pl_kernel(tc, xT, cT, us, ts, wt, wd, offs, out_0, out_1
 
         ts_all = sb.tile([P, SLOTS], F32, name="ts_all")
         spread_columns(ts_all[:], ts_cols[:], "bank7")
+        neg_us = sb.tile([P, LANES], F32, name="neg_us")
+        nc.gpsimd.tensor_scalar(neg_us[:], us_sb[:], -1.0, 1.0, ALU.mult, ALU.mult)
 
         x_by_d = sb.tile([P, R * LANES], BF16, name="x_by_d", align_bytes=64)
         nc.scalar.copy(
@@ -124,10 +126,9 @@ def tile_attend_gkmeans_pl_kernel(tc, xT, cT, us, ts, wt, wd, offs, out_0, out_1
         def listed(slots):
             return offsets[:, slots.start // 16:slots.stop // 16]
 
-        for slots in halves:
-            nc.vector.tensor_copy(c_lanes[:, slots, 3], c_planes[3][:].indirect(listed(slots)))
         c_codes, c_scales = mx_tiles("c", SLOTS)
         for slots in halves:
+            nc.vector.tensor_copy(c_lanes[:, slots, 3], c_planes[3][:].indirect(listed(slots)))
             nc.vector.quantize_mx(out=c_codes[:, slots].bitcast(FP8X4), scales=c_scales[:, slots],
                                   in_=c_by_d[:, slots.start * LANES:slots.stop * LANES])
         windows.append(sb.tile([P, T], F32, name="window3", tag="c_then_window3", align_bytes=64))
@@ -136,24 +137,40 @@ def tile_attend_gkmeans_pl_kernel(tc, xT, cT, us, ts, wt, wd, offs, out_0, out_1
         all_slots = slice(0, SLOTS)
         g_staged = sb.tile([P, SLOTS * LANES], BF16, name="g_staged")
         g_runs = g_staged[:].rearrange("s (a t i) -> s a t i", a=2, t=LANES)
-        den_ps = [ps.tile([P, HALF], F32, name=f"den_ps{a}", tag=f"bank{6 + a}") for a in range(2)]
         zs = [sb.tile([P, SLOTS], F32, name=f"z{t}") for t in range(LANES)]
         es = [sb.tile([P, SLOTS], F32, name=f"e{t}") for t in range(LANES)]
         hs = [sb.tile([P, SLOTS], F32, name=f"h{t}") for t in range(LANES)]
         tots = [sb.tile([P, 1], F32, name=f"tot{t}") for t in range(LANES)]
         inv_tots = [sb.tile([P, 1], F32, name=f"inv_tot{t}") for t in range(LANES)]
 
+        turned_scores = {t: ps.tile([P, SLOTS], F32, name=f"turned_scores{t}", tag=f"bank{4 + t}") for t in (2, 3)}
+        late_rows = slice(2 * P, 4 * P)
+
         def scaled_scores(t, slots, bank):
             rows = slice(t * P, (t + 1) * P)
             scores = ps.tile([P, slots.stop - slots.start], F32, name="scores", tag=bank)
             nc.tensor.matmul_mx(out=scores[:], lhsT=xd_codes[:, rows].bitcast(FP8X4), lhsT_scale=xd_scales[:, rows],
                                 rhs=c_codes[:, slots].bitcast(FP8X4), rhs_scale=c_scales[:, slots], start=True, stop=True)
-            nc.vector.scalar_tensor_tensor(zs[t][:, slots], scores[:], us_sb[:, t:t + 1], ts_all[:, slots], ALU.mult, ALU.mult)
+            nc.vector.scalar_tensor_tensor(zs[t][:, slots], scores[:], neg_us[:, t:t + 1], ts_all[:, slots], ALU.mult, ALU.mult)
+
+        def scores_by_slot(a):
+            scores = ps.tile([P, 2, 2 * P], F32, name="scores_by_slot", tag=f"bank{4 + a}")
+            scaled = sb.tile([P, 2, 2 * P], F32, name=f"scaled{a}")
+            for b in range(2):
+                slots = slice((2 * a + b) * P, (2 * a + b + 1) * P)
+                nc.tensor.matmul_mx(out=scores[:, b, :], lhsT=c_codes[:, slots].bitcast(FP8X4), lhsT_scale=c_scales[:, slots],
+                                    rhs=xd_codes[:, late_rows].bitcast(FP8X4), rhs_scale=xd_scales[:, late_rows], start=True, stop=True)
+            for b in range(2):
+                nc.scalar.activation(scaled[:, b, :], scores[:, b, :], ACT.Copy, scale=ts_cols[:, 2 * a + b:2 * a + b + 1])
+            return scaled
 
         def exponentials(t):
             neg_max = sb.tile([P, 1], F32, name=f"neg_max{t}")
-            nc.vector.tensor_reduce(neg_max[:], zs[t][:], AXIS_X, ALU.max, negate=True)
-            nc.scalar.activation(es[t][:], zs[t][:], ACT.Exp, bias=neg_max[:], scale=1.0, accum_out=tots[t][:])
+            if t < 2:
+                nc.vector.tensor_reduce(neg_max[:], zs[t][:], AXIS_X, ALU.min)
+            else:
+                nc.vector.tensor_scalar(zs[t][:], turned_scores[t][:], neg_us[:, t:t + 1], None, ALU.mult, ALU.min, accum_out=neg_max[:])
+            nc.scalar.activation(es[t][:], zs[t][:], ACT.Exp, bias=neg_max[:], scale=-1.0, accum_out=tots[t][:])
 
         def invert_total(t):
             nc.vector.reciprocal(inv_tots[t][:], tots[t][:])
@@ -173,30 +190,28 @@ def tile_attend_gkmeans_pl_kernel(tc, xT, cT, us, ts, wt, wd, offs, out_0, out_1
             e_runs = es[t][:].rearrange("s (a i) -> s a i", a=2)
             engine.tensor_scalar(g_runs[:, some, t, :], e_runs[:, some, :], inv_tots[t][:], wt_sb[:, t:t + 1], ALU.mult, ALU.mult)
 
-        def weights_on_scalar(t, pieces):
-            g_factor = sb.tile([P, 1], F32, name=f"g_factor{t}")
-            nc.scalar.activation(g_factor[:], wt_sb[:, t:t + 1], ACT.Copy, scale=inv_tots[t][:])
-            e_runs = es[t][:].rearrange("s (a i) -> s a i", a=2)
-            for some in pieces:
-                nc.scalar.activation(g_runs[:, some, t, :], e_runs[:, some, :], ACT.Copy, scale=g_factor[:])
-
         for a in range(2):
             for t in range(2):
                 scaled_scores(t, halves[a], f"bank{2 * a + t}")
+        by_slot = [scores_by_slot(a) for a in range(2)]
+        for t in (2, 3):
+            for c in range(LANES):
+                nc.tensor.transpose(turned_scores[t][:, c * P:(c + 1) * P], by_slot[c // 2][:, c % 2, (t - 2) * P:(t - 1) * P], ident[:])
+        den_ps = [ps.tile([P, HALF], F32, name=f"den_ps{a}", tag=f"bank{a}") for a in range(2)]
         exponentials(0)
         exponentials(1)
         invert_total(0)
-        den_terms_of(nc.gpsimd, 0, (0, 1))
+        den_terms_of(nc.vector, 0, (0, 1))
         add_turned(0, 0)
         add_turned(0, 1)
-        weights_on_scalar(0, [slice(0, 2)])
         invert_total(1)
-        den_terms_of(nc.gpsimd, 1, (0, 1))
-        scaled_scores(2, all_slots, "bank4")
-        scaled_scores(3, all_slots, "bank5")
         exponentials(2)
         exponentials(3)
-        weights_on_scalar(1, [slice(0, 1)])
+        g_factor = sb.tile([P, 1], F32, name="g_factor")
+        nc.scalar.activation(g_factor[:], wt_sb[:, 1:2], ACT.Copy, scale=inv_tots[1][:])
+        nc.scalar.activation(g_runs[:, 0, 1, :], es[1][:, halves[0]], ACT.Copy, scale=g_factor[:])
+        den_terms_of(nc.vector, 1, (0, 1))
+        weights_of(nc.vector, 0, (0, 1))
         invert_total(2)
         den_terms_of(nc.vector, 2, (0, 1))
         weights_of(nc.vector, 2, (0, 1))
@@ -226,7 +241,7 @@ def tile_attend_gkmeans_pl_kernel(tc, xT, cT, us, ts, wt, wd, offs, out_0, out_1
         def spread_inverse_den(a):
             inv_den = sb.tile([P, 2], F32, name=f"inv_den{a}")
             nc.vector.reciprocal(inv_den[:], dens[a][:])
-            spread_columns(inv_den_all[a][:], inv_den[:], f"bank{a}")
+            spread_columns(inv_den_all[a][:], inv_den[:], f"bank{2 + a}")
             inv_dens.append(inv_den)
 
         def numerators(j, slots, bank):
@@ -253,17 +268,17 @@ def tile_attend_gkmeans_pl_kernel(tc, xT, cT, us, ts, wt, wd, offs, out_0, out_1
 
         last = LANES - 1
         den_terms_of(nc.vector, last, (0,))
-        for t in (2, 1, 3):
+        for t in (1, 2, 3):
             add_turned(t, 0)
         weights_of(nc.vector, last, (0,))
         den_terms_of(nc.vector, last, (1,))
-        for t in (2, 1, 3):
+        for t in (1, 2, 3):
             add_turned(t, 1)
         interleave_weights(0)
         nc.vector.tensor_reduce(dens[0][:], den_ps[0][:].rearrange("i (b s) -> i b s", b=2), AXIS_X, ALU.add)
         quantise_weights(0)
         spread_inverse_den(0)
-        numerators(0, halves[0], "bank2")
+        numerators(0, halves[0], "bank4")
         quantise_features(range(2, 4), "g_by_r0")
         weights_of(nc.vector, 1, (1,))
         sum_den(1)
@@ -271,10 +286,10 @@ def tile_attend_gkmeans_pl_kernel(tc, xT, cT, us, ts, wt, wd, offs, out_0, out_1
         spread_inverse_den(1)
         interleave_weights(1)
         quantise_weights(1)
-        numerators(0, halves[1], "bank3")
-        means_by_slot(SCATTER_ORDER[1], "bank4", "bank5")
-        means_by_slot(SCATTER_ORDER[2], "bank2", "bank6")
-        numerators(last, all_slots, "bank4")
+        numerators(0, halves[1], "bank5")
+        means_by_slot(SCATTER_ORDER[1], "bank6", "bank7")
+        means_by_slot(SCATTER_ORDER[2], "bank4", "bank0")
+        numerators(last, all_slots, "bank6")
         for a, slots in enumerate(halves):
             nc.gpsimd.tensor_tensor(means[last][:, slots], nums[last][:, slots], inv_den_all[a][:], ALU.mult)
 

@@ -47,7 +47,7 @@ def tile_attend_gkmeans_pl_kernel(tc, xT, cT, us, ts, wt, wd, offs, out_0, out_1
         ts_window = sb.tile([P, T], F32, name="ts_window", tag="ts_then_window2")
         nc.scalar.dma_start(out=ts_window[P - 1:P, :], in_=ts[0:1, :])
         nc.vector.memset(ts_window[0:P - 1, :], 0.0)
-        c_planes = [sb.tile([P, T], F32, name=f"c_plane{j}") for j in range(LANES)]
+        c_planes = [sb.tile([P, T], F32, name=f"c_plane{j}", tag=f"c_plane{j}", align_bytes=64) for j in range(LANES)]
         c_rows = cT.rearrange("(p j) n -> p j n", j=LANES)
         for j in range(LANES):
             nc.sync.dma_start(out=c_planes[j][:], in_=c_rows[:, j, :])
@@ -115,12 +115,16 @@ def tile_attend_gkmeans_pl_kernel(tc, xT, cT, us, ts, wt, wd, offs, out_0, out_1
                 feats = slice((j - planes.start) * P, (j - planes.start + 1) * P)
                 xr_tiles[j] = (codes[:, feats].bitcast(FP8X4), scales[:, feats])
 
-        quantise_features(range(0, 2), "")
 
         c_by_d = sb.tile([P, SLOTS * LANES], BF16, name="c_by_d", tag="c_then_window3", align_bytes=64)
         c_lanes = c_by_d[:].rearrange("p (i j) -> p i j", j=LANES)
         for j in range(LANES - 1):
             nc.vector.tensor_copy(c_lanes[:, :, j], c_planes[j][:].indirect(offsets[:]))
+        quantise_features(range(0, 2), "c_plane2")
+        warm_up = ps.tile([P, HALF], F32, name="warm_up", tag="bank7")
+        for n in range(4):
+            nc.tensor.matmul_mx(out=warm_up[:], lhsT=xr_tiles[n % 2][0], lhsT_scale=xr_tiles[n % 2][1],
+                                rhs=xd_codes[:, 0:HALF].bitcast(FP8X4), rhs_scale=xd_scales[:, 0:HALF], start=True, stop=True)
         halves = [slice(a * HALF, (a + 1) * HALF) for a in range(2)]
 
         def listed(slots):

@@ -215,10 +215,10 @@ def tile_attend_gkmeans_pl_kernel(tc, xT, cT, us, ts, wt, wd, offs, out_0, out_1
         nc.scalar.activation(g_factor[:], wt_sb[:, 1:2], ACT.Copy, scale=inv_tots[1][:])
         nc.scalar.activation(g_runs[:, 0, 1, :], es[1][:, halves[0]], ACT.Copy, scale=g_factor[:])
         den_terms_of(nc.vector, 1, (0, 1))
-        weights_of(nc.vector, 0, (0, 1))
+        weights_of(nc.vector, 0, (0,))
         invert_total(2)
         den_terms_of(nc.vector, 2, (0, 1))
-        weights_of(nc.vector, 2, (0, 1))
+        weights_of(nc.vector, 2, (0,))
         invert_total(3)
 
         g_codes, g_scales = mx_tiles("g", SLOTS)
@@ -284,9 +284,9 @@ def tile_attend_gkmeans_pl_kernel(tc, xT, cT, us, ts, wt, wd, offs, out_0, out_1
         spread_inverse_den(0)
         numerators(0, halves[0], "bank4")
         quantise_features(range(2, 4), "g_by_r0")
-        weights_of(nc.vector, 1, (1,))
+        for t in range(LANES):
+            weights_of(nc.vector, t, (1,))
         sum_den(1)
-        weights_of(nc.vector, last, (1,))
         spread_inverse_den(1)
         interleave_weights(1)
         quantise_weights(1)

@@ -96,34 +96,38 @@ def tile_attend_gkmeans_pl_kernel(tc, xT, cT, us, ts, wt, wd, offs, out_0, out_1
         nc.vector.quantize_mx(out=xd_codes[:].bitcast(FP8X4), scales=xd_scales[:], in_=x_by_d[:])
 
         x_pairs = x_by_d[:].bitcast(F32)
-        x_by_r = sb.tile([P, D * LANES], BF16, name="x_by_r", align_bytes=64)
+        turned = [ps.tile([P, LANES * P], F32, name=f"x_turned{u}", tag=f"bank{4 + u}") for u in range(2)]
         for u in range(2):
-            turned = ps.tile([P, LANES * P], F32, name=f"x_turned{u}", tag=f"bank{4 + u}")
             for t in range(LANES):
-                nc.tensor.transpose(turned[:, t * P:(t + 1) * P], x_pairs[:, 2 * P * t + u:2 * P * (t + 1):2], ident[:])
-            nc.scalar.copy(
-                x_by_r[:, u * 2 * R:(u + 1) * 2 * R].rearrange("s (e p t) -> s e p t", e=2, t=LANES),
-                turned[:].bitcast(BF16).rearrange("s (t p e) -> s e p t", t=LANES, e=2),
-            )
+                nc.tensor.transpose(turned[u][:, t * P:(t + 1) * P], x_pairs[:, 2 * P * t + u:2 * P * (t + 1):2], ident[:])
+        x_by_r = {}
         xr_tiles = {}
 
-        def quantise_features(planes, tag):
-            codes, scales = mx_tiles(f"xr{planes.start}", len(planes) * P, tag)
-            nc.vector.quantize_mx(out=codes[:].bitcast(FP8X4), scales=scales[:],
-                                  in_=x_by_r[:, planes.start * P * LANES:planes.stop * P * LANES])
-            for j in planes:
-                feats = slice((j - planes.start) * P, (j - planes.start + 1) * P)
-                xr_tiles[j] = (codes[:, feats].bitcast(FP8X4), scales[:, feats])
+        def copy_turned(j, tile):
+            u, e = divmod(j, 2)
+            nc.scalar.copy(tile[:].rearrange("s (p t) -> s p t", t=LANES),
+                           turned[u][:].bitcast(BF16).rearrange("s (t p e) -> s e p t", t=LANES, e=2)[:, e])
+            x_by_r[j] = tile
 
+        def quantise_features(j, tag):
+            codes, scales = mx_tiles(f"xr{j}", P, tag)
+            nc.vector.quantize_mx(out=codes[:].bitcast(FP8X4), scales=scales[:], in_=x_by_r[j][:])
+            xr_tiles[j] = (codes[:].bitcast(FP8X4), scales[:])
+
+        for j in range(LANES - 1):
+            copy_turned(j, sb.tile([P, P * LANES], BF16, name=f"x_by_r{j}", align_bytes=64))
+        for j in range(2):
+            quantise_features(j, "")
 
         c_by_d = sb.tile([P, SLOTS * LANES], BF16, name="c_by_d", tag="c_then_window3", align_bytes=64)
         c_lanes = c_by_d[:].rearrange("p (i j) -> p i j", j=LANES)
         for j in range(LANES - 1):
             nc.vector.tensor_copy(c_lanes[:, :, j], c_planes[j][:].indirect(offsets[:]))
-        quantise_features(range(0, 2), "c_plane2")
-        warm_up = ps.tile([P, HALF], F32, name="warm_up", tag="bank7")
-        for n in range(4):
-            nc.tensor.matmul_mx(out=warm_up[:], lhsT=xr_tiles[n % 2][0], lhsT_scale=xr_tiles[n % 2][1],
+        copy_turned(3, sb.tile([P, P * LANES], BF16, name="x_by_r3", tag="c_plane2", align_bytes=64))
+        warm_up = ps.tile([P, HALF], F32, name="warm_up", tag="bank5")
+        for t in range(LANES):
+            rows = slice(t * P, (t + 1) * P)
+            nc.tensor.matmul_mx(out=warm_up[:], lhsT=xd_codes[:, rows].bitcast(FP8X4), lhsT_scale=xd_scales[:, rows],
                                 rhs=xd_codes[:, 0:HALF].bitcast(FP8X4), rhs_scale=xd_scales[:, 0:HALF], start=True, stop=True)
         halves = [slice(a * HALF, (a + 1) * HALF) for a in range(2)]
 
@@ -283,13 +287,14 @@ def tile_attend_gkmeans_pl_kernel(tc, xT, cT, us, ts, wt, wd, offs, out_0, out_1
         quantise_weights(0)
         spread_inverse_den(0)
         numerators(0, halves[0], "bank4")
-        quantise_features(range(2, 4), "g_by_r0")
+        quantise_features(2, "g_by_r0")
         for t in range(LANES):
             weights_of(nc.vector, t, (1,))
         sum_den(1)
         spread_inverse_den(1)
         interleave_weights(1)
         quantise_weights(1)
+        quantise_features(last, "g_by_r1")
         numerators(0, halves[1], "bank5")
         means_by_slot(SCATTER_ORDER[1], "bank6", "bank7")
         means_by_slot(SCATTER_ORDER[2], "bank4", "bank0")

@@ -143,11 +143,10 @@ def tile_attend_gkmeans_pl_kernel(tc, xT, cT, us, ts, wt, wd, offs, out_0, out_1
         nc.gpsimd.memset(windows[3][:], 0.0)
 
         all_slots = slice(0, SLOTS)
-        g_staged = sb.tile([P, SLOTS * LANES], BF16, name="g_staged")
-        g_runs = g_staged[:].rearrange("s (a t i) -> s a t i", a=2, t=LANES)
-        zs = [sb.tile([P, SLOTS], F32, name=f"z{t}") for t in range(LANES)]
+        g_first = sb.tile([P, LANES, HALF], BF16, name="g_first", tag="g_first", align_bytes=64)
+        zs = [sb.tile([P, SLOTS], F32, name=f"z{t}", tag=f"z{t}", align_bytes=64) for t in range(LANES)]
         es = [sb.tile([P, SLOTS], F32, name=f"e{t}") for t in range(LANES)]
-        hs = [sb.tile([P, SLOTS], F32, name=f"h{t}") for t in range(LANES)]
+        hs = {0: sb.tile([P, LANES, HALF], F32, name="h_first")}
         tots = [sb.tile([P, 1], F32, name=f"tot{t}") for t in range(LANES)]
         inv_tots = [sb.tile([P, 1], F32, name=f"inv_tot{t}") for t in range(LANES)]
 
@@ -173,7 +172,7 @@ def tile_attend_gkmeans_pl_kernel(tc, xT, cT, us, ts, wt, wd, offs, out_0, out_1
             return scaled
 
         def exponentials(t):
-            neg_max = sb.tile([P, 1], F32, name=f"neg_max{t}")
+            neg_max = sb.tile([P, 1], F32, name=f"neg_max{t}", tag=f"neg_max{t}")
             if t < 2:
                 nc.vector.tensor_reduce(neg_max[:], zs[t][:], AXIS_X, ALU.min)
             else:
@@ -183,20 +182,16 @@ def tile_attend_gkmeans_pl_kernel(tc, xT, cT, us, ts, wt, wd, offs, out_0, out_1
         def invert_total(t):
             nc.vector.reciprocal(inv_tots[t][:], tots[t][:])
 
-        def den_terms_of(engine, t, halves_now):
-            slots = slice(halves_now[0] * HALF, (halves_now[-1] + 1) * HALF)
-            engine.tensor_scalar(hs[t][:, slots], es[t][:, slots], inv_tots[t][:], wd_sb[:, t:t + 1], ALU.mult, ALU.mult)
+        def den_terms_of(engine, t, a):
+            engine.tensor_scalar(hs[a][:, t, :], es[t][:, halves[a]], inv_tots[t][:], wd_sb[:, t:t + 1], ALU.mult, ALU.mult)
 
         def add_turned(t, a):
             for b in range(2):
-                c = 2 * a + b
-                nc.tensor.matmul(den_ps[a][:, b * P:(b + 1) * P], hs[t][:, c * P:(c + 1) * P], ident[:], is_transpose=True,
+                nc.tensor.matmul(den_ps[a][:, b * P:(b + 1) * P], hs[a][:, t, b * P:(b + 1) * P], ident[:], is_transpose=True,
                                  start=(t == 0 and b == 0), stop=(t == LANES - 1 and b == 1))
 
         def weights_of(engine, t, halves_now):
-            some = slice(halves_now[0], halves_now[-1] + 1)
-            e_runs = es[t][:].rearrange("s (a i) -> s a i", a=2)
-            engine.tensor_scalar(g_runs[:, some, t, :], e_runs[:, some, :], inv_tots[t][:], wt_sb[:, t:t + 1], ALU.mult, ALU.mult)
+            engine.tensor_scalar(g_first[:, t, :], es[t][:, halves[0]], inv_tots[t][:], wt_sb[:, t:t + 1], ALU.mult, ALU.mult)
 
         for a in range(2):
             for t in range(2):
@@ -206,28 +201,28 @@ def tile_attend_gkmeans_pl_kernel(tc, xT, cT, us, ts, wt, wd, offs, out_0, out_1
             for c in range(LANES):
                 nc.tensor.transpose(turned_scores[t][:, c * P:(c + 1) * P], by_slot[c // 2][:, c % 2, (t - 2) * P:(t - 1) * P], ident[:])
         den_ps = [ps.tile([P, HALF], F32, name=f"den_ps{a}", tag=f"bank{a}") for a in range(2)]
+        g_factors = [sb.tile([P, 1], F32, name=f"g_factor{t}") for t in range(LANES)]
+
+        def weight_factor(t):
+            nc.scalar.activation(g_factors[t][:], wt_sb[:, t:t + 1], ACT.Copy, scale=inv_tots[t][:])
+
         exponentials(0)
         exponentials(1)
         invert_total(0)
-        den_terms_of(nc.vector, 0, (0, 1))
+        weights_of(nc.gpsimd, 0, (0,))
+        den_terms_of(nc.gpsimd, 0, 0)
         add_turned(0, 0)
-        add_turned(0, 1)
-        invert_total(1)
         exponentials(2)
         exponentials(3)
-        g_factor = sb.tile([P, 1], F32, name="g_factor")
-        nc.scalar.activation(g_factor[:], wt_sb[:, 1:2], ACT.Copy, scale=inv_tots[1][:])
-        nc.scalar.activation(g_runs[:, 0, 1, :], es[1][:, halves[0]], ACT.Copy, scale=g_factor[:])
-        den_terms_of(nc.vector, 1, (0, 1))
-        weights_of(nc.vector, 0, (0,))
-        invert_total(2)
-        den_terms_of(nc.vector, 2, (0, 1))
-        weights_of(nc.vector, 2, (0,))
+        for t in (1, 2):
+            invert_total(t)
+            den_terms_of(nc.vector, t, 0)
+            weights_of(nc.vector, t, (0,))
         invert_total(3)
 
         g_codes, g_scales = mx_tiles("g", SLOTS)
+        g_by_r = [sb.tile([P, HALF * LANES], BF16, name=f"g_by_r{a}", tag=("g_by_r0", "inv_den_then_lanes0")[a], align_bytes=64) for a in range(2)]
         inv_den_all = [sb.tile([P, HALF], F32, name=f"inv_den_all{a}", tag=f"inv_den_then_lanes{a}", align_bytes=64) for a in range(2)]
-        g_by_r = [sb.tile([P, HALF * LANES], BF16, name=f"g_by_r{a}", tag=f"g_by_r{a}", align_bytes=64) for a in range(2)]
         dens = [sb.tile([P, 2], F32, name=f"den{a}") for a in range(2)]
         den_terms = sb.tile([P, P], F32, name="den_terms")
         nums = {j: sb.tile([P, SLOTS], F32, name=f"num{j}", tag=f"num{j}", align_bytes=64) for j in (0, 3)}
@@ -236,21 +231,12 @@ def tile_attend_gkmeans_pl_kernel(tc, xT, cT, us, ts, wt, wd, offs, out_0, out_1
 
         inv_dens = []
 
-        def interleave_weights(a):
-            interleave(nc.vector.tensor_copy, g_by_r[a][:], g_runs[:, a])
-
         def quantise_weights(a):
             nc.vector.quantize_mx(out=g_codes[:, halves[a]].bitcast(FP8X4), scales=g_scales[:, halves[a]], in_=g_by_r[a][:])
 
         def sum_den(a):
             for b in range(2):
                 nc.scalar.activation(den_terms[:], den_ps[a][:, b * P:(b + 1) * P], ACT.Copy, accum_out=dens[a][:, b:b + 1])
-
-        def spread_inverse_den(a):
-            inv_den = sb.tile([P, 2], F32, name=f"inv_den{a}")
-            nc.vector.reciprocal(inv_den[:], dens[a][:])
-            spread_columns(inv_den_all[a][:], inv_den[:], f"bank{2 + a}")
-            inv_dens.append(inv_den)
 
         def numerators(j, slots, bank):
             num_ps = ps.tile([P, slots.stop - slots.start], F32, name="num_ps", tag=bank)
@@ -275,26 +261,39 @@ def tile_attend_gkmeans_pl_kernel(tc, xT, cT, us, ts, wt, wd, offs, out_0, out_1
             nc.scalar.copy(means[j][:], mean_ps[:].rearrange("p c i -> p (c i)"))
 
         last = LANES - 1
-        den_terms_of(nc.vector, last, (0,))
+        weights_of(nc.vector, last, (0,))
+        den_terms_of(nc.vector, last, 0)
         for t in (1, 2, 3):
             add_turned(t, 0)
-        weights_of(nc.vector, last, (0,))
-        den_terms_of(nc.vector, last, (1,))
-        for t in (1, 2, 3):
-            add_turned(t, 1)
-        interleave_weights(0)
-        nc.vector.tensor_reduce(dens[0][:], den_ps[0][:].rearrange("i (b s) -> i b s", b=2), AXIS_X, ALU.add)
+        interleave(nc.vector.tensor_copy, g_by_r[0][:], g_first[:])
         quantise_weights(0)
-        spread_inverse_den(0)
+        nc.vector.tensor_reduce(dens[0][:], den_ps[0][:].rearrange("i (b s) -> i b s", b=2), AXIS_X, ALU.add)
+        inv_den0 = sb.tile([P, 2], F32, name="inv_den0")
+        nc.vector.reciprocal(inv_den0[:], dens[0][:])
+        inv_dens.append(inv_den0)
         numerators(0, halves[0], "bank4")
-        quantise_features(2, "g_by_r0")
+        spread0 = ps.tile([P, HALF], F32, name="spread0", tag="bank2")
+        for c in range(2):
+            nc.tensor.transpose(spread0[:, c * P:(c + 1) * P], inv_den0[:, c:c + 1].to_broadcast([P, P]), ident[:])
+        hs[1] = sb.tile([P, LANES, HALF], F32, name="h_second", tag="neg_max3")
         for t in range(LANES):
-            weights_of(nc.vector, t, (1,))
-        sum_den(1)
-        spread_inverse_den(1)
-        interleave_weights(1)
+            den_terms_of(nc.vector, t, 1)
+            add_turned(t, 1)
+        g_second = sb.tile([P, LANES, HALF], BF16, name="g_second", tag="z3", align_bytes=64)
+        for t in range(LANES):
+            weight_factor(t)
+        for t in range(LANES):
+            nc.scalar.activation(g_second[:, t, :], es[t][:, halves[1]], ACT.Copy, scale=g_factors[t][:])
+        interleave(nc.scalar.copy, g_by_r[1][:], g_second[:])
+        quantise_features(2, "g_first")
+        quantise_features(last, "g_by_r0")
         quantise_weights(1)
-        quantise_features(last, "g_by_r1")
+        sum_den(1)
+        inv_den1 = sb.tile([P, 2], F32, name="inv_den1")
+        nc.vector.reciprocal(inv_den1[:], dens[1][:])
+        nc.vector.tensor_copy(inv_den_all[0][:], spread0[:])
+        inv_dens.append(inv_den1)
+        spread_columns(inv_den_all[1][:], inv_den1[:], "bank3")
         numerators(0, halves[1], "bank5")
         means_by_slot(SCATTER_ORDER[1], "bank6", "bank7")
         means_by_slot(SCATTER_ORDER[2], "bank4", "bank0")

@@ -105,25 +105,30 @@ def tile_attend_gkmeans_pl_kernel(tc, xT, cT, us, ts, wt, wd, offs, out_0, out_1
 
         def copy_turned(j, tile):
             u, e = divmod(j, 2)
-            nc.scalar.copy(tile[:].rearrange("s (p t) -> s p t", t=LANES),
+            nc.scalar.copy(tile.rearrange("s (p t) -> s p t", t=LANES),
                            turned[u][:].bitcast(BF16).rearrange("s (t p e) -> s e p t", t=LANES, e=2)[:, e])
             x_by_r[j] = tile
 
         def quantise_features(j, tag):
             codes, scales = mx_tiles(f"xr{j}", P, tag)
-            nc.vector.quantize_mx(out=codes[:].bitcast(FP8X4), scales=scales[:], in_=x_by_r[j][:])
+            nc.vector.quantize_mx(out=codes[:].bitcast(FP8X4), scales=scales[:], in_=x_by_r[j])
             xr_tiles[j] = (codes[:].bitcast(FP8X4), scales[:])
 
-        for j in range(LANES - 1):
-            copy_turned(j, sb.tile([P, P * LANES], BF16, name=f"x_by_r{j}", align_bytes=64))
-        for j in range(2):
+        for j in SCATTER_ORDER[:2]:
+            copy_turned(j, sb.tile([P, P * LANES], BF16, name=f"x_by_r{j}", align_bytes=64)[:])
+        for j in SCATTER_ORDER[:2]:
             quantise_features(j, "")
 
         c_by_d = sb.tile([P, SLOTS * LANES], BF16, name="c_by_d", tag="c_then_window3", align_bytes=64)
         c_lanes = c_by_d[:].rearrange("p (i j) -> p i j", j=LANES)
-        for j in range(LANES - 1):
-            nc.vector.tensor_copy(c_lanes[:, :, j], c_planes[j][:].indirect(offsets[:]))
-        copy_turned(3, sb.tile([P, P * LANES], BF16, name="x_by_r3", tag="c_plane2", align_bytes=64))
+        c_low = sb.tile([P, 2, SLOTS], F32, name="c_low", tag="c_low", align_bytes=64)
+        for j in range(2):
+            nc.vector.tensor_copy(c_low[:, j, :], c_planes[j][:].indirect(offsets[:]))
+        nc.vector.tensor_copy(c_lanes[:, :, 0:2], c_low[:].rearrange("p j i -> p i j"))
+        nc.vector.tensor_copy(c_lanes[:, :, 2], c_planes[2][:].indirect(offsets[:]))
+        x_late = sb.tile([P, 2 * P * LANES], BF16, name="x_late", tag="c_low", align_bytes=64)
+        for k, j in enumerate(SCATTER_ORDER[2:]):
+            copy_turned(j, x_late[:, k * P * LANES:(k + 1) * P * LANES])
         warm_up = ps.tile([P, HALF], F32, name="warm_up", tag="bank5")
         for t in range(LANES):
             rows = slice(t * P, (t + 1) * P)
@@ -214,11 +219,14 @@ def tile_attend_gkmeans_pl_kernel(tc, xT, cT, us, ts, wt, wd, offs, out_0, out_1
         add_turned(0, 0)
         exponentials(2)
         exponentials(3)
-        for t in (1, 2):
+        invert_total(1)
+        weights_of(nc.vector, 1, (0,))
+        den_terms_of(nc.vector, 1, 0)
+        for t in (2, 3):
             invert_total(t)
-            den_terms_of(nc.vector, t, 0)
             weights_of(nc.vector, t, (0,))
-        invert_total(3)
+        for t in (2, 3):
+            den_terms_of(nc.vector, t, 0)
 
         g_codes, g_scales = mx_tiles("g", SLOTS)
         g_by_r = [sb.tile([P, HALF * LANES], BF16, name=f"g_by_r{a}", tag=("g_by_r0", "inv_den_then_lanes0")[a], align_bytes=64) for a in range(2)]
@@ -261,8 +269,6 @@ def tile_attend_gkmeans_pl_kernel(tc, xT, cT, us, ts, wt, wd, offs, out_0, out_1
             nc.scalar.copy(means[j][:], mean_ps[:].rearrange("p c i -> p (c i)"))
 
         last = LANES - 1
-        weights_of(nc.vector, last, (0,))
-        den_terms_of(nc.vector, last, 0)
         for t in (1, 2, 3):
             add_turned(t, 0)
         interleave(nc.vector.tensor_copy, g_by_r[0][:], g_first[:])
@@ -285,8 +291,10 @@ def tile_attend_gkmeans_pl_kernel(tc, xT, cT, us, ts, wt, wd, offs, out_0, out_1
         for t in range(LANES):
             nc.scalar.activation(g_second[:, t, :], es[t][:, halves[1]], ACT.Copy, scale=g_factors[t][:])
         interleave(nc.scalar.copy, g_by_r[1][:], g_second[:])
-        quantise_features(2, "g_first")
-        quantise_features(last, "g_by_r0")
+        late_codes, late_scales = mx_tiles("xr_late", 2 * P, "g_first")
+        nc.vector.quantize_mx(out=late_codes[:].bitcast(FP8X4), scales=late_scales[:], in_=x_late[:])
+        for k, j in enumerate(SCATTER_ORDER[2:]):
+            xr_tiles[j] = (late_codes[:, k * P:(k + 1) * P].bitcast(FP8X4), late_scales[:, k * P:(k + 1) * P])
         quantise_weights(1)
         sum_den(1)
         inv_den1 = sb.tile([P, 2], F32, name="inv_den1")
@@ -339,18 +347,20 @@ def tile_attend_gkmeans_pl_kernel(tc, xT, cT, us, ts, wt, wd, offs, out_0, out_1
         for piece in pieces:
             interleave(nc.vector.tensor_copy, y_of_vector[:, piece.start * LANES:piece.stop * LANES], y_staged[:, :, piece])
 
-        def quantise_and_store(cols, y_by_d, parts, tag):
+        def quantise_and_store(tile_cols, y_by_d, parts, tag):
+            cols = slice(tile_cols.start + parts[0].start, tile_cols.start + parts[-1].stop)
             y_codes = sb.tile([P, cols.stop - cols.start], U32, name=f"y_codes{cols.start}", tag=tag, align_bytes=64)
             for part in parts:
-                k, within = divmod(cols.start + part.start, GROUP)
-                nc.vector.quantize_mx(out=y_codes[:, part].bitcast(FP8X4), scales=y_scales[4 * k:P, within:within + part.stop - part.start],
+                k, within = divmod(tile_cols.start + part.start, GROUP)
+                nc.vector.quantize_mx(out=y_codes[:, part.start - parts[0].start:part.stop - parts[0].start].bitcast(FP8X4), scales=y_scales[4 * k:P, within:within + part.stop - part.start],
                                       in_=y_by_d[:, part.start * LANES:part.stop * LANES])
             nc.sync.dma_start(out=words_out[:, cols], in_=y_codes[:].bitcast(I32))
 
         quantise_and_store(staged_cols, y_of_vector, pieces, "")
         quantise_and_store(scalar_cols, y_of_scalar, (slice(0, 128), slice(128, 384), slice(384, 640)), "num3")
         for cols, y_by_d in zip(gpsimd_cols, y_of_gpsimd):
-            quantise_and_store(cols, y_by_d, [slice(lo, lo + 256) for lo in range(0, cols.stop - cols.start, 256)], "")
+            for lo in range(0, cols.stop - cols.start, 256):
+                quantise_and_store(cols, y_by_d, [slice(lo, lo + 256)], "")
         scales_out = out_2[0].rearrange("(q r) (k c) -> q k r c", r=4, c=GROUP)
         for q in range(4):
             nc.sync.dma_start(out=scales_out[q].bitcast(I32), in_=y_scales[32 * q:32 * q + 16, :].bitcast(I32))

@@ -19,7 +19,7 @@ LANES = 4
 D, R, SLOTS, T = 512, 512, 512, 2048
 FLOPS = 2 * 2 * D * R * SLOTS
 HALF = SLOTS // 2
-SCATTER_ORDER = (0, 2, 1, 3)
+SCATTER_ORDER = (0, 1, 2, 3)
 GROUP = 512
 
 
@@ -229,58 +229,49 @@ def tile_attend_gkmeans_pl_kernel(tc, xT, cT, us, ts, wt, wd, offs, out_0, out_1
             den_terms_of(nc.vector, t, 0)
 
         g_codes, g_scales = mx_tiles("g", SLOTS)
-        g_by_r = [sb.tile([P, HALF * LANES], BF16, name=f"g_by_r{a}", tag=("g_by_r0", "inv_den_then_lanes0")[a], align_bytes=64) for a in range(2)]
-        inv_den_all = [sb.tile([P, HALF], F32, name=f"inv_den_all{a}", tag=f"inv_den_then_lanes{a}", align_bytes=64) for a in range(2)]
+        g_by_r = [sb.tile([P, HALF * LANES], BF16, name=f"g_by_r{a}", align_bytes=64) for a in range(2)]
+        inv_den_all = [sb.tile([P, HALF], F32, name=f"inv_den_all{a}") for a in range(2)]
         dens = [sb.tile([P, 2], F32, name=f"den{a}") for a in range(2)]
+        inv_dens = [sb.tile([P, 2], F32, name=f"inv_den{a}") for a in range(2)]
         den_terms = sb.tile([P, P], F32, name="den_terms")
-        nums = {j: sb.tile([P, SLOTS], F32, name=f"num{j}", tag=f"num{j}", align_bytes=64) for j in (0, 3)}
-
-        means = {j: sb.tile([P, SLOTS], F32, name=f"mean{j}") for j in range(1, LANES)}
-
-        inv_dens = []
+        means = [sb.tile([P, SLOTS], F32, name=f"mean{j}") for j in range(LANES)]
 
         def quantise_weights(a):
             nc.vector.quantize_mx(out=g_codes[:, halves[a]].bitcast(FP8X4), scales=g_scales[:, halves[a]], in_=g_by_r[a][:])
 
-        def sum_den(a):
-            for b in range(2):
-                nc.scalar.activation(den_terms[:], den_ps[a][:, b * P:(b + 1) * P], ACT.Copy, accum_out=dens[a][:, b:b + 1])
+        def numerators(parts, bank):
+            num_ps = ps.tile([P, len(parts), HALF], F32, name="num_ps", tag=bank)
+            for k, (j, a) in enumerate(parts):
+                nc.tensor.matmul_mx(out=num_ps[:, k, :], lhsT=xr_tiles[j][0], lhsT_scale=xr_tiles[j][1],
+                                    rhs=g_codes[:, halves[a]].bitcast(FP8X4), rhs_scale=g_scales[:, halves[a]], start=True, stop=True)
+            return {part: num_ps[:, k, :] for k, part in enumerate(parts)}
 
-        def numerators(j, slots, bank):
-            num_ps = ps.tile([P, slots.stop - slots.start], F32, name="num_ps", tag=bank)
-            nc.tensor.matmul_mx(out=num_ps[:], lhsT=xr_tiles[j][0], lhsT_scale=xr_tiles[j][1],
-                                rhs=g_codes[:, slots].bitcast(FP8X4), rhs_scale=g_scales[:, slots], start=True, stop=True)
-            nc.scalar.copy(nums[j][:, slots], num_ps[:])
+        def spread_inverse(a, bank):
+            spread = ps.tile([P, HALF], F32, name="spread", tag=bank)
+            for c in range(2):
+                nc.tensor.transpose(spread[:, c * P:(c + 1) * P], inv_dens[a][:, c:c + 1].to_broadcast([P, P]), ident[:])
+            return spread
 
-        def scatter_means(j, slots):
-            nc.vector.tensor_copy(windows[j][:].indirect(listed(slots)), means[j][:, slots])
+        def divide(j, a):
+            nc.vector.tensor_tensor(means[j][:, halves[a]], nums[j, a], inv_den_all[a][:], ALU.mult)
 
-        def means_by_slot(j, product_bank, turned_bank):
-            num_by_slot = ps.tile([P, LANES, P], F32, name="num_by_slot", tag=product_bank)
-            mean_by_slot = sb.tile([P, LANES, P], F32, name=f"mean_by_slot{j}", tag=f"by_slot{j}", align_bytes=64)
-            mean_ps = ps.tile([P, LANES, P], F32, name="mean_ps", tag=turned_bank)
-            for c in range(LANES):
-                slots = slice(c * P, (c + 1) * P)
-                nc.tensor.matmul_mx(out=num_by_slot[:, c, :], lhsT=g_codes[:, slots].bitcast(FP8X4), lhsT_scale=g_scales[:, slots],
-                                    rhs=xr_tiles[j][0], rhs_scale=xr_tiles[j][1], start=True, stop=True)
-            for c in range(LANES):
-                nc.scalar.activation(mean_by_slot[:, c, :], num_by_slot[:, c, :], ACT.Copy, scale=inv_dens[c // 2][:, c % 2:c % 2 + 1])
-                nc.tensor.transpose(mean_ps[:, c, :], mean_by_slot[:, c, :], ident[:])
-            nc.scalar.copy(means[j][:], mean_ps[:].rearrange("p c i -> p (c i)"))
+        def scatter_on_scalar(j, a):
+            nc.scalar.activation(windows[j][:].indirect(listed(halves[a])), means[j][:, halves[a]], ACT.Copy)
 
-        last = LANES - 1
+        def scatter_on_vector(j):
+            nc.vector.tensor_copy(windows[j][:].indirect(offsets[:]), means[j][:])
+
         for t in (1, 2, 3):
             add_turned(t, 0)
         interleave(nc.vector.tensor_copy, g_by_r[0][:], g_first[:])
         quantise_weights(0)
         nc.vector.tensor_reduce(dens[0][:], den_ps[0][:].rearrange("i (b s) -> i b s", b=2), AXIS_X, ALU.add)
-        inv_den0 = sb.tile([P, 2], F32, name="inv_den0")
-        nc.vector.reciprocal(inv_den0[:], dens[0][:])
-        inv_dens.append(inv_den0)
-        numerators(0, halves[0], "bank4")
-        spread0 = ps.tile([P, HALF], F32, name="spread0", tag="bank2")
-        for c in range(2):
-            nc.tensor.transpose(spread0[:, c * P:(c + 1) * P], inv_den0[:, c:c + 1].to_broadcast([P, P]), ident[:])
+        nc.vector.reciprocal(inv_dens[0][:], dens[0][:])
+        nums = numerators([(0, 0)], "bank4")
+        first_num = sb.tile([P, HALF], F32, name="first_num")
+        nc.scalar.copy(first_num[:], nums[0, 0])
+        spread0 = spread_inverse(0, "bank2")
+        nums.update(numerators([(1, 0)], "bank5"))
         hs[1] = sb.tile([P, LANES, HALF], F32, name="h_second", tag="neg_max3")
         for t in range(LANES):
             den_terms_of(nc.vector, t, 1)
@@ -295,72 +286,84 @@ def tile_attend_gkmeans_pl_kernel(tc, xT, cT, us, ts, wt, wd, offs, out_0, out_1
         nc.vector.quantize_mx(out=late_codes[:].bitcast(FP8X4), scales=late_scales[:], in_=x_late[:])
         for k, j in enumerate(SCATTER_ORDER[2:]):
             xr_tiles[j] = (late_codes[:, k * P:(k + 1) * P].bitcast(FP8X4), late_scales[:, k * P:(k + 1) * P])
+        for b in range(2):
+            nc.scalar.activation(den_terms[:], den_ps[1][:, b * P:(b + 1) * P], ACT.Copy, accum_out=dens[1][:, b:b + 1])
+        nc.vector.tensor_tensor(means[0][:, halves[0]], spread0[:], first_num[:], ALU.mult)
+        scatter_on_scalar(0, 0)
         quantise_weights(1)
-        sum_den(1)
-        inv_den1 = sb.tile([P, 2], F32, name="inv_den1")
-        nc.vector.reciprocal(inv_den1[:], dens[1][:])
+        nc.vector.reciprocal(inv_dens[1][:], dens[1][:])
+        spread1 = spread_inverse(1, "bank3")
+        nums.update(numerators([(0, 1), (2, 1)], "bank6"))
+        nums.update(numerators([(3, 0), (3, 1)], "bank7"))
+        nc.vector.tensor_copy(inv_den_all[1][:], spread1[:])
+        nums.update(numerators([(2, 0), (1, 1)], "bank3"))
+        divide(0, 1)
+        scatter_on_scalar(0, 1)
         nc.vector.tensor_copy(inv_den_all[0][:], spread0[:])
-        inv_dens.append(inv_den1)
-        spread_columns(inv_den_all[1][:], inv_den1[:], "bank3")
-        numerators(0, halves[1], "bank5")
-        means_by_slot(SCATTER_ORDER[1], "bank6", "bank7")
-        means_by_slot(SCATTER_ORDER[2], "bank4", "bank0")
-        numerators(last, all_slots, "bank6")
-        for a, slots in enumerate(halves):
-            nc.gpsimd.tensor_tensor(means[last][:, slots], nums[last][:, slots], inv_den_all[a][:], ALU.mult)
+        for j, a in ((1, 0), (2, 1), (2, 0), (1, 1)):
+            divide(j, a)
 
-        staged_cols, scalar_cols = slice(0, 640), slice(640, 1280)
-        gpsimd_cols = (slice(1280, 1792), slice(1792, 2048))
-        pieces = (slice(0, 512), slice(512, 640))
+        out_rows = out_0.rearrange("(p j) n -> p j n", j=LANES)
 
-        def lanes_tile(cols, tag):
-            return sb.tile([P, (cols.stop - cols.start) * LANES], BF16, name=f"y_by_d{cols.start}", tag=tag, align_bytes=64)
+        def store_window(j):
+            nc.sync.dma_start(out=out_rows[:, j, :], in_=windows[j][:])
 
-        y_staged = sb.tile([P, LANES, staged_cols.stop], BF16, name="y_staged", tag="num3", align_bytes=64)
-        y_of_vector = lanes_tile(staged_cols, "")
-        y_of_scalar = lanes_tile(scalar_cols, f"by_slot{SCATTER_ORDER[2]}")
-        y_of_gpsimd = [lanes_tile(cols, f"inv_den_then_lanes{a}") for a, cols in enumerate(gpsimd_cols)]
+        store_window(0)
+        scatter_on_vector(1)
+        store_window(1)
+        for a in (1, 0):
+            scatter_on_scalar(2, a)
+        store_window(2)
+        for a in range(2):
+            divide(3, a)
+        scatter_on_vector(3)
+        store_window(3)
+
+        vector_cols, shared_cols, scalar_cols = slice(0, 768), slice(768, 1792), slice(1792, 2048)
+        pairs = {cols.start: sb.tile([P, (cols.stop - cols.start) * LANES], BF16, name=f"pairs{cols.start}", align_bytes=64)
+                 for cols in (vector_cols, shared_cols, scalar_cols)}
 
         def round_on_gpsimd(rounded, source):
             nc.gpsimd.tensor_scalar(rounded, source, 1.0, 1.0, ALU.mult, ALU.mult)
 
-        def lane(y_by_d, j):
-            return y_by_d[:].rearrange("p (n j) -> p n j", j=LANES)[:, :, j]
+        def round_lane(copy, j, tile_cols, cols):
+            u, e = divmod(j, 2)
+            lanes = pairs[tile_cols.start][:].rearrange("p (u n e) -> p u n e", u=2, e=2)
+            copy(lanes[:, u, cols.start - tile_cols.start:cols.stop - tile_cols.start, e], windows[j][:, cols])
 
-        out_rows = out_0.rearrange("(p j) n -> p j n", j=LANES)
-        for j in SCATTER_ORDER:
-            if j == 0:
-                for a, slots in enumerate(halves):
-                    nc.vector.tensor_tensor(windows[0][:].indirect(listed(slots)), nums[0][:, slots], inv_den_all[a][:], ALU.mult)
-            else:
-                scatter_means(j, all_slots)
-            nc.sync.dma_start(out=out_rows[:, j, :], in_=windows[j][:])
-            nc.scalar.copy(lane(y_of_scalar, j), windows[j][:, scalar_cols])
-            round_staged = round_on_gpsimd if j < last else nc.vector.tensor_copy
-            round_staged(y_staged[:, j, :], windows[j][:, staged_cols])
-            round_lane = round_on_gpsimd if j < 2 else nc.scalar.copy
-            for cols, y_by_d in zip(gpsimd_cols, y_of_gpsimd):
-                round_lane(lane(y_by_d, j), windows[j][:, cols])
+        def weave(copy, tile_cols, cols):
+            words = pairs[tile_cols.start][:].bitcast(F32).rearrange("p (u n) -> p n u", u=2)
+            y_by_d = sb.tile([P, (cols.stop - cols.start) * LANES], BF16, name=f"y_by_d{cols.start}", align_bytes=64)
+            copy(y_by_d[:].bitcast(F32).rearrange("p (n u) -> p n u", u=2), words[:, cols.start - tile_cols.start:cols.stop - tile_cols.start, :])
+            return y_by_d
 
         y_scales = sb.tile([P, GROUP], U8, name="y_scales", align_bytes=64)
         words_out = out_1[0].rearrange("p n l -> p (n l)").bitcast(I32)
-        for piece in pieces:
-            interleave(nc.vector.tensor_copy, y_of_vector[:, piece.start * LANES:piece.stop * LANES], y_staged[:, :, piece])
 
-        def quantise_and_store(tile_cols, y_by_d, parts, tag):
-            cols = slice(tile_cols.start + parts[0].start, tile_cols.start + parts[-1].stop)
-            y_codes = sb.tile([P, cols.stop - cols.start], U32, name=f"y_codes{cols.start}", tag=tag, align_bytes=64)
-            for part in parts:
-                k, within = divmod(tile_cols.start + part.start, GROUP)
-                nc.vector.quantize_mx(out=y_codes[:, part.start - parts[0].start:part.stop - parts[0].start].bitcast(FP8X4), scales=y_scales[4 * k:P, within:within + part.stop - part.start],
-                                      in_=y_by_d[:, part.start * LANES:part.stop * LANES])
+        def quantise_and_store(cols, y_by_d):
+            y_codes = sb.tile([P, cols.stop - cols.start], U32, name=f"y_codes{cols.start}", align_bytes=64)
+            k, within = divmod(cols.start, GROUP)
+            nc.vector.quantize_mx(out=y_codes[:].bitcast(FP8X4), scales=y_scales[4 * k:P, within:within + cols.stop - cols.start], in_=y_by_d[:])
             nc.sync.dma_start(out=words_out[:, cols], in_=y_codes[:].bitcast(I32))
 
-        quantise_and_store(staged_cols, y_of_vector, pieces, "")
-        quantise_and_store(scalar_cols, y_of_scalar, (slice(0, 128), slice(128, 384), slice(384, 640)), "num3")
-        for cols, y_by_d in zip(gpsimd_cols, y_of_gpsimd):
-            for lo in range(0, cols.stop - cols.start, 256):
-                quantise_and_store(cols, y_by_d, [slice(lo, lo + 256)], "")
+        for j in range(2):
+            for cols in (vector_cols, shared_cols):
+                round_lane(round_on_gpsimd, j, cols, cols)
+        round_lane(nc.scalar.copy, 2, shared_cols, shared_cols)
+        for j in range(3):
+            round_lane(nc.scalar.copy, j, scalar_cols, scalar_cols)
+        for j in (2, 3):
+            round_lane(nc.vector.tensor_copy, j, vector_cols, vector_cols)
+        vector_pieces = (slice(0, 512), slice(512, 768))
+        woven = [weave(nc.vector.tensor_copy, vector_cols, cols) for cols in vector_pieces]
+        for cols, y_by_d in zip(vector_pieces, woven):
+            quantise_and_store(cols, y_by_d)
+        scalar_pieces = ((scalar_cols, scalar_cols), (shared_cols, slice(1024, 1536)), (shared_cols, slice(768, 1024)), (shared_cols, slice(1536, 1792)))
+        round_lane(nc.scalar.copy, 3, *scalar_pieces[0])
+        for k, (tile_cols, cols) in enumerate(scalar_pieces):
+            for ahead in scalar_pieces[k + 1:k + 2]:
+                round_lane(nc.scalar.copy, 3, *ahead)
+            quantise_and_store(cols, weave(nc.scalar.copy, tile_cols, cols))
         scales_out = out_2[0].rearrange("(q r) (k c) -> q k r c", r=4, c=GROUP)
         for q in range(4):
             nc.sync.dma_start(out=scales_out[q].bitcast(I32), in_=y_scales[32 * q:32 * q + 16, :].bitcast(I32))

@@ -230,11 +230,11 @@ def tile_attend_gkmeans_pl_kernel(tc, xT, cT, us, ts, wt, wd, offs, out_0, out_1
 
         g_codes, g_scales = mx_tiles("g", SLOTS)
         g_by_r = [sb.tile([P, HALF * LANES], BF16, name=f"g_by_r{a}", align_bytes=64) for a in range(2)]
-        inv_den_all = [sb.tile([P, HALF], F32, name=f"inv_den_all{a}") for a in range(2)]
+        inv_den_all = sb.tile([P, SLOTS], F32, name="inv_den_all")
         dens = [sb.tile([P, 2], F32, name=f"den{a}") for a in range(2)]
         inv_dens = [sb.tile([P, 2], F32, name=f"inv_den{a}") for a in range(2)]
         den_terms = sb.tile([P, P], F32, name="den_terms")
-        means = [sb.tile([P, SLOTS], F32, name=f"mean{j}") for j in range(LANES)]
+        means = [sb.tile([P, SLOTS], F32, name=f"mean{j}", tag=f"mean{j}", align_bytes=64) for j in range(LANES)]
 
         def quantise_weights(a):
             nc.vector.quantize_mx(out=g_codes[:, halves[a]].bitcast(FP8X4), scales=g_scales[:, halves[a]], in_=g_by_r[a][:])
@@ -244,7 +244,7 @@ def tile_attend_gkmeans_pl_kernel(tc, xT, cT, us, ts, wt, wd, offs, out_0, out_1
             for k, (j, a) in enumerate(parts):
                 nc.tensor.matmul_mx(out=num_ps[:, k, :], lhsT=xr_tiles[j][0], lhsT_scale=xr_tiles[j][1],
                                     rhs=g_codes[:, halves[a]].bitcast(FP8X4), rhs_scale=g_scales[:, halves[a]], start=True, stop=True)
-            return {part: num_ps[:, k, :] for k, part in enumerate(parts)}
+            return num_ps[:].rearrange("p k i -> p (k i)")
 
         def spread_inverse(a, bank):
             spread = ps.tile([P, HALF], F32, name="spread", tag=bank)
@@ -252,8 +252,8 @@ def tile_attend_gkmeans_pl_kernel(tc, xT, cT, us, ts, wt, wd, offs, out_0, out_1
                 nc.tensor.transpose(spread[:, c * P:(c + 1) * P], inv_dens[a][:, c:c + 1].to_broadcast([P, P]), ident[:])
             return spread
 
-        def divide(j, a):
-            nc.vector.tensor_tensor(means[j][:, halves[a]], nums[j, a], inv_den_all[a][:], ALU.mult)
+        def divide(j, slots, num):
+            nc.vector.tensor_tensor(means[j][:, slots], num, inv_den_all[:, slots], ALU.mult)
 
         def scatter_on_scalar(j, a):
             nc.scalar.activation(windows[j][:].indirect(listed(halves[a])), means[j][:, halves[a]], ACT.Copy)
@@ -267,11 +267,11 @@ def tile_attend_gkmeans_pl_kernel(tc, xT, cT, us, ts, wt, wd, offs, out_0, out_1
         quantise_weights(0)
         nc.vector.tensor_reduce(dens[0][:], den_ps[0][:].rearrange("i (b s) -> i b s", b=2), AXIS_X, ALU.add)
         nc.vector.reciprocal(inv_dens[0][:], dens[0][:])
-        nums = numerators([(0, 0)], "bank4")
+        num0_first = numerators([(0, 0)], "bank4")
         first_num = sb.tile([P, HALF], F32, name="first_num")
-        nc.scalar.copy(first_num[:], nums[0, 0])
+        nc.scalar.copy(first_num[:], num0_first)
         spread0 = spread_inverse(0, "bank2")
-        nums.update(numerators([(1, 0)], "bank5"))
+        num1_first = numerators([(1, 0)], "bank5")
         hs[1] = sb.tile([P, LANES, HALF], F32, name="h_second", tag="neg_max3")
         for t in range(LANES):
             den_terms_of(nc.vector, t, 1)
@@ -293,15 +293,16 @@ def tile_attend_gkmeans_pl_kernel(tc, xT, cT, us, ts, wt, wd, offs, out_0, out_1
         quantise_weights(1)
         nc.vector.reciprocal(inv_dens[1][:], dens[1][:])
         spread1 = spread_inverse(1, "bank3")
-        nums.update(numerators([(0, 1), (2, 1)], "bank6"))
-        nums.update(numerators([(3, 0), (3, 1)], "bank7"))
-        nc.vector.tensor_copy(inv_den_all[1][:], spread1[:])
-        nums.update(numerators([(2, 0), (1, 1)], "bank3"))
-        divide(0, 1)
+        nums_second = numerators([(0, 1), (1, 1)], "bank6")
+        num2 = numerators([(2, 0), (2, 1)], "bank7")
+        num3 = numerators([(3, 0), (3, 1)], "bank0")
+        nc.vector.tensor_copy(inv_den_all[:, halves[1]], spread1[:])
+        divide(0, halves[1], nums_second[:, halves[0]])
         scatter_on_scalar(0, 1)
-        nc.vector.tensor_copy(inv_den_all[0][:], spread0[:])
-        for j, a in ((1, 0), (2, 1), (2, 0), (1, 1)):
-            divide(j, a)
+        nc.vector.tensor_copy(inv_den_all[:, halves[0]], spread0[:])
+        divide(1, halves[0], num1_first)
+        divide(1, halves[1], nums_second[:, halves[1]])
+        divide(2, all_slots, num2)
 
         out_rows = out_0.rearrange("(p j) n -> p j n", j=LANES)
 
@@ -311,17 +312,16 @@ def tile_attend_gkmeans_pl_kernel(tc, xT, cT, us, ts, wt, wd, offs, out_0, out_1
         store_window(0)
         scatter_on_vector(1)
         store_window(1)
-        for a in (1, 0):
+        for a in range(2):
             scatter_on_scalar(2, a)
         store_window(2)
-        for a in range(2):
-            divide(3, a)
+        divide(3, all_slots, num3)
         scatter_on_vector(3)
         store_window(3)
 
-        vector_cols, shared_cols, scalar_cols = slice(0, 768), slice(768, 1792), slice(1792, 2048)
-        pairs = {cols.start: sb.tile([P, (cols.stop - cols.start) * LANES], BF16, name=f"pairs{cols.start}", align_bytes=64)
-                 for cols in (vector_cols, shared_cols, scalar_cols)}
+        vector_cols, shared_cols, scalar_cols = slice(0, 1024), slice(1024, 1536), slice(1536, 2048)
+        pairs = {cols.start: sb.tile([P, (cols.stop - cols.start) * LANES], BF16, name=f"pairs{cols.start}", tag=tag, align_bytes=64)
+                 for cols, tag in ((vector_cols, ""), (shared_cols, ""), (scalar_cols, "mean2"))}
 
         def round_on_gpsimd(rounded, source):
             nc.gpsimd.tensor_scalar(rounded, source, 1.0, 1.0, ALU.mult, ALU.mult)
@@ -354,11 +354,11 @@ def tile_attend_gkmeans_pl_kernel(tc, xT, cT, us, ts, wt, wd, offs, out_0, out_1
             round_lane(nc.scalar.copy, j, scalar_cols, scalar_cols)
         for j in (2, 3):
             round_lane(nc.vector.tensor_copy, j, vector_cols, vector_cols)
-        vector_pieces = (slice(0, 512), slice(512, 768))
+        vector_pieces = (slice(0, 512), slice(512, 1024))
         woven = [weave(nc.vector.tensor_copy, vector_cols, cols) for cols in vector_pieces]
         for cols, y_by_d in zip(vector_pieces, woven):
             quantise_and_store(cols, y_by_d)
-        scalar_pieces = ((scalar_cols, scalar_cols), (shared_cols, slice(1024, 1536)), (shared_cols, slice(768, 1024)), (shared_cols, slice(1536, 1792)))
+        scalar_pieces = ((shared_cols, shared_cols), (scalar_cols, slice(1536, 1792)), (scalar_cols, slice(1792, 2048)))
         round_lane(nc.scalar.copy, 3, *scalar_pieces[0])
         for k, (tile_cols, cols) in enumerate(scalar_pieces):
             for ahead in scalar_pieces[k + 1:k + 2]:

@@ -319,22 +319,19 @@ def tile_attend_gkmeans_pl_kernel(tc, xT, cT, us, ts, wt, wd, offs, out_0, out_1
         scatter_on_vector(3)
         store_window(3)
 
-        vector_cols, shared_cols, scalar_cols = slice(0, 1024), slice(1024, 1536), slice(1536, 2048)
-        pairs = {cols.start: sb.tile([P, (cols.stop - cols.start) * LANES], BF16, name=f"pairs{cols.start}", tag=tag, align_bytes=64)
-                 for cols, tag in ((vector_cols, ""), (shared_cols, ""), (scalar_cols, "mean2"))}
+        vector_cols, scalar_cols = slice(0, 1024), slice(1024, 2048)
+        staged = {cols.start: sb.tile([P, LANES, cols.stop - cols.start], BF16, name=f"staged{cols.start}", align_bytes=64)
+                  for cols in (vector_cols, scalar_cols)}
 
         def round_on_gpsimd(rounded, source):
             nc.gpsimd.tensor_scalar(rounded, source, 1.0, 1.0, ALU.mult, ALU.mult)
 
-        def round_lane(copy, j, tile_cols, cols):
-            u, e = divmod(j, 2)
-            lanes = pairs[tile_cols.start][:].rearrange("p (u n e) -> p u n e", u=2, e=2)
-            copy(lanes[:, u, cols.start - tile_cols.start:cols.stop - tile_cols.start, e], windows[j][:, cols])
+        def round_plane(copy, j, tile_cols, cols):
+            copy(staged[tile_cols.start][:, j, cols.start - tile_cols.start:cols.stop - tile_cols.start], windows[j][:, cols])
 
         def weave(copy, tile_cols, cols):
-            words = pairs[tile_cols.start][:].bitcast(F32).rearrange("p (u n) -> p n u", u=2)
             y_by_d = sb.tile([P, (cols.stop - cols.start) * LANES], BF16, name=f"y_by_d{cols.start}", align_bytes=64)
-            copy(y_by_d[:].bitcast(F32).rearrange("p (n u) -> p n u", u=2), words[:, cols.start - tile_cols.start:cols.stop - tile_cols.start, :])
+            interleave(copy, y_by_d[:], staged[tile_cols.start][:, :, cols.start - tile_cols.start:cols.stop - tile_cols.start])
             return y_by_d
 
         y_scales = sb.tile([P, GROUP], U8, name="y_scales", align_bytes=64)
@@ -347,23 +344,19 @@ def tile_attend_gkmeans_pl_kernel(tc, xT, cT, us, ts, wt, wd, offs, out_0, out_1
             nc.sync.dma_start(out=words_out[:, cols], in_=y_codes[:].bitcast(I32))
 
         for j in range(2):
-            for cols in (vector_cols, shared_cols):
-                round_lane(round_on_gpsimd, j, cols, cols)
-        round_lane(nc.scalar.copy, 2, shared_cols, shared_cols)
-        for j in range(3):
-            round_lane(nc.scalar.copy, j, scalar_cols, scalar_cols)
-        for j in (2, 3):
-            round_lane(nc.vector.tensor_copy, j, vector_cols, vector_cols)
+            for cols in (vector_cols, scalar_cols):
+                round_plane(round_on_gpsimd, j, cols, cols)
+        for cols in (vector_cols, scalar_cols):
+            round_plane(nc.scalar.copy, 2, cols, cols)
+        round_plane(nc.vector.tensor_copy, 3, vector_cols, vector_cols)
+        round_plane(nc.vector.tensor_copy, 3, scalar_cols, slice(1536, 2048))
         vector_pieces = (slice(0, 512), slice(512, 1024))
         woven = [weave(nc.vector.tensor_copy, vector_cols, cols) for cols in vector_pieces]
         for cols, y_by_d in zip(vector_pieces, woven):
             quantise_and_store(cols, y_by_d)
-        scalar_pieces = ((shared_cols, shared_cols), (scalar_cols, slice(1536, 1792)), (scalar_cols, slice(1792, 2048)))
-        round_lane(nc.scalar.copy, 3, *scalar_pieces[0])
-        for k, (tile_cols, cols) in enumerate(scalar_pieces):
-            for ahead in scalar_pieces[k + 1:k + 2]:
-                round_lane(nc.scalar.copy, 3, *ahead)
-            quantise_and_store(cols, weave(nc.scalar.copy, tile_cols, cols))
+        round_plane(nc.scalar.copy, 3, scalar_cols, slice(1024, 1536))
+        for cols in (slice(1024, 1536), slice(1536, 1792), slice(1792, 2048)):
+            quantise_and_store(cols, weave(nc.scalar.copy, scalar_cols, cols))
         scales_out = out_2[0].rearrange("(q r) (k c) -> q k r c", r=4, c=GROUP)
         for q in range(4):
             nc.sync.dma_start(out=scales_out[q].bitcast(I32), in_=y_scales[32 * q:32 * q + 16, :].bitcast(I32))

@@ -52,12 +52,11 @@ def tile_attend_gkmeans_pl_kernel(tc, xT, cT, us, ts, wt, wd, offs, out_0, out_1
         for j in range(LANES):
             nc.sync.dma_start(out=c_planes[j][:], in_=c_rows[:, j, :])
 
-        row_factors = []
-        for name, vec in (("us_sb", us), ("wt_sb", wt), ("wd_sb", wd)):
-            tile = sb.tile([P, LANES], F32, name=name)
-            nc.sync.dma_start(out=tile[:], in_=vec.rearrange("(s t) o -> s (t o)", t=LANES))
-            row_factors.append(tile)
-        us_sb, wt_sb, wd_sb = row_factors
+        us_sb = sb.tile([P, LANES], F32, name="us_sb")
+        row_weights = sb.tile([P, 2, 2 * LANES], F32, name="row_weights")
+        wt_sb, wd_sb = row_weights[:, 0, 0:LANES], row_weights[:, 1, 0:LANES]
+        for tile, vec in ((us_sb[:], us), (wt_sb, wt), (wd_sb, wd)):
+            nc.sync.dma_start(out=tile, in_=vec.rearrange("(s t) o -> s (t o)", t=LANES))
 
         ident = sb.tile([P, P], F32, name="ident")
         make_identity(nc, ident[:])
@@ -206,10 +205,11 @@ def tile_attend_gkmeans_pl_kernel(tc, xT, cT, us, ts, wt, wd, offs, out_0, out_1
             for c in range(LANES):
                 nc.tensor.transpose(turned_scores[t][:, c * P:(c + 1) * P], by_slot[c // 2][:, c % 2, (t - 2) * P:(t - 1) * P], ident[:])
         den_ps = [ps.tile([P, HALF], F32, name=f"den_ps{a}", tag=f"bank{a}") for a in range(2)]
-        g_factors = [sb.tile([P, 1], F32, name=f"g_factor{t}") for t in range(LANES)]
+        factors = [sb.tile([P, 2 if t >= 2 else 1], F32, name=f"factors{t}") for t in range(LANES)]
 
-        def weight_factor(t):
-            nc.scalar.activation(g_factors[t][:], wt_sb[:, t:t + 1], ACT.Copy, scale=inv_tots[t][:])
+        def weight_factors(t):
+            weights = row_weights[:, :, t] if t >= 2 else wd_sb[:, t:t + 1]
+            nc.scalar.activation(factors[t][:], weights, ACT.Copy, scale=inv_tots[t][:])
 
         exponentials(0)
         exponentials(1)
@@ -233,18 +233,14 @@ def tile_attend_gkmeans_pl_kernel(tc, xT, cT, us, ts, wt, wd, offs, out_0, out_1
         inv_den_all = sb.tile([P, SLOTS], F32, name="inv_den_all")
         dens = [sb.tile([P, 2], F32, name=f"den{a}") for a in range(2)]
         inv_dens = [sb.tile([P, 2], F32, name=f"inv_den{a}") for a in range(2)]
-        den_terms = sb.tile([P, P], F32, name="den_terms")
         means = [sb.tile([P, SLOTS], F32, name=f"mean{j}", tag=f"mean{j}", align_bytes=64) for j in range(LANES)]
 
         def quantise_weights(a):
             nc.vector.quantize_mx(out=g_codes[:, halves[a]].bitcast(FP8X4), scales=g_scales[:, halves[a]], in_=g_by_r[a][:])
 
-        def numerators(parts, bank):
-            num_ps = ps.tile([P, len(parts), HALF], F32, name="num_ps", tag=bank)
-            for k, (j, a) in enumerate(parts):
-                nc.tensor.matmul_mx(out=num_ps[:, k, :], lhsT=xr_tiles[j][0], lhsT_scale=xr_tiles[j][1],
-                                    rhs=g_codes[:, halves[a]].bitcast(FP8X4), rhs_scale=g_scales[:, halves[a]], start=True, stop=True)
-            return num_ps[:].rearrange("p k i -> p (k i)")
+        def numerators(j, slots, num_ps):
+            nc.tensor.matmul_mx(out=num_ps, lhsT=xr_tiles[j][0], lhsT_scale=xr_tiles[j][1],
+                                rhs=g_codes[:, slots].bitcast(FP8X4), rhs_scale=g_scales[:, slots], start=True, stop=True)
 
         def spread_inverse(a, bank):
             spread = ps.tile([P, HALF], F32, name="spread", tag=bank)
@@ -263,46 +259,46 @@ def tile_attend_gkmeans_pl_kernel(tc, xT, cT, us, ts, wt, wd, offs, out_0, out_1
 
         for t in (1, 2, 3):
             add_turned(t, 0)
-        interleave(nc.vector.tensor_copy, g_by_r[0][:], g_first[:])
-        quantise_weights(0)
-        nc.vector.tensor_reduce(dens[0][:], den_ps[0][:].rearrange("i (b s) -> i b s", b=2), AXIS_X, ALU.add)
-        nc.vector.reciprocal(inv_dens[0][:], dens[0][:])
-        num0_first = numerators([(0, 0)], "bank4")
-        first_num = sb.tile([P, HALF], F32, name="first_num")
-        nc.scalar.copy(first_num[:], num0_first)
-        spread0 = spread_inverse(0, "bank2")
-        num1_first = numerators([(1, 0)], "bank5")
         hs[1] = sb.tile([P, LANES, HALF], F32, name="h_second", tag="neg_max3")
         for t in range(LANES):
-            den_terms_of(nc.vector, t, 1)
+            weight_factors(t)
+        for t in range(LANES):
+            nc.scalar.activation(hs[1][:, t, :], es[t][:, halves[1]], ACT.Copy, scale=factors[t][:, factors[t].shape[1] - 1:])
             add_turned(t, 1)
+        interleave(nc.vector.tensor_copy, g_by_r[0][:], g_first[:])
+        quantise_weights(0)
+        for a in range(2):
+            nc.vector.tensor_reduce(dens[a][:], den_ps[a][:].rearrange("i (b s) -> i b s", b=2), AXIS_X, ALU.add)
+        for a in range(2):
+            nc.vector.reciprocal(inv_dens[a][:], dens[a][:])
+        num0 = [ps.tile([P, HALF], F32, name=f"num0_{a}", tag=bank) for a, bank in enumerate(("bank4", "bank6"))]
+        nums = {j: ps.tile([P, SLOTS], F32, name=f"num{j}", tag=bank) for j, bank in ((1, "bank5"), (2, "bank7"), (3, "bank1"))}
+        numerators(0, halves[0], num0[0][:])
+        numerators(1, halves[0], nums[1][:, halves[0]])
+        spreads = [spread_inverse(a, f"bank{2 + a}") for a in range(2)]
         g_second = sb.tile([P, LANES, HALF], BF16, name="g_second", tag="z3", align_bytes=64)
-        for t in range(LANES):
-            weight_factor(t)
-        for t in range(LANES):
-            nc.scalar.activation(g_second[:, t, :], es[t][:, halves[1]], ACT.Copy, scale=g_factors[t][:])
+        for t in range(2):
+            nc.vector.tensor_scalar(g_second[:, t, :], es[t][:, halves[1]], inv_tots[t][:], wt_sb[:, t:t + 1], ALU.mult, ALU.mult)
+        for t in (2, 3):
+            nc.scalar.activation(g_second[:, t, :], es[t][:, halves[1]], ACT.Copy, scale=factors[t][:, 0:1])
         interleave(nc.scalar.copy, g_by_r[1][:], g_second[:])
+        for a in range(2):
+            nc.scalar.copy(inv_den_all[:, halves[a]], spreads[a][:])
         late_codes, late_scales = mx_tiles("xr_late", 2 * P, "g_first")
         nc.vector.quantize_mx(out=late_codes[:].bitcast(FP8X4), scales=late_scales[:], in_=x_late[:])
         for k, j in enumerate(SCATTER_ORDER[2:]):
             xr_tiles[j] = (late_codes[:, k * P:(k + 1) * P].bitcast(FP8X4), late_scales[:, k * P:(k + 1) * P])
-        for b in range(2):
-            nc.scalar.activation(den_terms[:], den_ps[1][:, b * P:(b + 1) * P], ACT.Copy, accum_out=dens[1][:, b:b + 1])
-        nc.vector.tensor_tensor(means[0][:, halves[0]], spread0[:], first_num[:], ALU.mult)
+        divide(0, halves[0], num0[0][:])
         scatter_on_scalar(0, 0)
         quantise_weights(1)
-        nc.vector.reciprocal(inv_dens[1][:], dens[1][:])
-        spread1 = spread_inverse(1, "bank3")
-        nums_second = numerators([(0, 1), (1, 1)], "bank6")
-        num2 = numerators([(2, 0), (2, 1)], "bank7")
-        num3 = numerators([(3, 0), (3, 1)], "bank0")
-        nc.vector.tensor_copy(inv_den_all[:, halves[1]], spread1[:])
-        divide(0, halves[1], nums_second[:, halves[0]])
+        numerators(0, halves[1], num0[1][:])
+        numerators(1, halves[1], nums[1][:, halves[1]])
+        for j in (2, 3):
+            numerators(j, all_slots, nums[j][:])
+        divide(0, halves[1], num0[1][:])
         scatter_on_scalar(0, 1)
-        nc.vector.tensor_copy(inv_den_all[:, halves[0]], spread0[:])
-        divide(1, halves[0], num1_first)
-        divide(1, halves[1], nums_second[:, halves[1]])
-        divide(2, all_slots, num2)
+        for j in (1, 2):
+            divide(j, all_slots, nums[j][:])
 
         out_rows = out_0.rearrange("(p j) n -> p j n", j=LANES)
 
@@ -315,11 +311,11 @@ def tile_attend_gkmeans_pl_kernel(tc, xT, cT, us, ts, wt, wd, offs, out_0, out_1
         for a in range(2):
             scatter_on_scalar(2, a)
         store_window(2)
-        divide(3, all_slots, num3)
+        divide(3, all_slots, nums[3][:])
         scatter_on_vector(3)
         store_window(3)
 
-        vector_cols, scalar_cols = slice(0, 1024), slice(1024, 2048)
+        vector_cols, scalar_cols = slice(0, 1152), slice(1152, 2048)
         staged = {cols.start: sb.tile([P, LANES, cols.stop - cols.start], BF16, name=f"staged{cols.start}", align_bytes=64)
                   for cols in (vector_cols, scalar_cols)}
 
@@ -337,26 +333,31 @@ def tile_attend_gkmeans_pl_kernel(tc, xT, cT, us, ts, wt, wd, offs, out_0, out_1
         y_scales = sb.tile([P, GROUP], U8, name="y_scales", align_bytes=64)
         words_out = out_1[0].rearrange("p n l -> p (n l)").bitcast(I32)
 
-        def quantise_and_store(cols, y_by_d):
+        def quantise_and_store(pieces, woven):
+            cols = slice(pieces[0].start, pieces[-1].stop)
             y_codes = sb.tile([P, cols.stop - cols.start], U32, name=f"y_codes{cols.start}", align_bytes=64)
-            k, within = divmod(cols.start, GROUP)
-            nc.vector.quantize_mx(out=y_codes[:].bitcast(FP8X4), scales=y_scales[4 * k:P, within:within + cols.stop - cols.start], in_=y_by_d[:])
+            for piece, y_by_d in zip(pieces, woven):
+                k, within = divmod(piece.start, GROUP)
+                nc.vector.quantize_mx(out=y_codes[:, piece.start - cols.start:piece.stop - cols.start].bitcast(FP8X4),
+                                      scales=y_scales[4 * k:P, within:within + piece.stop - piece.start], in_=y_by_d[:])
             nc.sync.dma_start(out=words_out[:, cols], in_=y_codes[:].bitcast(I32))
 
-        for j in range(2):
-            for cols in (vector_cols, scalar_cols):
-                round_plane(round_on_gpsimd, j, cols, cols)
+        for cols in (vector_cols, scalar_cols):
+            round_plane(round_on_gpsimd, 0, cols, cols)
+        round_plane(round_on_gpsimd, 1, vector_cols, vector_cols)
+        round_plane(round_on_gpsimd, 1, scalar_cols, slice(1536, 2048))
         for cols in (vector_cols, scalar_cols):
             round_plane(nc.scalar.copy, 2, cols, cols)
+        round_plane(nc.scalar.copy, 1, scalar_cols, slice(1152, 1536))
+        vector_pieces = (slice(0, 512), slice(512, 1024), slice(1024, 1152))
         round_plane(nc.vector.tensor_copy, 3, vector_cols, vector_cols)
-        round_plane(nc.vector.tensor_copy, 3, scalar_cols, slice(1536, 2048))
-        vector_pieces = (slice(0, 512), slice(512, 1024))
+        round_plane(nc.vector.tensor_copy, 3, scalar_cols, slice(1152, 1536))
+        round_plane(nc.scalar.copy, 3, scalar_cols, slice(1536, 2048))
         woven = [weave(nc.vector.tensor_copy, vector_cols, cols) for cols in vector_pieces]
-        for cols, y_by_d in zip(vector_pieces, woven):
-            quantise_and_store(cols, y_by_d)
-        round_plane(nc.scalar.copy, 3, scalar_cols, slice(1024, 1536))
-        for cols in (slice(1024, 1536), slice(1536, 1792), slice(1792, 2048)):
-            quantise_and_store(cols, weave(nc.scalar.copy, scalar_cols, cols))
+        quantise_and_store(vector_pieces[:1], woven[:1])
+        quantise_and_store(vector_pieces[1:], woven[1:])
+        for cols in (slice(1536, 2048), slice(1280, 1536), slice(1152, 1280)):
+            quantise_and_store([cols], [weave(nc.scalar.copy, scalar_cols, cols)])
         scales_out = out_2[0].rearrange("(q r) (k c) -> q k r c", r=4, c=GROUP)
         for q in range(4):
             nc.sync.dma_start(out=scales_out[q].bitcast(I32), in_=y_scales[32 * q:32 * q + 16, :].bitcast(I32))

@@ -128,11 +128,6 @@ def tile_attend_gkmeans_pl_kernel(tc, xT, cT, us, ts, wt, wd, offs, out_0, out_1
         x_late = sb.tile([P, 2 * P * LANES], BF16, name="x_late", tag="c_low", align_bytes=64)
         for k, j in enumerate(SCATTER_ORDER[2:]):
             copy_turned(j, x_late[:, k * P * LANES:(k + 1) * P * LANES])
-        warm_up = ps.tile([P, HALF], F32, name="warm_up", tag="bank5")
-        for t in range(LANES):
-            rows = slice(t * P, (t + 1) * P)
-            nc.tensor.matmul_mx(out=warm_up[:], lhsT=xd_codes[:, rows].bitcast(FP8X4), lhsT_scale=xd_scales[:, rows],
-                                rhs=xd_codes[:, 0:HALF].bitcast(FP8X4), rhs_scale=xd_scales[:, 0:HALF], start=True, stop=True)
         halves = [slice(a * HALF, (a + 1) * HALF) for a in range(2)]
 
         def listed(slots):

@@ -113,9 +113,9 @@ def tile_attend_gkmeans_pl_kernel(tc, xT, cT, us, ts, wt, wd, offs, out_0, out_1
             nc.vector.quantize_mx(out=codes[:].bitcast(FP8X4), scales=scales[:], in_=x_by_r[j])
             xr_tiles[j] = (codes[:].bitcast(FP8X4), scales[:])
 
-        for j in SCATTER_ORDER[:2]:
+        for j in range(LANES):
             copy_turned(j, sb.tile([P, P * LANES], BF16, name=f"x_by_r{j}", align_bytes=64)[:])
-        for j in SCATTER_ORDER[:2]:
+        for j in range(LANES):
             quantise_features(j, "")
 
         c_by_d = sb.tile([P, SLOTS * LANES], BF16, name="c_by_d", tag="c_then_window3", align_bytes=64)
@@ -125,9 +125,6 @@ def tile_attend_gkmeans_pl_kernel(tc, xT, cT, us, ts, wt, wd, offs, out_0, out_1
             nc.vector.tensor_copy(c_low[:, j, :], c_planes[j][:].indirect(offsets[:]))
         nc.vector.tensor_copy(c_lanes[:, :, 0:2], c_low[:].rearrange("p j i -> p i j"))
         nc.vector.tensor_copy(c_lanes[:, :, 2], c_planes[2][:].indirect(offsets[:]))
-        x_late = sb.tile([P, 2 * P * LANES], BF16, name="x_late", tag="c_low", align_bytes=64)
-        for k, j in enumerate(SCATTER_ORDER[2:]):
-            copy_turned(j, x_late[:, k * P * LANES:(k + 1) * P * LANES])
         halves = [slice(a * HALF, (a + 1) * HALF) for a in range(2)]
 
         def listed(slots):
@@ -203,8 +200,10 @@ def tile_attend_gkmeans_pl_kernel(tc, xT, cT, us, ts, wt, wd, offs, out_0, out_1
         factors = [sb.tile([P, 2 if t >= 2 else 1], F32, name=f"factors{t}") for t in range(LANES)]
 
         def weight_factors(t):
-            weights = row_weights[:, :, t] if t >= 2 else wd_sb[:, t:t + 1]
-            nc.scalar.activation(factors[t][:], weights, ACT.Copy, scale=inv_tots[t][:])
+            if t < 2:
+                nc.scalar.activation(factors[t][:], wd_sb[:, t:t + 1], ACT.Copy, scale=inv_tots[t][:])
+            else:
+                nc.vector.tensor_scalar(factors[t][:], row_weights[:, :, t], inv_tots[t][:], None, ALU.mult)
 
         exponentials(0)
         exponentials(1)
@@ -219,9 +218,9 @@ def tile_attend_gkmeans_pl_kernel(tc, xT, cT, us, ts, wt, wd, offs, out_0, out_1
         den_terms_of(nc.vector, 1, 0)
         for t in (2, 3):
             invert_total(t)
+            weight_factors(t)
             weights_of(nc.vector, t, (0,))
-        for t in (2, 3):
-            den_terms_of(nc.vector, t, 0)
+            nc.vector.scalar_tensor_tensor(hs[0][:, t, :], es[t][:, halves[0]], factors[t][:, 1:2], hs[0][:, t - 1, :], ALU.mult, ALU.add)
 
         g_codes, g_scales = mx_tiles("g", SLOTS)
         g_by_r = [sb.tile([P, HALF * LANES], BF16, name=f"g_by_r{a}", align_bytes=64) for a in range(2)]
@@ -252,20 +251,19 @@ def tile_attend_gkmeans_pl_kernel(tc, xT, cT, us, ts, wt, wd, offs, out_0, out_1
         def scatter_on_vector(j):
             nc.vector.tensor_copy(windows[j][:].indirect(offsets[:]), means[j][:])
 
-        for t in (1, 2, 3):
-            add_turned(t, 0)
+        add_turned(LANES - 1, 0)
         hs[1] = sb.tile([P, LANES, HALF], F32, name="h_second", tag="neg_max3")
-        for t in range(LANES):
+        for t in range(2):
             weight_factors(t)
         for t in range(LANES):
             nc.scalar.activation(hs[1][:, t, :], es[t][:, halves[1]], ACT.Copy, scale=factors[t][:, factors[t].shape[1] - 1:])
             add_turned(t, 1)
         interleave(nc.vector.tensor_copy, g_by_r[0][:], g_first[:])
-        quantise_weights(0)
         for a in range(2):
             nc.vector.tensor_reduce(dens[a][:], den_ps[a][:].rearrange("i (b s) -> i b s", b=2), AXIS_X, ALU.add)
         for a in range(2):
             nc.vector.reciprocal(inv_dens[a][:], dens[a][:])
+        quantise_weights(0)
         num0 = [ps.tile([P, HALF], F32, name=f"num0_{a}", tag=bank) for a, bank in enumerate(("bank4", "bank6"))]
         nums = {j: ps.tile([P, SLOTS], F32, name=f"num{j}", tag=bank) for j, bank in ((1, "bank5"), (2, "bank7"), (3, "bank1"))}
         numerators(0, halves[0], num0[0][:])
@@ -279,10 +277,6 @@ def tile_attend_gkmeans_pl_kernel(tc, xT, cT, us, ts, wt, wd, offs, out_0, out_1
         interleave(nc.scalar.copy, g_by_r[1][:], g_second[:])
         for a in range(2):
             nc.scalar.copy(inv_den_all[:, halves[a]], spreads[a][:])
-        late_codes, late_scales = mx_tiles("xr_late", 2 * P, "g_first")
-        nc.vector.quantize_mx(out=late_codes[:].bitcast(FP8X4), scales=late_scales[:], in_=x_late[:])
-        for k, j in enumerate(SCATTER_ORDER[2:]):
-            xr_tiles[j] = (late_codes[:, k * P:(k + 1) * P].bitcast(FP8X4), late_scales[:, k * P:(k + 1) * P])
         divide(0, halves[0], num0[0][:])
         scatter_on_scalar(0, 0)
         quantise_weights(1)
@@ -339,10 +333,11 @@ def tile_attend_gkmeans_pl_kernel(tc, xT, cT, us, ts, wt, wd, offs, out_0, out_1
 
         for cols in (vector_cols, scalar_cols):
             round_plane(round_on_gpsimd, 0, cols, cols)
-        round_plane(round_on_gpsimd, 1, vector_cols, vector_cols)
+        round_plane(round_on_gpsimd, 1, vector_cols, slice(0, 896))
         round_plane(round_on_gpsimd, 1, scalar_cols, slice(1536, 2048))
         for cols in (vector_cols, scalar_cols):
             round_plane(nc.scalar.copy, 2, cols, cols)
+        round_plane(nc.scalar.copy, 1, vector_cols, slice(896, 1152))
         round_plane(nc.scalar.copy, 1, scalar_cols, slice(1152, 1536))
         vector_pieces = (slice(0, 512), slice(512, 1024), slice(1024, 1152))
         round_plane(nc.vector.tensor_copy, 3, vector_cols, vector_cols)

@@ -113,9 +113,9 @@ def tile_attend_gkmeans_pl_kernel(tc, xT, cT, us, ts, wt, wd, offs, out_0, out_1
             nc.vector.quantize_mx(out=codes[:].bitcast(FP8X4), scales=scales[:], in_=x_by_r[j])
             xr_tiles[j] = (codes[:].bitcast(FP8X4), scales[:])
 
-        for j in range(LANES):
+        for j in SCATTER_ORDER[:2]:
             copy_turned(j, sb.tile([P, P * LANES], BF16, name=f"x_by_r{j}", align_bytes=64)[:])
-        for j in range(LANES):
+        for j in SCATTER_ORDER[:2]:
             quantise_features(j, "")
 
         c_by_d = sb.tile([P, SLOTS * LANES], BF16, name="c_by_d", tag="c_then_window3", align_bytes=64)
@@ -125,6 +125,9 @@ def tile_attend_gkmeans_pl_kernel(tc, xT, cT, us, ts, wt, wd, offs, out_0, out_1
             nc.vector.tensor_copy(c_low[:, j, :], c_planes[j][:].indirect(offsets[:]))
         nc.vector.tensor_copy(c_lanes[:, :, 0:2], c_low[:].rearrange("p j i -> p i j"))
         nc.vector.tensor_copy(c_lanes[:, :, 2], c_planes[2][:].indirect(offsets[:]))
+        x_late = sb.tile([P, 2 * P * LANES], BF16, name="x_late", tag="c_low", align_bytes=64)
+        for k, j in enumerate(SCATTER_ORDER[2:]):
+            copy_turned(j, x_late[:, k * P * LANES:(k + 1) * P * LANES])
         halves = [slice(a * HALF, (a + 1) * HALF) for a in range(2)]
 
         def listed(slots):
@@ -277,6 +280,10 @@ def tile_attend_gkmeans_pl_kernel(tc, xT, cT, us, ts, wt, wd, offs, out_0, out_1
         interleave(nc.scalar.copy, g_by_r[1][:], g_second[:])
         for a in range(2):
             nc.scalar.copy(inv_den_all[:, halves[a]], spreads[a][:])
+        late_codes, late_scales = mx_tiles("xr_late", 2 * P, "g_first")
+        nc.vector.quantize_mx(out=late_codes[:].bitcast(FP8X4), scales=late_scales[:], in_=x_late[:])
+        for k, j in enumerate(SCATTER_ORDER[2:]):
+            xr_tiles[j] = (late_codes[:, k * P:(k + 1) * P].bitcast(FP8X4), late_scales[:, k * P:(k + 1) * P])
         divide(0, halves[0], num0[0][:])
         scatter_on_scalar(0, 0)
         quantise_weights(1)

@@ -227,7 +227,7 @@ def tile_attend_gkmeans_pl_kernel(tc, xT, cT, us, ts, wt, wd, offs, out_0, out_1
 
         g_codes, g_scales = mx_tiles("g", SLOTS)
         g_by_r = [sb.tile([P, HALF * LANES], BF16, name=f"g_by_r{a}", align_bytes=64) for a in range(2)]
-        inv_den_all = sb.tile([P, SLOTS], F32, name="inv_den_all")
+        inv_den_all = sb.tile([P, SLOTS], F32, name="inv_den_all", tag="inv_den_then_staged", align_bytes=64)
         dens = [sb.tile([P, 2], F32, name=f"den{a}") for a in range(2)]
         inv_dens = [sb.tile([P, 2], F32, name=f"inv_den{a}") for a in range(2)]
         means = [sb.tile([P, SLOTS], F32, name=f"mean{j}", tag=f"mean{j}", align_bytes=64) for j in range(LANES)]
@@ -289,11 +289,11 @@ def tile_attend_gkmeans_pl_kernel(tc, xT, cT, us, ts, wt, wd, offs, out_0, out_1
         quantise_weights(1)
         numerators(0, halves[1], num0[1][:])
         numerators(1, halves[1], nums[1][:, halves[1]])
-        for j in (2, 3):
+        for j in (3, 2):
             numerators(j, all_slots, nums[j][:])
         divide(0, halves[1], num0[1][:])
         scatter_on_scalar(0, 1)
-        for j in (1, 2):
+        for j in (1, 3, 2):
             divide(j, all_slots, nums[j][:])
 
         out_rows = out_0.rearrange("(p j) n -> p j n", j=LANES)
@@ -301,17 +301,7 @@ def tile_attend_gkmeans_pl_kernel(tc, xT, cT, us, ts, wt, wd, offs, out_0, out_1
         def store_window(j):
             nc.sync.dma_start(out=out_rows[:, j, :], in_=windows[j][:])
 
-        store_window(0)
-        scatter_on_vector(1)
-        store_window(1)
-        for a in range(2):
-            scatter_on_scalar(2, a)
-        store_window(2)
-        divide(3, all_slots, nums[3][:])
-        scatter_on_vector(3)
-        store_window(3)
-
-        vector_cols, scalar_cols = slice(0, 1152), slice(1152, 2048)
+        vector_cols, late_cols, scalar_cols = slice(0, 1152), slice(1152, 1536), slice(1536, 2048)
         staged = {cols.start: sb.tile([P, LANES, cols.stop - cols.start], BF16, name=f"staged{cols.start}", align_bytes=64)
                   for cols in (vector_cols, scalar_cols)}
 
@@ -338,23 +328,33 @@ def tile_attend_gkmeans_pl_kernel(tc, xT, cT, us, ts, wt, wd, offs, out_0, out_1
                                       scales=y_scales[4 * k:P, within:within + piece.stop - piece.start], in_=y_by_d[:])
             nc.sync.dma_start(out=words_out[:, cols], in_=y_codes[:].bitcast(I32))
 
-        for cols in (vector_cols, scalar_cols):
-            round_plane(round_on_gpsimd, 0, cols, cols)
-        round_plane(round_on_gpsimd, 1, vector_cols, slice(0, 896))
-        round_plane(round_on_gpsimd, 1, scalar_cols, slice(1536, 2048))
+        store_window(0)
+        scatter_on_vector(1)
+        store_window(1)
+        scatter_on_scalar(2, 0)
+        staged[late_cols.start] = sb.tile([P, LANES, late_cols.stop - late_cols.start], BF16, name="staged_late", tag="inv_den_then_staged", align_bytes=64)
+        round_plane(nc.scalar.copy, 0, late_cols, late_cols)
+        scatter_on_scalar(2, 1)
+        store_window(2)
+        scatter_on_vector(3)
+        store_window(3)
+
+        for j in range(2):
+            for cols in (vector_cols, scalar_cols):
+                round_plane(round_on_gpsimd, j, cols, cols)
+        round_plane(nc.scalar.copy, 1, late_cols, late_cols)
         for cols in (vector_cols, scalar_cols):
             round_plane(nc.scalar.copy, 2, cols, cols)
-        round_plane(nc.scalar.copy, 1, vector_cols, slice(896, 1152))
-        round_plane(nc.scalar.copy, 1, scalar_cols, slice(1152, 1536))
+        round_plane(nc.vector.tensor_copy, 2, late_cols, late_cols)
         vector_pieces = (slice(0, 512), slice(512, 1024), slice(1024, 1152))
         round_plane(nc.vector.tensor_copy, 3, vector_cols, vector_cols)
-        round_plane(nc.vector.tensor_copy, 3, scalar_cols, slice(1152, 1536))
-        round_plane(nc.scalar.copy, 3, scalar_cols, slice(1536, 2048))
+        round_plane(nc.vector.tensor_copy, 3, late_cols, late_cols)
+        round_plane(nc.scalar.copy, 3, scalar_cols, scalar_cols)
         woven = [weave(nc.vector.tensor_copy, vector_cols, cols) for cols in vector_pieces]
         quantise_and_store(vector_pieces[:1], woven[:1])
         quantise_and_store(vector_pieces[1:], woven[1:])
-        for cols in (slice(1536, 2048), slice(1280, 1536), slice(1152, 1280)):
-            quantise_and_store([cols], [weave(nc.scalar.copy, scalar_cols, cols)])
+        for tile_cols, cols in ((scalar_cols, scalar_cols), (late_cols, slice(1280, 1536)), (late_cols, slice(1152, 1280))):
+            quantise_and_store([cols], [weave(nc.scalar.copy, tile_cols, cols)])
         scales_out = out_2[0].rearrange("(q r) (k c) -> q k r c", r=4, c=GROUP)
         for q in range(4):
             nc.sync.dma_start(out=scales_out[q].bitcast(I32), in_=y_scales[32 * q:32 * q + 16, :].bitcast(I32))

@@ -345,7 +345,7 @@ def tile_attend_gkmeans_pl_kernel(tc, xT, cT, us, ts, wt, wd, offs, out_0, out_1
         round_plane(nc.scalar.copy, 1, late_cols, late_cols)
         for cols in (vector_cols, scalar_cols):
             round_plane(nc.scalar.copy, 2, cols, cols)
-        round_plane(nc.vector.tensor_copy, 2, late_cols, late_cols)
+        round_plane(round_on_gpsimd, 2, late_cols, late_cols)
         vector_pieces = (slice(0, 512), slice(512, 1024), slice(1024, 1152))
         round_plane(nc.vector.tensor_copy, 3, vector_cols, vector_cols)
         round_plane(nc.vector.tensor_copy, 3, late_cols, late_cols)

@@ -301,7 +301,7 @@ def tile_attend_gkmeans_pl_kernel(tc, xT, cT, us, ts, wt, wd, offs, out_0, out_1
         def store_window(j):
             nc.sync.dma_start(out=out_rows[:, j, :], in_=windows[j][:])
 
-        vector_cols, late_cols, scalar_cols = slice(0, 1152), slice(1152, 1536), slice(1536, 2048)
+        vector_cols, late_cols, scalar_cols = slice(0, 1280), slice(1280, 1536), slice(1536, 2048)
         staged = {cols.start: sb.tile([P, LANES, cols.stop - cols.start], BF16, name=f"staged{cols.start}", align_bytes=64)
                   for cols in (vector_cols, scalar_cols)}
 
@@ -320,12 +320,12 @@ def tile_attend_gkmeans_pl_kernel(tc, xT, cT, us, ts, wt, wd, offs, out_0, out_1
         words_out = out_1[0].rearrange("p n l -> p (n l)").bitcast(I32)
 
         def quantise_and_store(pieces, woven):
-            cols = slice(pieces[0].start, pieces[-1].stop)
+            cols = slice(min(piece.start for piece in pieces), max(piece.stop for piece in pieces))
             y_codes = sb.tile([P, cols.stop - cols.start], U32, name=f"y_codes{cols.start}", align_bytes=64)
             for piece, y_by_d in zip(pieces, woven):
                 k, within = divmod(piece.start, GROUP)
                 nc.vector.quantize_mx(out=y_codes[:, piece.start - cols.start:piece.stop - cols.start].bitcast(FP8X4),
-                                      scales=y_scales[4 * k:P, within:within + piece.stop - piece.start], in_=y_by_d[:])
+                                      scales=y_scales[4 * k:P, within:within + piece.stop - piece.start], in_=y_by_d)
             nc.sync.dma_start(out=words_out[:, cols], in_=y_codes[:].bitcast(I32))
 
         store_window(0)
@@ -346,15 +346,18 @@ def tile_attend_gkmeans_pl_kernel(tc, xT, cT, us, ts, wt, wd, offs, out_0, out_1
         for cols in (vector_cols, scalar_cols):
             round_plane(nc.scalar.copy, 2, cols, cols)
         round_plane(round_on_gpsimd, 2, late_cols, late_cols)
-        vector_pieces = (slice(0, 512), slice(512, 1024), slice(1024, 1152))
+        vector_pieces = (slice(0, 512), slice(512, 1024), slice(1024, 1280))
         round_plane(nc.vector.tensor_copy, 3, vector_cols, vector_cols)
         round_plane(nc.vector.tensor_copy, 3, late_cols, late_cols)
         round_plane(nc.scalar.copy, 3, scalar_cols, scalar_cols)
-        woven = [weave(nc.vector.tensor_copy, vector_cols, cols) for cols in vector_pieces]
-        quantise_and_store(vector_pieces[:1], woven[:1])
-        quantise_and_store(vector_pieces[1:], woven[1:])
-        for tile_cols, cols in ((scalar_cols, scalar_cols), (late_cols, slice(1280, 1536)), (late_cols, slice(1152, 1280))):
-            quantise_and_store([cols], [weave(nc.scalar.copy, tile_cols, cols)])
+        first, second = [weave(nc.vector.tensor_copy, vector_cols, cols) for cols in vector_pieces[:2]]
+        quantise_and_store(vector_pieces[:1], [first[:]])
+        third = weave(nc.vector.tensor_copy, vector_cols, vector_pieces[2])
+        quantise_and_store([slice(512, 768), slice(768, 1024), vector_pieces[2]], [second[:, 0:1024], second[:, 1024:2048], third[:]])
+        fourth = weave(nc.scalar.copy, scalar_cols, scalar_cols)
+        quantise_and_store([slice(1792, 2048), slice(1536, 1792)], [fourth[:, 1024:2048], fourth[:, 0:1024]])
+        for cols in (slice(1408, 1536), slice(1280, 1408)):
+            quantise_and_store([cols], [weave(nc.scalar.copy, late_cols, cols)[:]])
         scales_out = out_2[0].rearrange("(q r) (k c) -> q k r c", r=4, c=GROUP)
         for q in range(4):
             nc.sync.dma_start(out=scales_out[q].bitcast(I32), in_=y_scales[32 * q:32 * q + 16, :].bitcast(I32))

@@ -343,9 +343,10 @@ def tile_attend_gkmeans_pl_kernel(tc, xT, cT, us, ts, wt, wd, offs, out_0, out_1
             for cols in (vector_cols, scalar_cols):
                 round_plane(round_on_gpsimd, j, cols, cols)
         round_plane(nc.scalar.copy, 1, late_cols, late_cols)
-        for cols in (vector_cols, scalar_cols):
+        round_plane(nc.scalar.copy, 2, vector_cols, slice(0, 512))
+        round_plane(nc.scalar.copy, 2, vector_cols, slice(512, 1280))
+        for cols in (scalar_cols, late_cols):
             round_plane(nc.scalar.copy, 2, cols, cols)
-        round_plane(round_on_gpsimd, 2, late_cols, late_cols)
         vector_pieces = (slice(0, 512), slice(512, 1024), slice(1024, 1280))
         round_plane(nc.vector.tensor_copy, 3, vector_cols, vector_cols)
         round_plane(nc.vector.tensor_copy, 3, late_cols, late_cols)

@@ -210,7 +210,9 @@ def tile_attend_gkmeans_pl_kernel(tc, xT, cT, us, ts, wt, wd, offs, out_0, out_1
 
         exponentials(0)
         exponentials(1)
-        invert_total(0)
+        minus_one = sb.tile([P, 1], F32, name="minus_one")
+        nc.gpsimd.memset(minus_one[:], -1.0)
+        nc.gpsimd.tensor_tensor(inv_tots[0][:], tots[0][:], minus_one[:], ALU.pow)
         weights_of(nc.gpsimd, 0, (0,))
         den_terms_of(nc.gpsimd, 0, 0)
         add_turned(0, 0)

@@ -81,7 +81,7 @@ def tile_attend_gkmeans_pl_kernel(tc, xT, cT, us, ts, wt, wd, offs, out_0, out_1
                 nc.tensor.transpose(spread_ps[:, c * P:(c + 1) * P], cols[:, c:c + 1].to_broadcast([P, P]), ident[:])
             nc.scalar.copy(spread, spread_ps[:])
 
-        ts_all = sb.tile([P, SLOTS], F32, name="ts_all")
+        ts_all = sb.tile([P, SLOTS], F32, name="ts_all", tag="ts_then_x", align_bytes=64)
         spread_columns(ts_all[:], ts_cols[:], "bank7")
         neg_us = sb.tile([P, LANES], F32, name="neg_us")
         nc.gpsimd.tensor_scalar(neg_us[:], us_sb[:], -1.0, 1.0, ALU.mult, ALU.mult)
@@ -210,6 +210,10 @@ def tile_attend_gkmeans_pl_kernel(tc, xT, cT, us, ts, wt, wd, offs, out_0, out_1
 
         exponentials(0)
         exponentials(1)
+        late_codes, late_scales = mx_tiles("xr_late", 2 * P, "ts_then_x")
+        nc.vector.quantize_mx(out=late_codes[:].bitcast(FP8X4), scales=late_scales[:], in_=x_late[:])
+        for k, j in enumerate(SCATTER_ORDER[2:]):
+            xr_tiles[j] = (late_codes[:, k * P:(k + 1) * P].bitcast(FP8X4), late_scales[:, k * P:(k + 1) * P])
         minus_one = sb.tile([P, 1], F32, name="minus_one")
         nc.gpsimd.memset(minus_one[:], -1.0)
         nc.gpsimd.tensor_tensor(inv_tots[0][:], tots[0][:], minus_one[:], ALU.pow)
@@ -282,10 +286,6 @@ def tile_attend_gkmeans_pl_kernel(tc, xT, cT, us, ts, wt, wd, offs, out_0, out_1
         interleave(nc.scalar.copy, g_by_r[1][:], g_second[:])
         for a in range(2):
             nc.scalar.copy(inv_den_all[:, halves[a]], spreads[a][:])
-        late_codes, late_scales = mx_tiles("xr_late", 2 * P, "g_first")
-        nc.vector.quantize_mx(out=late_codes[:].bitcast(FP8X4), scales=late_scales[:], in_=x_late[:])
-        for k, j in enumerate(SCATTER_ORDER[2:]):
-            xr_tiles[j] = (late_codes[:, k * P:(k + 1) * P].bitcast(FP8X4), late_scales[:, k * P:(k + 1) * P])
         divide(0, halves[0], num0[0][:])
         scatter_on_scalar(0, 0)
         quantise_weights(1)

from contextlib import ExitStack

import concourse.mybir as mybir
from concourse.masks import make_identity

F32 = mybir.dt.float32
BF16 = mybir.dt.bfloat16
I32 = mybir.dt.int32
U32 = mybir.dt.uint32
U16 = mybir.dt.uint16
U8 = mybir.dt.uint8
FP8X4 = mybir.dt.float8_e4m3fn_x4
ALU = mybir.AluOpType
ACT = mybir.ActivationFunctionType
AXIS_X = mybir.AxisListType.X

P = 128
LANES = 4
D, R, SLOTS, T = 512, 512, 512, 2048
FLOPS = 2 * 2 * D * R * SLOTS
HALF = SLOTS // 2
SCATTER_ORDER = (0, 1, 2, 3)
GROUP = 512


def tile_attend_gkmeans_pl_kernel(tc, xT, cT, us, ts, wt, wd, offs, out_0, out_1, out_2):
    nc = tc.nc
    with ExitStack() as ctx:
        sb = ctx.enter_context(tc.tile_pool(name="sb", bufs=1))
        ps = ctx.enter_context(tc.psum_pool(name="ps", bufs=1))

        def mx_tiles(name, width, tag=""):
            codes = sb.tile([P, width], U32, name=name + "_codes", tag=tag, align_bytes=64)
            scales = sb.tile([P, width], U8, name=name + "_scales", align_bytes=64)
            return codes, scales

        def interleave(copy, lanes_last, staged):
            copy(
                lanes_last.rearrange("p (c n j) -> p c j n", n=4, j=LANES),
                staged.rearrange("p j (c n) -> p c j n", n=4),
            )

        x_raw = sb.tile([P, LANES, R], F32, name="x_raw")
        nc.sync.dma_start(out=x_raw[:], in_=xT.rearrange("(p j) r -> p j r", j=LANES))
        offsets = sb.tile([P, SLOTS // 16], U16, name="offsets")
        nc.sync.dma_start(offsets[:], offs)
        ts_window = sb.tile([P, T], F32, name="ts_window", tag="ts_then_window2")
        nc.scalar.dma_start(out=ts_window[P - 1:P, :], in_=ts[0:1, :])
        nc.vector.memset(ts_window[0:P - 1, :], 0.0)
        c_planes = [sb.tile([P, T], F32, name=f"c_plane{j}", tag=f"c_plane{j}", align_bytes=64) for j in range(LANES)]
        c_rows = cT.rearrange("(p j) n -> p j n", j=LANES)
        for j in range(LANES):
            nc.sync.dma_start(out=c_planes[j][:], in_=c_rows[:, j, :])

        us_sb = sb.tile([P, LANES], F32, name="us_sb")
        row_weights = sb.tile([P, 2, 2 * LANES], F32, name="row_weights")
        wt_sb, wd_sb = row_weights[:, 0, 0:LANES], row_weights[:, 1, 0:LANES]
        for tile, vec in ((us_sb[:], us), (wt_sb, wt), (wd_sb, wd)):
            nc.sync.dma_start(out=tile, in_=vec.rearrange("(s t) o -> s (t o)", t=LANES))

        ident = sb.tile([P, P], F32, name="ident")
        make_identity(nc, ident[:])

        ts_row = sb.tile([P, SLOTS], F32, name="ts_row")
        nc.vector.tensor_copy(ts_row[:], ts_window[:].indirect(offsets[:]))
        windows = [sb.tile([P, T], F32, name=f"window{j}") for j in range(2)]
        nc.vector.memset(windows[0][:], 0.0)
        nc.gpsimd.memset(windows[1][:], 0.0)
        windows.append(sb.tile([P, T], F32, name="window2", tag="ts_then_window2"))
        nc.gpsimd.memset(windows[2][:], 0.0)
        ts_turned = ps.tile([P, LANES, P], F32, name="ts_turned", tag="bank6")
        for c in range(LANES):
            nc.tensor.transpose(ts_turned[:, c, :], ts_row[:, c * P:(c + 1) * P], ident[:])
        ts_cols = sb.tile([P, LANES], F32, name="ts_cols")
        nc.scalar.copy(ts_cols[:], ts_turned[:, :, P - 1])

        def spread_columns(spread, cols, bank):
            count = cols.shape[1]
            spread_ps = ps.tile([P, count * P], F32, name="spread_ps", tag=bank)
            for c in range(count):
                nc.tensor.transpose(spread_ps[:, c * P:(c + 1) * P], cols[:, c:c + 1].to_broadcast([P, P]), ident[:])
            nc.scalar.copy(spread, spread_ps[:])

        ts_all = sb.tile([P, SLOTS], F32, name="ts_all", tag="ts_then_x", align_bytes=64)
        spread_columns(ts_all[:], ts_cols[:], "bank7")
        neg_us = sb.tile([P, LANES], F32, name="neg_us")
        nc.gpsimd.tensor_scalar(neg_us[:], us_sb[:], -1.0, 1.0, ALU.mult, ALU.mult)

        x_by_d = sb.tile([P, R * LANES], BF16, name="x_by_d", align_bytes=64)
        nc.scalar.copy(
            x_by_d[:].rearrange("p (t s j) -> p s t j", t=LANES, j=LANES),
            x_raw[:].rearrange("p j (s t) -> p s t j", t=LANES),
        )
        xd_codes, xd_scales = mx_tiles("xd", R)
        nc.vector.quantize_mx(out=xd_codes[:].bitcast(FP8X4), scales=xd_scales[:], in_=x_by_d[:])

        x_pairs = x_by_d[:].bitcast(F32)
        turned = [ps.tile([P, LANES * P], F32, name=f"x_turned{u}", tag=f"bank{4 + u}") for u in range(2)]
        for u in range(2):
            for t in range(LANES):
                nc.tensor.transpose(turned[u][:, t * P:(t + 1) * P], x_pairs[:, 2 * P * t + u:2 * P * (t + 1):2], ident[:])
        x_by_r = {}
        xr_tiles = {}

        def copy_turned(j, tile):
            u, e = divmod(j, 2)
            nc.scalar.copy(tile.rearrange("s (p t) -> s p t", t=LANES),
                           turned[u][:].bitcast(BF16).rearrange("s (t p e) -> s e p t", t=LANES, e=2)[:, e])
            x_by_r[j] = tile

        def quantise_features(j, tag):
            codes, scales = mx_tiles(f"xr{j}", P, tag)
            nc.vector.quantize_mx(out=codes[:].bitcast(FP8X4), scales=scales[:], in_=x_by_r[j])
            xr_tiles[j] = (codes[:].bitcast(FP8X4), scales[:])

        for j in SCATTER_ORDER[:2]:
            copy_turned(j, sb.tile([P, P * LANES], BF16, name=f"x_by_r{j}", align_bytes=64)[:])
        for j in SCATTER_ORDER[:2]:
            quantise_features(j, "")

        c_by_d = sb.tile([P, SLOTS * LANES], BF16, name="c_by_d", tag="c_then_window3", align_bytes=64)
        c_lanes = c_by_d[:].rearrange("p (i j) -> p i j", j=LANES)
        c_low = sb.tile([P, 2, SLOTS], F32, name="c_low", tag="c_low", align_bytes=64)
        for j in range(2):
            nc.vector.tensor_copy(c_low[:, j, :], c_planes[j][:].indirect(offsets[:]))
        nc.vector.tensor_copy(c_lanes[:, :, 0:2], c_low[:].rearrange("p j i -> p i j"))
        nc.vector.tensor_copy(c_lanes[:, :, 2], c_planes[2][:].indirect(offsets[:]))
        x_late = sb.tile([P, 2 * P * LANES], BF16, name="x_late", tag="c_low", align_bytes=64)
        for k, j in enumerate(SCATTER_ORDER[2:]):
            copy_turned(j, x_late[:, k * P * LANES:(k + 1) * P * LANES])
        halves = [slice(a * HALF, (a + 1) * HALF) for a in range(2)]

        def listed(slots):
            return offsets[:, slots.start // 16:slots.stop // 16]

        c_codes, c_scales = mx_tiles("c", SLOTS)
        for slots in halves:
            nc.vector.tensor_copy(c_lanes[:, slots, 3], c_planes[3][:].indirect(listed(slots)))
            nc.vector.quantize_mx(out=c_codes[:, slots].bitcast(FP8X4), scales=c_scales[:, slots],
                                  in_=c_by_d[:, slots.start * LANES:slots.stop * LANES])
        windows.append(sb.tile([P, T], F32, name="window3", tag="c_then_window3", align_bytes=64))
        nc.gpsimd.memset(windows[3][:], 0.0)

        all_slots = slice(0, SLOTS)
        g_first = sb.tile([P, LANES, HALF], BF16, name="g_first", tag="g_first", align_bytes=64)
        zs = [sb.tile([P, SLOTS], F32, name=f"z{t}", tag=f"z{t}", align_bytes=64) for t in range(LANES)]
        es = [sb.tile([P, SLOTS], F32, name=f"e{t}") for t in range(LANES)]
        hs = {0: sb.tile([P, LANES, HALF], F32, name="h_first")}
        tots = [sb.tile([P, 1], F32, name=f"tot{t}") for t in range(LANES)]
        inv_tots = [sb.tile([P, 1], F32, name=f"inv_tot{t}") for t in range(LANES)]

        turned_scores = {t: ps.tile([P, SLOTS], F32, name=f"turned_scores{t}", tag=f"bank{4 + t}") for t in (2, 3)}
        late_rows = slice(2 * P, 4 * P)

        def scaled_scores(t, slots, bank):
            rows = slice(t * P, (t + 1) * P)
            scores = ps.tile([P, slots.stop - slots.start], F32, name="scores", tag=bank)
            nc.tensor.matmul_mx(out=scores[:], lhsT=xd_codes[:, rows].bitcast(FP8X4), lhsT_scale=xd_scales[:, rows],
                                rhs=c_codes[:, slots].bitcast(FP8X4), rhs_scale=c_scales[:, slots], start=True, stop=True)
            nc.vector.scalar_tensor_tensor(zs[t][:, slots], scores[:], neg_us[:, t:t + 1], ts_all[:, slots], ALU.mult, ALU.mult)

        def scores_by_slot(a):
            scores = ps.tile([P, 2, 2 * P], F32, name="scores_by_slot", tag=f"bank{4 + a}")
            scaled = sb.tile([P, 2, 2 * P], F32, name=f"scaled{a}")
            for b in range(2):
                slots = slice((2 * a + b) * P, (2 * a + b + 1) * P)
                nc.tensor.matmul_mx(out=scores[:, b, :], lhsT=c_codes[:, slots].bitcast(FP8X4), lhsT_scale=c_scales[:, slots],
                                    rhs=xd_codes[:, late_rows].bitcast(FP8X4), rhs_scale=xd_scales[:, late_rows], start=True, stop=True)
            for b in range(2):
                nc.scalar.activation(scaled[:, b, :], scores[:, b, :], ACT.Copy, scale=ts_cols[:, 2 * a + b:2 * a + b + 1])
            return scaled

        def exponentials(t):
            neg_max = sb.tile([P, 1], F32, name=f"neg_max{t}", tag=f"neg_max{t}")
            if t < 2:
                nc.vector.tensor_reduce(neg_max[:], zs[t][:], AXIS_X, ALU.min)
            else:
                nc.vector.tensor_scalar(zs[t][:], turned_scores[t][:], neg_us[:, t:t + 1], None, ALU.mult, ALU.min, accum_out=neg_max[:])
            nc.scalar.activation(es[t][:], zs[t][:], ACT.Exp, bias=neg_max[:], scale=-1.0, accum_out=tots[t][:])

        def invert_total(t):
            nc.vector.reciprocal(inv_tots[t][:], tots[t][:])

        def den_terms_of(engine, t, a):
            engine.tensor_scalar(hs[a][:, t, :], es[t][:, halves[a]], inv_tots[t][:], wd_sb[:, t:t + 1], ALU.mult, ALU.mult)

        def add_turned(t, a):
            for b in range(2):
                nc.tensor.matmul(den_ps[a][:, b * P:(b + 1) * P], hs[a][:, t, b * P:(b + 1) * P], ident[:], is_transpose=True,
                                 start=(t == 0 and b == 0), stop=(t == LANES - 1 and b == 1))

        def weights_of(engine, t, halves_now):
            engine.tensor_scalar(g_first[:, t, :], es[t][:, halves[0]], inv_tots[t][:], wt_sb[:, t:t + 1], ALU.mult, ALU.mult)

        for a in range(2):
            for t in range(2):
                scaled_scores(t, halves[a], f"bank{2 * a + t}")
        by_slot = [scores_by_slot(a) for a in range(2)]
        for t in (2, 3):
            for c in range(LANES):
                nc.tensor.transpose(turned_scores[t][:, c * P:(c + 1) * P], by_slot[c // 2][:, c % 2, (t - 2) * P:(t - 1) * P], ident[:])
        den_ps = [ps.tile([P, HALF], F32, name=f"den_ps{a}", tag=f"bank{a}") for a in range(2)]
        factors = [sb.tile([P, 2 if t >= 2 else 1], F32, name=f"factors{t}") for t in range(LANES)]

        def weight_factors(t):
            if t < 2:
                nc.scalar.activation(factors[t][:], wd_sb[:, t:t + 1], ACT.Copy, scale=inv_tots[t][:])
            else:
                nc.vector.tensor_scalar(factors[t][:], row_weights[:, :, t], inv_tots[t][:], None, ALU.mult)

        exponentials(0)
        exponentials(1)
        late_codes, late_scales = mx_tiles("xr_late", 2 * P, "ts_then_x")
        nc.vector.quantize_mx(out=late_codes[:].bitcast(FP8X4), scales=late_scales[:], in_=x_late[:])
        for k, j in enumerate(SCATTER_ORDER[2:]):
            xr_tiles[j] = (late_codes[:, k * P:(k + 1) * P].bitcast(FP8X4), late_scales[:, k * P:(k + 1) * P])
        minus_one = sb.tile([P, 1], F32, name="minus_one")
        nc.gpsimd.memset(minus_one[:], -1.0)
        nc.gpsimd.tensor_tensor(inv_tots[0][:], tots[0][:], minus_one[:], ALU.pow)
        weights_of(nc.gpsimd, 0, (0,))
        den_terms_of(nc.gpsimd, 0, 0)
        add_turned(0, 0)
        exponentials(2)
        exponentials(3)
        invert_total(1)
        weights_of(nc.vector, 1, (0,))
        den_terms_of(nc.vector, 1, 0)
        for t in (2, 3):
            invert_total(t)
            weight_factors(t)
            weights_of(nc.vector, t, (0,))
            nc.vector.scalar_tensor_tensor(hs[0][:, t, :], es[t][:, halves[0]], factors[t][:, 1:2], hs[0][:, t - 1, :], ALU.mult, ALU.add)

        g_codes, g_scales = mx_tiles("g", SLOTS)
        g_by_r = [sb.tile([P, HALF * LANES], BF16, name=f"g_by_r{a}", align_bytes=64) for a in range(2)]
        inv_den_all = sb.tile([P, SLOTS], F32, name="inv_den_all", tag="inv_den_then_staged", align_bytes=64)
        dens = [sb.tile([P, 2], F32, name=f"den{a}") for a in range(2)]
        inv_dens = [sb.tile([P, 2], F32, name=f"inv_den{a}") for a in range(2)]
        means = [sb.tile([P, SLOTS], F32, name=f"mean{j}", tag=f"mean{j}", align_bytes=64) for j in range(LANES)]

        def quantise_weights(a):
            nc.vector.quantize_mx(out=g_codes[:, halves[a]].bitcast(FP8X4), scales=g_scales[:, halves[a]], in_=g_by_r[a][:])

        def numerators(j, slots, num_ps):
            nc.tensor.matmul_mx(out=num_ps, lhsT=xr_tiles[j][0], lhsT_scale=xr_tiles[j][1],
                                rhs=g_codes[:, slots].bitcast(FP8X4), rhs_scale=g_scales[:, slots], start=True, stop=True)

        def spread_inverse(a, bank):
            spread = ps.tile([P, HALF], F32, name="spread", tag=bank)
            for c in range(2):
                nc.tensor.transpose(spread[:, c * P:(c + 1) * P], inv_dens[a][:, c:c + 1].to_broadcast([P, P]), ident[:])
            return spread

        def divide(j, slots, num):
            nc.vector.tensor_tensor(means[j][:, slots], num, inv_den_all[:, slots], ALU.mult)

        def scatter_on_scalar(j, a):
            nc.scalar.activation(windows[j][:].indirect(listed(halves[a])), means[j][:, halves[a]], ACT.Copy)

        def scatter_on_vector(j):
            nc.vector.tensor_copy(windows[j][:].indirect(offsets[:]), means[j][:])

        add_turned(LANES - 1, 0)
        hs[1] = sb.tile([P, LANES, HALF], F32, name="h_second", tag="neg_max3")
        for t in range(2):
            weight_factors(t)
        for t in range(LANES):
            nc.scalar.activation(hs[1][:, t, :], es[t][:, halves[1]], ACT.Copy, scale=factors[t][:, factors[t].shape[1] - 1:])
            add_turned(t, 1)
        interleave(nc.vector.tensor_copy, g_by_r[0][:], g_first[:])
        for a in range(2):
            nc.vector.tensor_reduce(dens[a][:], den_ps[a][:].rearrange("i (b s) -> i b s", b=2), AXIS_X, ALU.add)
        for a in range(2):
            nc.vector.reciprocal(inv_dens[a][:], dens[a][:])
        quantise_weights(0)
        num0 = [ps.tile([P, HALF], F32, name=f"num0_{a}", tag=bank) for a, bank in enumerate(("bank4", "bank6"))]
        nums = {j: ps.tile([P, SLOTS], F32, name=f"num{j}", tag=bank) for j, bank in ((1, "bank5"), (2, "bank7"), (3, "bank1"))}
        numerators(0, halves[0], num0[0][:])
        numerators(1, halves[0], nums[1][:, halves[0]])
        spreads = [spread_inverse(a, f"bank{2 + a}") for a in range(2)]
        g_second = sb.tile([P, LANES, HALF], BF16, name="g_second", tag="z3", align_bytes=64)
        for t in range(2):
            nc.vector.tensor_scalar(g_second[:, t, :], es[t][:, halves[1]], inv_tots[t][:], wt_sb[:, t:t + 1], ALU.mult, ALU.mult)
        for t in (2, 3):
            nc.scalar.activation(g_second[:, t, :], es[t][:, halves[1]], ACT.Copy, scale=factors[t][:, 0:1])
        interleave(nc.scalar.copy, g_by_r[1][:], g_second[:])
        for a in range(2):
            nc.scalar.copy(inv_den_all[:, halves[a]], spreads[a][:])
        divide(0, halves[0], num0[0][:])
        scatter_on_scalar(0, 0)
        quantise_weights(1)
        numerators(0, halves[1], num0[1][:])
        numerators(1, halves[1], nums[1][:, halves[1]])
        for j in (3, 2):
            numerators(j, all_slots, nums[j][:])
        divide(0, halves[1], num0[1][:])
        scatter_on_scalar(0, 1)
        for j in (1, 3, 2):
            divide(j, all_slots, nums[j][:])

        out_rows = out_0.rearrange("(p j) n -> p j n", j=LANES)

        def store_window(j):
            nc.sync.dma_start(out=out_rows[:, j, :], in_=windows[j][:])

        vector_cols, late_cols, scalar_cols = slice(0, 1280), slice(1280, 1536), slice(1536, 2048)
        staged = {cols.start: sb.tile([P, LANES, cols.stop - cols.start], BF16, name=f"staged{cols.start}", align_bytes=64)
                  for cols in (vector_cols, scalar_cols)}

        def round_on_gpsimd(rounded, source):
            nc.gpsimd.tensor_scalar(rounded, source, 1.0, 1.0, ALU.mult, ALU.mult)

        def round_plane(copy, j, tile_cols, cols):
            copy(staged[tile_cols.start][:, j, cols.start - tile_cols.start:cols.stop - tile_cols.start], windows[j][:, cols])

        def weave(copy, tile_cols, cols):
            y_by_d = sb.tile([P, (cols.stop - cols.start) * LANES], BF16, name=f"y_by_d{cols.start}", align_bytes=64)
            interleave(copy, y_by_d[:], staged[tile_cols.start][:, :, cols.start - tile_cols.start:cols.stop - tile_cols.start])
            return y_by_d

        y_scales = sb.tile([P, GROUP], U8, name="y_scales", align_bytes=64)
        words_out = out_1[0].rearrange("p n l -> p (n l)").bitcast(I32)

        def quantise_and_store(pieces, woven):
            cols = slice(min(piece.start for piece in pieces), max(piece.stop for piece in pieces))
            y_codes = sb.tile([P, cols.stop - cols.start], U32, name=f"y_codes{cols.start}", align_bytes=64)
            for piece, y_by_d in zip(pieces, woven):
                k, within = divmod(piece.start, GROUP)
                nc.vector.quantize_mx(out=y_codes[:, piece.start - cols.start:piece.stop - cols.start].bitcast(FP8X4),
                                      scales=y_scales[4 * k:P, within:within + piece.stop - piece.start], in_=y_by_d)
            nc.sync.dma_start(out=words_out[:, cols], in_=y_codes[:].bitcast(I32))

        store_window(0)
        scatter_on_vector(1)
        store_window(1)
        scatter_on_scalar(2, 0)
        staged[late_cols.start] = sb.tile([P, LANES, late_cols.stop - late_cols.start], BF16, name="staged_late", tag="inv_den_then_staged", align_bytes=64)
        round_plane(nc.scalar.copy, 0, late_cols, late_cols)
        scatter_on_scalar(2, 1)
        store_window(2)
        scatter_on_vector(3)
        store_window(3)

        for j in range(2):
            for cols in (vector_cols, scalar_cols):
                round_plane(round_on_gpsimd, j, cols, cols)
        round_plane(nc.scalar.copy, 1, late_cols, late_cols)
        round_plane(nc.scalar.copy, 2, vector_cols, slice(0, 512))
        round_plane(nc.scalar.copy, 2, vector_cols, slice(512, 1280))
        for cols in (scalar_cols, late_cols):
            round_plane(nc.scalar.copy, 2, cols, cols)
        vector_pieces = (slice(0, 512), slice(512, 1024), slice(1024, 1280))
        round_plane(nc.vector.tensor_copy, 3, vector_cols, vector_cols)
        round_plane(nc.vector.tensor_copy, 3, late_cols, late_cols)
        round_plane(nc.scalar.copy, 3, scalar_cols, scalar_cols)
        first, second = [weave(nc.vector.tensor_copy, vector_cols, cols) for cols in vector_pieces[:2]]
        quantise_and_store(vector_pieces[:1], [first[:]])
        third = weave(nc.vector.tensor_copy, vector_cols, vector_pieces[2])
        quantise_and_store([slice(512, 768), slice(768, 1024), vector_pieces[2]], [second[:, 0:1024], second[:, 1024:2048], third[:]])
        fourth = weave(nc.scalar.copy, scalar_cols, scalar_cols)
        quantise_and_store([slice(1792, 2048), slice(1536, 1792)], [fourth[:, 1024:2048], fourth[:, 0:1024]])
        for cols in (slice(1408, 1536), slice(1280, 1408)):
            quantise_and_store([cols], [weave(nc.scalar.copy, late_cols, cols)[:]])
        scales_out = out_2[0].rearrange("(q r) (k c) -> q k r c", r=4, c=GROUP)
        for q in range(4):
            nc.sync.dma_start(out=scales_out[q].bitcast(I32), in_=y_scales[32 * q:32 * q + 16, :].bitcast(I32))
